import numpy as np
import ml_dtypes


def mxq(x, axis, fmt="e4m3"):
    dtype, down = {"e4m3": (ml_dtypes.float8_e4m3fn, 7), "e5m2": (ml_dtypes.float8_e5m2, 14)}[fmt]
    v = np.moveaxis(np.asarray(x, np.float32).astype(ml_dtypes.bfloat16).astype(np.float64), axis, -1)
    blocks = v.reshape(v.shape[:-1] + (-1, 32))
    amax = np.abs(blocks).max(-1, keepdims=True)
    byte = np.maximum(np.where(amax > 0, np.frexp(amax)[1] - 1 + 127, 0) - down, 1)
    scale = np.exp2(byte - 127.0)
    codes = (blocks / scale).astype(np.float32).astype(dtype).astype(np.float64)
    return np.moveaxis((codes * scale).reshape(v.shape), -1, axis)


WIDE = False


def mx_kscale(k):
    if not WIDE:
        return np.ones(k)
    levels = np.array([10, -10, 5, -5, 0])
    if k % 512:
        return np.exp2(np.random.permutation(np.resize(levels, k // 32))).repeat(32)
    a = np.empty((k // 512, 16))
    for p in range(k // 512):
        a[p, :8] = np.random.permutation(np.resize(levels, 8))
        for g in range(8):
            far = levels[np.abs(levels - a[p, g]) >= 10]
            a[p, g + 8] = far[np.random.randint(len(far))]
    return np.exp2(a.ravel()).repeat(32)


def f64(x):
    return np.asarray(x).astype(np.float64)


def striped(idx):
    return np.tile(idx.reshape(-1, 16).T, (8, 1)).astype(np.uint16)


def unstriped(offs):
    return offs[:16].T.reshape(-1).astype(np.int64)


def pack_weight(w):
    k, n = w.shape
    w = f64(np.asarray(w, np.float32).astype(ml_dtypes.bfloat16)).reshape(k // 32, 32, n)
    amax = np.abs(w).max(1)
    byte = np.clip(np.where(amax > 0, np.frexp(amax)[1] - 1 + 127 - 7, 1), 1, 254)
    scaled = (w * np.exp2(127.0 - byte)[:, None, :]).reshape(k, n).astype(np.float32)
    words = np.ascontiguousarray(scaled.reshape(k // 512, 128, 4, n).transpose(0, 1, 3, 2)).astype(ml_dtypes.float8_e4m3fn).view(np.uint8)
    return words, np.ascontiguousarray(byte.astype(np.uint8).reshape(k // 512, 16, n))


def unpack_weight(words, scales):
    g, p, n, _ = words.shape
    vals = np.ascontiguousarray(words).view(ml_dtypes.float8_e4m3fn).astype(np.float64) * np.repeat(np.exp2(scales.astype(np.float64) - 127.0), 8, axis=1)[..., None]
    return vals.transpose(0, 1, 3, 2).reshape(g * 512, n)


E2M1 = np.array([0.0, 0.5, 1.0, 1.5, 2.0, 3.0, 4.0, 6.0, -0.0, -0.5, -1.0, -1.5, -2.0, -3.0, -4.0, -6.0])


def pack_fp4(w):
    k, n = w.shape
    w = f64(np.asarray(w, np.float32).astype(ml_dtypes.bfloat16)).reshape(k // 32, 32, n)
    amax = np.abs(w).max(1)
    mant, ex = np.frexp(amax / 6.0)
    byte = np.clip(np.where(amax > 0, np.where(mant > 0.5, ex, ex - 1) + 127, 1), 1, 254)
    scaled = (w * np.exp2(127.0 - byte)[:, None, :]).reshape(k, n).astype(np.float32)
    c = np.ascontiguousarray(scaled.reshape(k // 512, 128, 4, n).transpose(0, 1, 3, 2)).astype(ml_dtypes.float4_e2m1fn).view(np.uint8) & 0xF
    words = (c[..., 0::2] | (c[..., 1::2] << 4)).reshape(k // 512, 128, 2 * n)
    return np.ascontiguousarray(words), np.ascontiguousarray(byte.astype(np.uint8).reshape(k // 512, 16, n))


def unpack_fp4(words, scales):
    g, _, n = scales.shape
    words = np.ascontiguousarray(words).reshape(g, 128, n, 2)
    nib = np.empty((g, 128, n, 4), np.uint8)
    nib[..., 0::2] = words & 0xF
    nib[..., 1::2] = words >> 4
    vals = E2M1[nib] * np.repeat(np.exp2(scales.astype(np.float64) - 127.0), 8, axis=1)[..., None]
    return vals.transpose(0, 1, 3, 2).reshape(g * 512, n)


def planes(y):
    n, m = y.shape
    v = y.astype(np.float32).astype(ml_dtypes.bfloat16).astype(np.float64).reshape(n // 32, 32, m)
    top = np.abs(v).max(1)
    byte = np.clip(np.where(top > 0, np.frexp(top)[1] - 1 + 127 - 7, 1), 1, 254)
    codes = (v * np.exp2(127.0 - byte)[:, None, :]).reshape(n, m).astype(np.float32).astype(ml_dtypes.float8_e4m3fn).view(np.uint8)
    words = codes.reshape(n // 512, 128, 4, m).transpose(0, 1, 3, 2)
    return np.ascontiguousarray(words), np.ascontiguousarray(byte.astype(np.uint8).reshape(n // 512, 16, m))


K, T, S, H, N, D = 1024, 2048, 512, 512, 512, 2
P = 2 ** 7


def setup_inputs():
    n = np.random.standard_normal
    s = mx_kscale(K)[:, None]
    u = mx_kscale(H)
    packed_xT = pack_weight(n((K, T)) * s)
    packed_w2 = pack_fp4(n((H, N)) / np.sqrt(H) / u[:, None])
    return {
        "x_words": packed_xT[0],
        "x_scales": packed_xT[1],
        "w1": (n((K, H)) / np.sqrt(K) / s * u).astype(np.float32),
        "w2_words": packed_w2[0],
        "w2_scales": packed_w2[1],
        "gate": (np.tile(np.random.uniform(0.3, 0.7, (D, 1, S)), (1, P, 1))).astype(np.float32),
        "offs": striped(np.random.permutation(T)[:S]),
        "pos1": striped(np.random.permutation(S)[:S]),
        "pos2": striped(np.random.permutation(S)[:S]),
    }


def reference(x_words, x_scales, w1, w2_words, w2_scales, gate, offs, pos1, pos2):
    xq = unpack_weight(x_words, x_scales)[:, unstriped(offs)]
    h = mxq(f64(w1), 0, "e4m3").T @ xq
    gg = h[:, unstriped(pos1)] * f64(gate)[0, :1] + h[:, unstriped(pos2)] * f64(gate)[1, :1]
    ee = gg[:, unstriped(pos1)] * f64(gate)[0, :1] + gg[:, unstriped(pos2)] * f64(gate)[1, :1]
    z = np.maximum(np.maximum(h, gg), ee)
    out_0 = unpack_fp4(w2_words, w2_scales).T @ mxq(z, 0, "e4m3")
    return (out_0,) + planes(out_0)

@@ -1,0 +1,262 @@
+from contextlib import ExitStack
+
+import concourse.mybir as mybir
+from concourse.masks import make_identity
+
+F32 = mybir.dt.float32
+BF16 = mybir.dt.bfloat16
+I32 = mybir.dt.int32
+U32 = mybir.dt.uint32
+U16 = mybir.dt.uint16
+U8 = mybir.dt.uint8
+FP8X4 = mybir.dt.float8_e4m3fn_x4
+FP4X4 = mybir.dt.float4_e2m1fn_x4
+MULT = mybir.AluOpType.mult
+MAX = mybir.AluOpType.max
+
+P = 128
+K, T, S, H, N = 1024, 2048, 512, 512, 512
+PASSES = K // 512
+TILES = H // P
+BLOCKS = S // P
+SPARE = 16
+
+FLOPS = 2 * K * H * S + 2 * H * N * S
+
+
+def tile_picked_yjk_none_po_kernel(
+    tc, x_words, x_scales, w1, w2_words, w2_scales, gate, offs, pos1, pos2, out_0, out_1, out_2
+):
+    nc = tc.nc
+    with ExitStack() as ctx:
+        keep = ctx.enter_context(tc.tile_pool(name="keep", bufs=1))
+        shared = ctx.enter_context(tc.tile_pool(name="shared", bufs=1))
+        ring = ctx.enter_context(tc.tile_pool(name="ring", bufs=2))
+        psum = ctx.enter_context(tc.psum_pool(name="psum", bufs=2))
+
+        offs_sb = keep.tile([P, S // 16], U16, name="offs_sb")
+        pos_sb = [keep.tile([P, S // 16], U16, name=f"pos_sb{d}") for d in range(2)]
+        x_table = [shared.tile([P, T], I32, name=f"x_table{o}", offset=4 * T * o) for o in range(PASSES)]
+        xs_table = keep.tile([P, T], U8, name="xs_table")
+        w1_raw = [[keep.tile([P, 4, P], F32, name=f"w1_raw{i}_{o}") for o in range(PASSES)] for i in range(TILES)]
+        gate_sb = [keep.tile([P, S], F32, name=f"gate_sb{d}") for d in range(2)]
+        w2_raw = keep.tile([P, 2 * N], U8, name="w2_raw")
+        w2s_raw = keep.tile([P, N], U8, name="w2s_raw")
+        ident = keep.tile([P, P], F32, name="ident")
+        last = TILES - 1
+        h_sb = [keep.tile([P, S + (4 * S if i == last else SPARE)], F32, name=f"h_sb{i}") for i in range(TILES)]
+        gg_sb = [keep.tile([P, S + (4 * S if i == last else 0)], F32, name=f"gg_sb{i}") for i in range(TILES)]
+        tail_terms = keep.tile([P, 4 * P], F32, name="tail_terms")
+
+        def load_w1(i):
+            for o in range(PASSES):
+                rows = w1[512 * o : 512 * (o + 1), P * i : P * (i + 1)]
+                nc.sync.dma_start(out=w1_raw[i][o][:], in_=rows.rearrange("(p j) c -> p j c", j=4))
+
+        nc.vector.memset(xs_table[:].bitcast(I32), 0)
+        nc.sync.dma_start(offs_sb[:], offs)
+        load_w1(0)
+        nc.sync.dma_start(out=x_table[0][:], in_=x_words[0].rearrange("p n t -> p (n t)").bitcast(I32))
+        for q in range(4):
+            nc.sync.dma_start(
+                out=xs_table[32 * q : 32 * q + 4 * PASSES, :].bitcast(I32),
+                in_=x_scales[:, 4 * q : 4 * q + 4, :].bitcast(I32),
+            )
+        nc.sync.dma_start(pos_sb[0][:], pos1)
+        nc.sync.dma_start(pos_sb[1][:], pos2)
+        nc.sync.dma_start(out=x_table[1][:], in_=x_words[1].rearrange("p n t -> p (n t)").bitcast(I32))
+        nc.sync.dma_start(out=gate_sb[0][:], in_=gate[0])
+        load_w1(1)
+        nc.sync.dma_start(out=gate_sb[1][:], in_=gate[1])
+        load_w1(2)
+        load_w1(3)
+
+        nc.gpsimd.memset(w2s_raw[:].bitcast(I32), 0)
+        nc.gpsimd.dma_start(out=w2_raw[:].bitcast(I32), in_=w2_words[0].bitcast(I32))
+        for q in range(4):
+            nc.gpsimd.dma_start(
+                out=w2s_raw[32 * q : 32 * q + 4, :].bitcast(I32),
+                in_=w2_scales[0, 4 * q : 4 * q + 4, :].bitcast(I32),
+            )
+        make_identity(nc, ident[:])
+        for i in range(last):
+            nc.gpsimd.memset(h_sb[i][:, S:], 0.0)
+
+        w1_codes = keep.tile([P, TILES * PASSES * P], U32, name="w1_codes", align_bytes=64)
+        w1_scales = keep.tile([P, TILES * PASSES * P], U8, name="w1_scales", align_bytes=64)
+
+        def quantise_w1(i):
+            for o in range(PASSES):
+                grouped = ring.tile([P, P, 4], BF16, name="w1_grouped", align_bytes=64, bufs=4)
+                src = w1_raw[i][o][:].rearrange("p j c -> p c j")
+                if i == 0:
+                    nc.vector.tensor_copy(out=grouped[:], in_=src)
+                else:
+                    nc.scalar.copy(out=grouped[:], in_=src)
+                cols = slice((i * PASSES + o) * P, (i * PASSES + o + 1) * P)
+                nc.vector.quantize_mx(
+                    out=w1_codes[:, cols].bitcast(FP8X4),
+                    scales=w1_scales[:, cols],
+                    in_=grouped[:].rearrange("p c j -> p (c j)"),
+                )
+
+        quantise_w1(0)
+        xs_picked = keep.tile([P, S], U8, name="xs_picked", align_bytes=64)
+        nc.vector.tensor_copy(xs_picked[:], xs_table[:].indirect(offs_sb[:]))
+        x_picked = [keep.tile([P, S], U32, name=f"x_picked{o}", align_bytes=64) for o in range(PASSES)]
+        for o in range(PASSES):
+            nc.vector.tensor_copy(x_picked[o][:], x_table[o][:].bitcast(U32).indirect(offs_sb[:]))
+
+        def first_product(i):
+            acc = psum.tile([P, S], F32, name="acc")
+            for o in range(PASSES):
+                cols = slice((i * PASSES + o) * P, (i * PASSES + o + 1) * P)
+                nc.tensor.matmul_mx(
+                    out=acc[:],
+                    lhsT=w1_codes[:, cols].bitcast(FP8X4),
+                    lhsT_scale=w1_scales[:, cols],
+                    rhs=x_picked[o][:].bitcast(FP8X4),
+                    rhs_scale=xs_picked[4 * o : P, :],
+                    start=(o == 0),
+                    stop=(o == PASSES - 1),
+                )
+            nc.scalar.copy(out=h_sb[i][:, :S], in_=acc[:])
+
+        def weighted_neighbours(window, first, count, room, at):
+            terms = []
+            for d in range(2):
+                term = room[:, at + d * count : at + (d + 1) * count]
+                nc.vector.tensor_tensor(
+                    term,
+                    window[:].indirect(pos_sb[d][:, first // 16 : (first + count) // 16]),
+                    gate_sb[d][:, first : first + count],
+                    MULT,
+                )
+                terms.append(term)
+            return terms
+
+        def transposed_sum(out, terms, first):
+            for d in range(2):
+                nc.tensor.matmul(
+                    out, terms[d][:, first : first + P], ident[:], start=(d == 0), stop=(d == 1), is_transpose=True
+                )
+
+        ggT = keep.tile([P, BLOCKS, H], F32, name="ggT")
+        mT = keep.tile([P, BLOCKS, H], F32, name="mT")
+
+        def sum_first_hop(i, terms):
+            bank = psum.tile([P, BLOCKS, P], F32, name="summed")
+            for b in range(BLOCKS):
+                transposed_sum(bank[:, b, :], terms, P * b)
+            nc.scalar.copy(out=ggT[:, :, P * i : P * (i + 1)], in_=bank[:])
+
+        def turn_back(i):
+            bank = psum.tile([P, S], F32, name="back")
+            for b in range(BLOCKS):
+                nc.tensor.transpose(bank[:, P * b : P * (b + 1)], ggT[:, b, P * i : P * (i + 1)], ident[:])
+            nc.scalar.copy(out=gg_sb[i][:, :S], in_=bank[:])
+
+        def first_max(b):
+            bank = psum.tile([P, H], F32, name="hT")
+            for i in range(TILES):
+                nc.tensor.transpose(bank[:, P * i : P * (i + 1)], h_sb[i][:, P * b : P * (b + 1)], ident[:])
+            nc.vector.tensor_tensor(mT[:, b, :], bank[:], ggT[:, b, :], MAX)
+
+        first_product(0)
+        quantise_w1(1)
+        first_product(1)
+        for i in range(TILES):
+            room = h_sb[last] if i < 2 else gg_sb[last]
+            terms = weighted_neighbours(h_sb[i], 0, S, room, S + 2 * S * (i % 2))
+            if i + 2 < TILES:
+                quantise_w1(i + 2)
+                first_product(i + 2)
+            if i == 0:
+                w2_codes = shared.tile([P, 4, P, 2], U8, name="w2_codes", align_bytes=64, offset=4 * T)
+                w2_sc = shared.tile([P, 4, P], U8, name="w2_sc", align_bytes=64, offset=4 * T + 2 * N)
+                nc.vector.tensor_copy(out=w2_codes[:], in_=w2_raw[:].rearrange("p (m t b) -> p t m b", t=4, b=2))
+                nc.vector.tensor_copy(out=w2_sc[:], in_=w2s_raw[:].rearrange("p (m t) -> p t m", t=4))
+            sum_first_hop(i, terms)
+            turn_back(i)
+
+        y_words = keep.tile([P, S], U32, name="y_words", align_bytes=64)
+        y_scales = keep.tile([P, S], U8, name="y_scales", align_bytes=64)
+        out_rows = out_0.rearrange("(p t) n -> p t n", t=4)
+        out_words = out_1[0].rearrange("p n t -> p (n t)").bitcast(I32)
+
+        def depth_max(b, terms, first):
+            bank = psum.tile([P, TILES, P], F32, name="summed")
+            for i in range(TILES):
+                transposed_sum(bank[:, i, :], terms[i], first)
+            zT = ring.tile([P, H], BF16, name="zT")
+            nc.vector.tensor_tensor(zT[:], bank[:].rearrange("p i c -> p (i c)"), mT[:, b, :], MAX)
+            return zT
+
+        def group_z(zT):
+            bank = psum.tile([P, S], F32, name="back")
+            words = zT[:].bitcast(F32)
+            for u in range(2):
+                nc.tensor.transpose(bank[:, P * u : P * (u + 1)], words[:, u : H // 2 : 2], ident[:])
+            grouped = ring.tile([P, 4 * P], BF16, name="z_grouped", align_bytes=64)
+            nc.scalar.copy(
+                out=grouped[:].bitcast(F32).rearrange("p (n u) -> p n u", u=2),
+                in_=bank[:, : 2 * P].rearrange("p (u n) -> p n u", u=2),
+            )
+            return grouped
+
+        def second_product(b, grouped):
+            z_codes = ring.tile([P, P], U32, name="z_codes", align_bytes=64)
+            z_scales = ring.tile([P, P], U8, name="z_scales", align_bytes=64)
+            nc.vector.quantize_mx(out=z_codes[:].bitcast(FP8X4), scales=z_scales[:], in_=grouped[:])
+            acc = psum.tile([P, S], F32, name="acc")
+            for t in range(4):
+                nc.tensor.matmul_mx(
+                    out=acc[:, P * t : P * (t + 1)],
+                    lhsT=w2_codes[:, t].rearrange("p m b -> p (m b)").bitcast(FP4X4),
+                    lhsT_scale=w2_sc[:, t, :],
+                    rhs=z_codes[:].bitcast(FP8X4),
+                    rhs_scale=z_scales[:],
+                    start=True,
+                    stop=True,
+                )
+            y_grouped = ring.tile([P, P, 4], BF16, name="y_grouped", align_bytes=64)
+            nc.scalar.copy(out=y_grouped[:], in_=acc[:].rearrange("p (t n) -> p n t", t=4))
+            y = ring.tile([P, 4, P], F32, name="y")
+            nc.scalar.copy(out=y[:], in_=acc[:].rearrange("p (t n) -> p t n", t=4))
+            nc.sync.dma_start(out=out_rows[:, :, P * b : P * (b + 1)], in_=y[:])
+            return y_grouped
+
+        def planes(b, y_grouped):
+            cols = slice(P * b, P * (b + 1))
+            nc.vector.quantize_mx(
+                out=y_words[:, cols].bitcast(FP8X4),
+                scales=y_scales[:, cols],
+                in_=y_grouped[:].rearrange("p n t -> p (n t)"),
+            )
+            nc.sync.dma_start(out=out_words[:, cols], in_=y_words[:, cols].bitcast(I32))
+
+        def finish(b, terms, first):
+            planes(b, second_product(b, group_z(depth_max(b, terms, first))))
+
+        wide = [weighted_neighbours(gg_sb[i], 0, 2 * P, h_sb[last], S + 4 * P * i) for i in range(TILES)]
+        first_max(0)
+        first_max(1)
+        narrow = []
+        for n in range(2):
+            b = 2 + n
+            terms = [weighted_neighbours(gg_sb[i], P * b, P, gg_sb[last], S + 2 * S * n + 2 * P * i) for i in range(last)]
+            terms.append(weighted_neighbours(gg_sb[last], P * b, P, tail_terms, 2 * P * n))
+            narrow.append(terms)
+            if n == 0:
+                finish(0, wide, 0)
+                finish(1, wide, P)
+            first_max(b)
+        finish(2, narrow[0], 0)
+        finish(3, narrow[1], 0)
+
+        for q in range(4):
+            queue = nc.sync if q % 2 == 0 else nc.scalar
+            queue.dma_start(
+                out=out_2[0, 4 * q : 4 * q + 4, :].bitcast(I32),
+                in_=y_scales[32 * q : 32 * q + 4, :].bitcast(I32),
+            )

@@ -38,14 +38,14 @@ def tile_picked_yjk_none_po_kernel(
         pos_sb = [keep.tile([P, S // 16], U16, name=f"pos_sb{d}") for d in range(2)]
         x_table = [shared.tile([P, T], I32, name=f"x_table{o}", offset=4 * T * o) for o in range(PASSES)]
         xs_table = keep.tile([P, T], U8, name="xs_table")
-        w1_raw = [[keep.tile([P, 4, P], F32, name=f"w1_raw{i}_{o}") for o in range(PASSES)] for i in range(TILES)]
+        w1_raw = [[keep.tile([P, 4, P], F32, name=f"w1_raw{i}_{o}") for o in range(PASSES)] for i in range(2)]
         gate_sb = [keep.tile([P, S], F32, name=f"gate_sb{d}") for d in range(2)]
         w2_raw = keep.tile([P, 2 * N], U8, name="w2_raw")
         w2s_raw = keep.tile([P, N], U8, name="w2s_raw")
         ident = keep.tile([P, P], F32, name="ident")
         last = TILES - 1
-        h_sb = [keep.tile([P, S + (4 * S if i == last else SPARE)], F32, name=f"h_sb{i}") for i in range(TILES)]
-        gg_sb = [keep.tile([P, S + (4 * S if i == last else 0)], F32, name=f"gg_sb{i}") for i in range(TILES)]
+        h_sb = [keep.tile([P, S + (2 * S if i == last else SPARE)], F32, name=f"h_sb{i}", align_bytes=64) for i in range(TILES)]
+        gg_sb = [keep.tile([P, S], F32, name=f"gg_sb{i}") for i in range(last)]
         tail_terms = keep.tile([P, 4 * P], F32, name="tail_terms")
 
         def load_w1(i):
@@ -53,8 +53,10 @@ def tile_picked_yjk_none_po_kernel(
                 rows = w1[512 * o : 512 * (o + 1), P * i : P * (i + 1)]
                 nc.sync.dma_start(out=w1_raw[i][o][:], in_=rows.rearrange("(p j) c -> p j c", j=4))
 
-        nc.vector.memset(xs_table[:].bitcast(I32), 0)
+        nc.gpsimd.memset(xs_table[:].bitcast(I32), 0)
+        nc.gpsimd.memset(w2s_raw[:].bitcast(I32), 0)
         nc.sync.dma_start(offs_sb[:], offs)
+        nc.sync.dma_start(out=w2_raw[:].bitcast(I32), in_=w2_words[0].bitcast(I32))
         load_w1(0)
         nc.sync.dma_start(out=x_table[0][:], in_=x_words[0].rearrange("p n t -> p (n t)").bitcast(I32))
         for q in range(4):
@@ -65,47 +67,61 @@ def tile_picked_yjk_none_po_kernel(
         nc.sync.dma_start(pos_sb[0][:], pos1)
         nc.sync.dma_start(pos_sb[1][:], pos2)
         nc.sync.dma_start(out=x_table[1][:], in_=x_words[1].rearrange("p n t -> p (n t)").bitcast(I32))
-        nc.sync.dma_start(out=gate_sb[0][:], in_=gate[0])
         load_w1(1)
+        nc.sync.dma_start(out=gate_sb[0][:], in_=gate[0])
         nc.sync.dma_start(out=gate_sb[1][:], in_=gate[1])
-        load_w1(2)
-        load_w1(3)
 
-        nc.gpsimd.memset(w2s_raw[:].bitcast(I32), 0)
-        nc.gpsimd.dma_start(out=w2_raw[:].bitcast(I32), in_=w2_words[0].bitcast(I32))
         for q in range(4):
             nc.gpsimd.dma_start(
                 out=w2s_raw[32 * q : 32 * q + 4, :].bitcast(I32),
                 in_=w2_scales[0, 4 * q : 4 * q + 4, :].bitcast(I32),
             )
-        make_identity(nc, ident[:])
+        w2_sc = keep.tile([P, 4, P], U8, name="w2_sc", align_bytes=64)
+        nc.gpsimd.tensor_copy(out=w2_sc[:], in_=w2s_raw[:].rearrange("p (m t) -> p t m", t=4))
         for i in range(last):
             nc.gpsimd.memset(h_sb[i][:, S:], 0.0)
+        make_identity(nc, ident[:])
 
         w1_codes = keep.tile([P, TILES * PASSES * P], U32, name="w1_codes", align_bytes=64)
         w1_scales = keep.tile([P, TILES * PASSES * P], U8, name="w1_scales", align_bytes=64)
 
-        def quantise_w1(i):
-            for o in range(PASSES):
-                grouped = ring.tile([P, P, 4], BF16, name="w1_grouped", align_bytes=64, bufs=4)
-                src = w1_raw[i][o][:].rearrange("p j c -> p c j")
-                if i == 0:
-                    nc.vector.tensor_copy(out=grouped[:], in_=src)
-                else:
-                    nc.scalar.copy(out=grouped[:], in_=src)
-                cols = slice((i * PASSES + o) * P, (i * PASSES + o + 1) * P)
-                nc.vector.quantize_mx(
-                    out=w1_codes[:, cols].bitcast(FP8X4),
-                    scales=w1_scales[:, cols],
-                    in_=grouped[:].rearrange("p c j -> p (c j)"),
-                )
+        grouped_at = [9 * T, 8 * T - 1024, 10 * T, 12 * T]
+        w1_grouped = [
+            shared.tile([P, PASSES * 4 * P], BF16, name=f"w1_grouped{i}", align_bytes=64, offset=grouped_at[i])
+            for i in range(TILES)
+        ]
 
-        quantise_w1(0)
+        def group_w1(i, o, copy):
+            copy(
+                out=w1_grouped[i][:, 512 * o : 512 * (o + 1)].rearrange("p (c e j) -> p c j e", e=4, j=4),
+                in_=w1_raw[i][o][:].rearrange("p j (c e) -> p c j e", e=4),
+            )
+
+        def quantise_w1(i, first, count):
+            cols = slice((i * PASSES + first) * P, (i * PASSES + first + count) * P)
+            nc.vector.quantize_mx(
+                out=w1_codes[:, cols].bitcast(FP8X4),
+                scales=w1_scales[:, cols],
+                in_=w1_grouped[i][:, 512 * first : 512 * (first + count)],
+            )
+
+        for o in range(PASSES):
+            group_w1(0, o, nc.vector.tensor_copy)
+        quantise_w1(0, 0, PASSES)
+        w2_codes = keep.tile([P, 4, P, 2], U8, name="w2_codes", align_bytes=64)
+        nc.vector.tensor_copy(out=w2_codes[:], in_=w2_raw[:].rearrange("p (m t b) -> p t m b", t=4, b=2))
         xs_picked = keep.tile([P, S], U8, name="xs_picked", align_bytes=64)
         nc.vector.tensor_copy(xs_picked[:], xs_table[:].indirect(offs_sb[:]))
         x_picked = [keep.tile([P, S], U32, name=f"x_picked{o}", align_bytes=64) for o in range(PASSES)]
         for o in range(PASSES):
             nc.vector.tensor_copy(x_picked[o][:], x_table[o][:].bitcast(U32).indirect(offs_sb[:]))
+
+        for i in range(2, TILES):
+            w1_raw.append([
+                shared.tile([P, 4, P], F32, name=f"w1_raw{i}_{o}", align_bytes=64, offset=4 * T - 1024 + 2048 * (2 * (i - 2) + o))
+                for o in range(PASSES)
+            ])
+            load_w1(i)
 
         def first_product(i):
             acc = psum.tile([P, S], F32, name="acc")
@@ -142,7 +158,10 @@ def tile_picked_yjk_none_po_kernel(
                 )
 
         ggT = keep.tile([P, BLOCKS, H], F32, name="ggT")
-        mT = keep.tile([P, BLOCKS, H], F32, name="mT")
+        mT_early = keep.tile([P, BLOCKS - 1, H], F32, name="mT_early")
+
+        def mT(b):
+            return mT_early[:, b, :] if b < BLOCKS - 1 else gg_sb[last][:, 4 * S :]
 
         def sum_first_hop(i, terms):
             bank = psum.tile([P, BLOCKS, P], F32, name="summed")
@@ -160,22 +179,24 @@ def tile_picked_yjk_none_po_kernel(
             bank = psum.tile([P, H], F32, name="hT")
             for i in range(TILES):
                 nc.tensor.transpose(bank[:, P * i : P * (i + 1)], h_sb[i][:, P * b : P * (b + 1)], ident[:])
-            nc.vector.tensor_tensor(mT[:, b, :], bank[:], ggT[:, b, :], MAX)
+            nc.vector.tensor_tensor(mT(b), bank[:], ggT[:, b, :], MAX)
 
         first_product(0)
-        quantise_w1(1)
-        first_product(1)
+        def hidden_tile(i, copy):
+            for o in range(PASSES):
+                group_w1(i, o, copy)
+            quantise_w1(i, 0, PASSES)
+            first_product(i)
+
+        hidden_tile(1, nc.vector.tensor_copy)
+        hidden_tile(2, nc.scalar.copy)
+        gg_sb.append(shared.tile([P, 5 * S], F32, name="gg_last", align_bytes=64, offset=grouped_at[3]))
+        second_room = shared.tile([P, 2 * S], F32, name="second_room", align_bytes=64, offset=grouped_at[2])
+        rooms = [h_sb[last][:, S:], second_room[:], gg_sb[last][:, S : 3 * S], gg_sb[last][:, 3 * S :]]
         for i in range(TILES):
-            room = h_sb[last] if i < 2 else gg_sb[last]
-            terms = weighted_neighbours(h_sb[i], 0, S, room, S + 2 * S * (i % 2))
-            if i + 2 < TILES:
-                quantise_w1(i + 2)
-                first_product(i + 2)
+            terms = weighted_neighbours(h_sb[i], 0, S, rooms[i], 0)
             if i == 0:
-                w2_codes = shared.tile([P, 4, P, 2], U8, name="w2_codes", align_bytes=64, offset=4 * T)
-                w2_sc = shared.tile([P, 4, P], U8, name="w2_sc", align_bytes=64, offset=4 * T + 2 * N)
-                nc.vector.tensor_copy(out=w2_codes[:], in_=w2_raw[:].rearrange("p (m t b) -> p t m b", t=4, b=2))
-                nc.vector.tensor_copy(out=w2_sc[:], in_=w2s_raw[:].rearrange("p (m t) -> p t m", t=4))
+                hidden_tile(last, nc.scalar.copy)
             sum_first_hop(i, terms)
             turn_back(i)
 
@@ -189,7 +210,7 @@ def tile_picked_yjk_none_po_kernel(
             for i in range(TILES):
                 transposed_sum(bank[:, i, :], terms[i], first)
             zT = ring.tile([P, H], BF16, name="zT")
-            nc.vector.tensor_tensor(zT[:], bank[:].rearrange("p i c -> p (i c)"), mT[:, b, :], MAX)
+            nc.vector.tensor_tensor(zT[:], bank[:].rearrange("p i c -> p (i c)"), mT(b), MAX)
             return zT
 
         def group_z(zT):
@@ -220,10 +241,16 @@ def tile_picked_yjk_none_po_kernel(
                     stop=True,
                 )
             y_grouped = ring.tile([P, P, 4], BF16, name="y_grouped", align_bytes=64)
-            nc.scalar.copy(out=y_grouped[:], in_=acc[:].rearrange("p (t n) -> p n t", t=4))
             y = ring.tile([P, 4, P], F32, name="y")
             nc.scalar.copy(out=y[:], in_=acc[:].rearrange("p (t n) -> p t n", t=4))
             nc.sync.dma_start(out=out_rows[:, :, P * b : P * (b + 1)], in_=y[:])
+            if b < 2:
+                nc.scalar.copy(out=y_grouped[:], in_=acc[:].rearrange("p (t n) -> p n t", t=4))
+            else:
+                nc.vector.tensor_copy(
+                    out=y_grouped[:].rearrange("p (c e) t -> p c t e", e=4),
+                    in_=y[:].rearrange("p t (c e) -> p c t e", e=4),
+                )
             return y_grouped
 
         def planes(b, y_grouped):
@@ -238,21 +265,17 @@ def tile_picked_yjk_none_po_kernel(
         def finish(b, terms, first):
             planes(b, second_product(b, group_z(depth_max(b, terms, first))))
 
-        wide = [weighted_neighbours(gg_sb[i], 0, 2 * P, h_sb[last], S + 4 * P * i) for i in range(TILES)]
+        wide = [weighted_neighbours(gg_sb[i], 0, 2 * P, rooms[i // 2], S * (i % 2)) for i in range(TILES)]
         first_max(0)
         first_max(1)
-        narrow = []
-        for n in range(2):
-            b = 2 + n
-            terms = [weighted_neighbours(gg_sb[i], P * b, P, gg_sb[last], S + 2 * S * n + 2 * P * i) for i in range(last)]
-            terms.append(weighted_neighbours(gg_sb[last], P * b, P, tail_terms, 2 * P * n))
-            narrow.append(terms)
-            if n == 0:
-                finish(0, wide, 0)
-                finish(1, wide, P)
-            first_max(b)
-        finish(2, narrow[0], 0)
-        finish(3, narrow[1], 0)
+        finish(0, wide, 0)
+        finish(1, wide, P)
+        first_max(2)
+        late = [weighted_neighbours(gg_sb[i], 2 * P, 2 * P, gg_sb[last], S + 4 * P * i) for i in range(last)]
+        late.append(weighted_neighbours(gg_sb[last], 2 * P, 2 * P, tail_terms, 0))
+        first_max(3)
+        finish(2, late, 0)
+        finish(3, late, P)
 
         for q in range(4):
             queue = nc.sync if q % 2 == 0 else nc.scalar

@@ -32,104 +32,134 @@ def tile_picked_yjk_none_po_kernel(
         keep = ctx.enter_context(tc.tile_pool(name="keep", bufs=1))
         shared = ctx.enter_context(tc.tile_pool(name="shared", bufs=1))
         ring = ctx.enter_context(tc.tile_pool(name="ring", bufs=2))
-        psum = ctx.enter_context(tc.psum_pool(name="psum", bufs=2))
+        psum = ctx.enter_context(tc.psum_pool(name="psum", bufs=1))
+
+        def bank_tile(bank, name):
+            return psum.tile([P, 512], F32, name=name, offset=2048 * bank)
 
         offs_sb = keep.tile([P, S // 16], U16, name="offs_sb")
         pos_sb = [keep.tile([P, S // 16], U16, name=f"pos_sb{d}") for d in range(2)]
-        x_table = [shared.tile([P, T], I32, name=f"x_table{o}", offset=4 * T * o) for o in range(PASSES)]
+        x_table = []
         xs_table = keep.tile([P, T], U8, name="xs_table")
-        w1_raw = [[keep.tile([P, 4, P], F32, name=f"w1_raw{i}_{o}") for o in range(PASSES)] for i in range(2)]
+        raw_at = 8 * T
+        w1_raw = [[None, None] for i in range(TILES)]
+        gate_rows = keep.tile([P, P], F32, name="gate_rows")
         gate_sb = [keep.tile([P, S], F32, name=f"gate_sb{d}") for d in range(2)]
-        w2_raw = keep.tile([P, 2 * N], U8, name="w2_raw")
-        w2s_raw = keep.tile([P, N], U8, name="w2s_raw")
+        w2_sc = keep.tile([P, N], U8, name="w2_sc", align_bytes=64)
         ident = keep.tile([P, P], F32, name="ident")
-        last = TILES - 1
-        h_sb = [keep.tile([P, S + (2 * S if i == last else SPARE)], F32, name=f"h_sb{i}", align_bytes=64) for i in range(TILES)]
-        gg_sb = [keep.tile([P, S], F32, name=f"gg_sb{i}") for i in range(last)]
-        tail_terms = keep.tile([P, 4 * P], F32, name="tail_terms")
+        h_sb = [keep.tile([P, S + SPARE], F32, name=f"h_sb{i}", align_bytes=64) for i in range(TILES)]
+        gg_sb = [keep.tile([P, S], F32, name=f"gg_sb{i}") for i in range(TILES)]
 
-        def load_w1(i):
-            for o in range(PASSES):
-                rows = w1[512 * o : 512 * (o + 1), P * i : P * (i + 1)]
-                nc.sync.dma_start(out=w1_raw[i][o][:], in_=rows.rearrange("(p j) c -> p j c", j=4))
+        def load_w1(i, o):
+            offset = raw_at + 4096 * i + 2048 * o
+            w1_raw[i][o] = shared.tile([P, 4, P], F32, name=f"w1_raw{i}_{o}", offset=offset, align_bytes=64)
+            rows = w1[512 * o : 512 * (o + 1), P * i : P * (i + 1)]
+            nc.sync.dma_start(out=w1_raw[i][o][:], in_=rows.rearrange("(p j) c -> p j c", j=4))
+
+        def load_x(o):
+            x_table.append(shared.tile([P, T], I32, name=f"x_table{o}", offset=4 * T * o, align_bytes=64))
+            nc.sync.dma_start(out=x_table[o][:], in_=x_words[o].rearrange("p n t -> p (n t)").bitcast(I32))
 
         nc.gpsimd.memset(xs_table[:].bitcast(I32), 0)
-        nc.gpsimd.memset(w2s_raw[:].bitcast(I32), 0)
+        nc.vector.memset(gate_rows[:], 0.0)
+        w2s_raw = keep.tile([P, N], U8, name="w2s_raw")
+        nc.vector.memset(w2s_raw[:].bitcast(I32), 0)
+        make_identity(nc, ident[:])
+        nc.gpsimd.memset(w2_sc[:].bitcast(I32), 0)
+        for i in range(TILES):
+            nc.gpsimd.memset(h_sb[i][:, S:], 0.0)
+
         nc.sync.dma_start(offs_sb[:], offs)
+        w2_raw = keep.tile([P, 2 * N], U8, name="w2_raw")
         nc.sync.dma_start(out=w2_raw[:].bitcast(I32), in_=w2_words[0].bitcast(I32))
-        load_w1(0)
-        nc.sync.dma_start(out=x_table[0][:], in_=x_words[0].rearrange("p n t -> p (n t)").bitcast(I32))
+        load_w1(0, 0)
+        load_w1(0, 1)
+        load_x(0)
         for q in range(4):
             nc.sync.dma_start(
                 out=xs_table[32 * q : 32 * q + 4 * PASSES, :].bitcast(I32),
                 in_=x_scales[:, 4 * q : 4 * q + 4, :].bitcast(I32),
             )
+        nc.sync.dma_start(out=gate_rows[: 2 * BLOCKS, :], in_=gate[:, 0, :].rearrange("d (b c) -> d b c", c=P))
+        load_x(1)
         nc.sync.dma_start(pos_sb[0][:], pos1)
         nc.sync.dma_start(pos_sb[1][:], pos2)
-        nc.sync.dma_start(out=x_table[1][:], in_=x_words[1].rearrange("p n t -> p (n t)").bitcast(I32))
-        load_w1(1)
-        nc.sync.dma_start(out=gate_sb[0][:], in_=gate[0])
-        nc.sync.dma_start(out=gate_sb[1][:], in_=gate[1])
+        for i in range(1, TILES):
+            for o in range(PASSES):
+                load_w1(i, o)
+            if i == 1:
+                nc.sync.dma_start(out=w2s_raw[:16, :].bitcast(I32), in_=w2_scales[0].bitcast(I32))
 
-        for q in range(4):
-            nc.gpsimd.dma_start(
-                out=w2s_raw[32 * q : 32 * q + 4, :].bitcast(I32),
-                in_=w2_scales[0, 4 * q : 4 * q + 4, :].bitcast(I32),
-            )
-        w2_sc = keep.tile([P, 4, P], U8, name="w2_sc", align_bytes=64)
-        nc.gpsimd.tensor_copy(out=w2_sc[:], in_=w2s_raw[:].rearrange("p (m t) -> p t m", t=4))
-        for i in range(last):
-            nc.gpsimd.memset(h_sb[i][:, S:], 0.0)
-        make_identity(nc, ident[:])
+        gate_cols = keep.tile([P, 2 * BLOCKS], F32, name="gate_cols")
+        turned = bank_tile(2, "turned")
+        nc.tensor.transpose(turned[:, :P], gate_rows[:], ident[:])
+        nc.scalar.copy(out=gate_cols[:], in_=turned[:, : 2 * BLOCKS])
+        for d in range(2):
+            spread = bank_tile(d, f"spread{d}")
+            for b in range(BLOCKS):
+                j = BLOCKS * d + b
+                nc.tensor.transpose(spread[:, P * b : P * (b + 1)], gate_cols[:, j : j + 1].to_broadcast([P, P]), ident[:])
+            nc.scalar.copy(out=gate_sb[d][:], in_=spread[:])
 
-        w1_codes = keep.tile([P, TILES * PASSES * P], U32, name="w1_codes", align_bytes=64)
+        at = 4 * T
+        codes_at = [None, None, None, None]
+        chain_at = at + 4096
+        grouped_at = [None, chain_at, chain_at, chain_at + 2048]
+        grouped_extent = [2, 4, 2, 2]
+
+        def place(pool_tile_shape, dtype, name, offset):
+            if offset is None:
+                return keep.tile(pool_tile_shape, dtype, name=name, align_bytes=64)
+            return shared.tile(pool_tile_shape, dtype, name=name, align_bytes=64, offset=offset)
+
         w1_scales = keep.tile([P, TILES * PASSES * P], U8, name="w1_scales", align_bytes=64)
-
-        grouped_at = [9 * T, 8 * T - 1024, 10 * T, 12 * T]
-        w1_grouped = [
-            shared.tile([P, PASSES * 4 * P], BF16, name=f"w1_grouped{i}", align_bytes=64, offset=grouped_at[i])
-            for i in range(TILES)
-        ]
+        w1_codes = {}
+        w1_grouped = {}
 
         def group_w1(i, o, copy):
             copy(
-                out=w1_grouped[i][:, 512 * o : 512 * (o + 1)].rearrange("p (c e j) -> p c j e", e=4, j=4),
+                out=w1_grouped[i, o].rearrange("p (c e j) -> p c j e", e=4, j=4),
                 in_=w1_raw[i][o][:].rearrange("p j (c e) -> p c j e", e=4),
             )
 
-        def quantise_w1(i, first, count):
+        def quantise_w1(i, first, count, grouped, codes):
             cols = slice((i * PASSES + first) * P, (i * PASSES + first + count) * P)
             nc.vector.quantize_mx(
-                out=w1_codes[:, cols].bitcast(FP8X4),
+                out=codes[:].bitcast(FP8X4),
                 scales=w1_scales[:, cols],
-                in_=w1_grouped[i][:, 512 * first : 512 * (first + count)],
+                in_=grouped,
             )
+            for o in range(count):
+                w1_codes[i, first + o] = codes[:, P * o : P * (o + 1)]
 
-        for o in range(PASSES):
-            group_w1(0, o, nc.vector.tensor_copy)
-        quantise_w1(0, 0, PASSES)
+        xs_picked = keep.tile([P, S], U8, name="xs_picked", align_bytes=64)
+        x_picked = [keep.tile([P, S], U32, name=f"x_picked{o}", align_bytes=64) for o in range(PASSES)]
         w2_codes = keep.tile([P, 4, P, 2], U8, name="w2_codes", align_bytes=64)
         nc.vector.tensor_copy(out=w2_codes[:], in_=w2_raw[:].rearrange("p (m t b) -> p t m b", t=4, b=2))
-        xs_picked = keep.tile([P, S], U8, name="xs_picked", align_bytes=64)
-        nc.vector.tensor_copy(xs_picked[:], xs_table[:].indirect(offs_sb[:]))
-        x_picked = [keep.tile([P, S], U32, name=f"x_picked{o}", align_bytes=64) for o in range(PASSES)]
+        early = place([P, PASSES * 512], BF16, "w1_grouped0", None)
         for o in range(PASSES):
-            nc.vector.tensor_copy(x_picked[o][:], x_table[o][:].bitcast(U32).indirect(offs_sb[:]))
-
-        for i in range(2, TILES):
-            w1_raw.append([
-                shared.tile([P, 4, P], F32, name=f"w1_raw{i}_{o}", align_bytes=64, offset=4 * T - 1024 + 2048 * (2 * (i - 2) + o))
-                for o in range(PASSES)
-            ])
-            load_w1(i)
+            w1_grouped[0, o] = early[:, 512 * o : 512 * (o + 1)]
+            group_w1(0, o, nc.vector.tensor_copy)
+        quantise_w1(0, 0, PASSES, early[:], place([P, PASSES * P], U32, "w1_codes0", None))
+        nc.vector.tensor_copy(x_picked[0][:], x_table[0][:].bitcast(U32).indirect(offs_sb[:]))
+        nc.vector.tensor_copy(xs_picked[:], xs_table[:].indirect(offs_sb[:]))
+        nc.vector.tensor_copy(x_picked[1][:], x_table[1][:].bitcast(U32).indirect(offs_sb[:]))
+        w2s_dealt = shared.tile([P, N], U8, name="w2s_dealt", align_bytes=64, offset=at)
+        nc.vector.tensor_copy(
+            out=w2s_dealt[:].rearrange("p (t m) -> p t m", t=4), in_=w2s_raw[:].rearrange("p (m t) -> p t m", t=4)
+        )
+        for q in range(4):
+            nc.sync.dma_start(
+                out=w2_sc[32 * q : 32 * q + 4, :].bitcast(I32), in_=w2s_dealt[4 * q : 4 * q + 4, :].bitcast(I32)
+            )
 
         def first_product(i):
-            acc = psum.tile([P, S], F32, name="acc")
+            acc = bank_tile(i % 2, f"acc{i}")
             for o in range(PASSES):
                 cols = slice((i * PASSES + o) * P, (i * PASSES + o + 1) * P)
                 nc.tensor.matmul_mx(
                     out=acc[:],
-                    lhsT=w1_codes[:, cols].bitcast(FP8X4),
+                    lhsT=w1_codes[i, o].bitcast(FP8X4),
                     lhsT_scale=w1_scales[:, cols],
                     rhs=x_picked[o][:].bitcast(FP8X4),
                     rhs_scale=xs_picked[4 * o : P, :],
@@ -138,18 +168,23 @@ def tile_picked_yjk_none_po_kernel(
                 )
             nc.scalar.copy(out=h_sb[i][:, :S], in_=acc[:])
 
-        def weighted_neighbours(window, first, count, room, at):
-            terms = []
+        def hidden_tile(i, copy):
+            extent = place([P, grouped_extent[i] * 512], BF16, f"w1_grouped{i}", grouped_at[i])
+            grouped = extent[:, : PASSES * 512]
+            for o in range(PASSES):
+                w1_grouped[i, o] = grouped[:, 512 * o : 512 * (o + 1)]
+                group_w1(i, o, copy)
+            quantise_w1(i, 0, PASSES, grouped, place([P, PASSES * P], U32, f"w1_codes{i}", codes_at[i]))
+            first_product(i)
+
+        def weighted_neighbours(window, first, count, rooms):
             for d in range(2):
-                term = room[:, at + d * count : at + (d + 1) * count]
                 nc.vector.tensor_tensor(
-                    term,
+                    rooms[d],
                     window[:].indirect(pos_sb[d][:, first // 16 : (first + count) // 16]),
                     gate_sb[d][:, first : first + count],
                     MULT,
                 )
-                terms.append(term)
-            return terms
 
         def transposed_sum(out, terms, first):
             for d in range(2):
@@ -157,129 +192,140 @@ def tile_picked_yjk_none_po_kernel(
                     out, terms[d][:, first : first + P], ident[:], start=(d == 0), stop=(d == 1), is_transpose=True
                 )
 
-        ggT = keep.tile([P, BLOCKS, H], F32, name="ggT")
-        mT_early = keep.tile([P, BLOCKS - 1, H], F32, name="mT_early")
+        mT = keep.tile([P, BLOCKS * H], F32, name="mT")
+        ggT = []
 
-        def mT(b):
-            return mT_early[:, b, :] if b < BLOCKS - 1 else gg_sb[last][:, 4 * S :]
-
-        def sum_first_hop(i, terms):
-            bank = psum.tile([P, BLOCKS, P], F32, name="summed")
+        def first_round(i, terms):
+            weighted_neighbours(h_sb[i], 0, S, terms)
+            bank = bank_tile([2, 0, 1, 2][i], f"first_sum{i}")
             for b in range(BLOCKS):
-                transposed_sum(bank[:, b, :], terms, P * b)
-            nc.scalar.copy(out=ggT[:, :, P * i : P * (i + 1)], in_=bank[:])
-
-        def turn_back(i):
-            bank = psum.tile([P, S], F32, name="back")
+                transposed_sum(bank[:, P * b : P * (b + 1)], terms, P * b)
+            ggT.append(shared.tile([P, S], F32, name=f"ggT{i}", align_bytes=64, offset=raw_at + 3 * 4096 + 2048 * i))
+            nc.scalar.copy(out=ggT[i][:], in_=bank[:])
+            bank = bank_tile(3 + i % 2, f"back{i}")
             for b in range(BLOCKS):
-                nc.tensor.transpose(bank[:, P * b : P * (b + 1)], ggT[:, b, P * i : P * (i + 1)], ident[:])
-            nc.scalar.copy(out=gg_sb[i][:, :S], in_=bank[:])
-
-        def first_max(b):
-            bank = psum.tile([P, H], F32, name="hT")
-            for i in range(TILES):
-                nc.tensor.transpose(bank[:, P * i : P * (i + 1)], h_sb[i][:, P * b : P * (b + 1)], ident[:])
-            nc.vector.tensor_tensor(mT(b), bank[:], ggT[:, b, :], MAX)
+                nc.tensor.transpose(bank[:, P * b : P * (b + 1)], ggT[i][:, P * b : P * (b + 1)], ident[:])
+            nc.scalar.copy(out=gg_sb[i][:], in_=bank[:])
 
         first_product(0)
-        def hidden_tile(i, copy):
-            for o in range(PASSES):
-                group_w1(i, o, copy)
-            quantise_w1(i, 0, PASSES)
-            first_product(i)
-
         hidden_tile(1, nc.vector.tensor_copy)
         hidden_tile(2, nc.scalar.copy)
-        gg_sb.append(shared.tile([P, 5 * S], F32, name="gg_last", align_bytes=64, offset=grouped_at[3]))
-        second_room = shared.tile([P, 2 * S], F32, name="second_room", align_bytes=64, offset=grouped_at[2])
-        rooms = [h_sb[last][:, S:], second_room[:], gg_sb[last][:, S : 3 * S], gg_sb[last][:, 3 * S :]]
+        hidden_tile(3, nc.scalar.copy)
+        terms_at = [None, chain_at, chain_at + 2048, None]
         for i in range(TILES):
-            terms = weighted_neighbours(h_sb[i], 0, S, rooms[i], 0)
-            if i == 0:
-                hidden_tile(last, nc.scalar.copy)
-            sum_first_hop(i, terms)
-            turn_back(i)
+            first = place([P, S], F32, f"first_term{i}", terms_at[i])
+            second = place([P, S], F32, f"second_term{i}", None)
+            first_round(i, [first[:], second[:]])
+
+        def pairs(ap):
+            return ap.rearrange("n (p u e) -> n u p e", u=2, e=2)
+
+        def sorted_pairs(ap):
+            return ap.rearrange("n (u p e) -> n u p e", u=2, e=2)
+
+        def first_max(i):
+            bank = bank_tile(5 + i % 2, f"hT{i}")
+            for b in range(BLOCKS):
+                nc.tensor.transpose(bank[:, P * b : P * (b + 1)], h_sb[i][:, P * b : P * (b + 1)], ident[:])
+            sorted_out = mT[:].rearrange("n (b u p e) -> n u b p e", b=BLOCKS, u=2, e=2)[:, :, :, 32 * i : 32 * (i + 1), :]
+            nc.vector.tensor_tensor(
+                sorted_out,
+                bank[:].rearrange("n (b p u e) -> n u b p e", b=BLOCKS, u=2, e=2),
+                ggT[i][:].rearrange("n (b p u e) -> n u b p e", b=BLOCKS, u=2, e=2),
+                MAX,
+            )
 
         y_words = keep.tile([P, S], U32, name="y_words", align_bytes=64)
         y_scales = keep.tile([P, S], U8, name="y_scales", align_bytes=64)
         out_rows = out_0.rearrange("(p t) n -> p t n", t=4)
         out_words = out_1[0].rearrange("p n t -> p (n t)").bitcast(I32)
+        zT = [keep.tile([P, H], BF16, name=f"zT{b}") for b in range(BLOCKS)]
+        z_grouped = [keep.tile([P, 4 * c], BF16, name=f"z_grouped{c}_{k}", align_bytes=64) for k, c in enumerate((2 * P, P, P))]
+        y_grouped = [keep.tile([P, 4 * c], BF16, name=f"y_grouped{c}_{k}", align_bytes=64) for k, c in enumerate((2 * P, P, P))]
+        z_codes = keep.tile([P, S], U32, name="z_codes", align_bytes=64)
+        z_scales = keep.tile([P, S], U8, name="z_scales", align_bytes=64)
+        summed = {}
 
-        def depth_max(b, terms, first):
-            bank = psum.tile([P, TILES, P], F32, name="summed")
-            for i in range(TILES):
-                transposed_sum(bank[:, i, :], terms[i], first)
-            zT = ring.tile([P, H], BF16, name="zT")
-            nc.vector.tensor_tensor(zT[:], bank[:].rearrange("p i c -> p (i c)"), mT(b), MAX)
-            return zT
+        def second_round(i, blocks, terms):
+            weighted_neighbours(gg_sb[i], P * blocks[0], P * len(blocks), terms)
+            for k, b in enumerate(blocks):
+                if b not in summed:
+                    summed[b] = bank_tile([4, 3, 1, 2][b], f"second_sum{b}")
+                transposed_sum(summed[b][:, P * i : P * (i + 1)], terms, P * k)
 
-        def group_z(zT):
-            bank = psum.tile([P, S], F32, name="back")
-            words = zT[:].bitcast(F32)
-            for u in range(2):
-                nc.tensor.transpose(bank[:, P * u : P * (u + 1)], words[:, u : H // 2 : 2], ident[:])
-            grouped = ring.tile([P, 4 * P], BF16, name="z_grouped", align_bytes=64)
+        def depth_max(b):
+            nc.vector.tensor_tensor(sorted_pairs(zT[b][:]), pairs(summed[b][:]), sorted_pairs(mT[:, H * b : H * (b + 1)]), MAX)
+
+        def quantise_z(k, blocks):
+            bank = bank_tile([7, 0, 7][k], f"z_back{k}")
+            count = len(blocks)
+            for j, b in enumerate(blocks):
+                words = zT[b][:].bitcast(F32)
+                for u in range(2):
+                    at_bank = P * (count * u + j)
+                    nc.tensor.transpose(bank[:, at_bank : at_bank + P], words[:, P * u : P * (u + 1)], ident[:])
             nc.scalar.copy(
-                out=grouped[:].bitcast(F32).rearrange("p (n u) -> p n u", u=2),
-                in_=bank[:, : 2 * P].rearrange("p (u n) -> p n u", u=2),
+                out=z_grouped[k][:].bitcast(F32).rearrange("p (n u) -> p n u", u=2),
+                in_=bank[:, : 2 * P * count].rearrange("p (u n) -> p n u", u=2),
             )
-            return grouped
+            cols = slice(P * blocks[0], P * (blocks[0] + count))
+            nc.vector.quantize_mx(out=z_codes[:, cols].bitcast(FP8X4), scales=z_scales[:, cols], in_=z_grouped[k][:])
 
-        def second_product(b, grouped):
-            z_codes = ring.tile([P, P], U32, name="z_codes", align_bytes=64)
-            z_scales = ring.tile([P, P], U8, name="z_scales", align_bytes=64)
-            nc.vector.quantize_mx(out=z_codes[:].bitcast(FP8X4), scales=z_scales[:], in_=grouped[:])
-            acc = psum.tile([P, S], F32, name="acc")
+        def second_product(b, rounded, round_copy):
+            cols = slice(P * b, P * (b + 1))
+            acc = bank_tile([4, 3, 5, 6][b], f"y_acc{b}")
             for t in range(4):
                 nc.tensor.matmul_mx(
                     out=acc[:, P * t : P * (t + 1)],
                     lhsT=w2_codes[:, t].rearrange("p m b -> p (m b)").bitcast(FP4X4),
-                    lhsT_scale=w2_sc[:, t, :],
-                    rhs=z_codes[:].bitcast(FP8X4),
-                    rhs_scale=z_scales[:],
+                    lhsT_scale=w2_sc[:, P * t : P * (t + 1)],
+                    rhs=z_codes[:, cols].bitcast(FP8X4),
+                    rhs_scale=z_scales[:, cols],
                     start=True,
                     stop=True,
                 )
-            y_grouped = ring.tile([P, P, 4], BF16, name="y_grouped", align_bytes=64)
+            round_copy(out=rounded.rearrange("p (n t) -> p n t", t=4), in_=acc[:].rearrange("p (t n) -> p n t", t=4))
             y = ring.tile([P, 4, P], F32, name="y")
             nc.scalar.copy(out=y[:], in_=acc[:].rearrange("p (t n) -> p t n", t=4))
-            nc.sync.dma_start(out=out_rows[:, :, P * b : P * (b + 1)], in_=y[:])
-            if b < 2:
-                nc.scalar.copy(out=y_grouped[:], in_=acc[:].rearrange("p (t n) -> p n t", t=4))
-            else:
-                nc.vector.tensor_copy(
-                    out=y_grouped[:].rearrange("p (c e) t -> p c t e", e=4),
-                    in_=y[:].rearrange("p t (c e) -> p c t e", e=4),
-                )
-            return y_grouped
+            nc.sync.dma_start(out=out_rows[:, :, cols], in_=y[:])
 
-        def planes(b, y_grouped):
-            cols = slice(P * b, P * (b + 1))
-            nc.vector.quantize_mx(
-                out=y_words[:, cols].bitcast(FP8X4),
-                scales=y_scales[:, cols],
-                in_=y_grouped[:].rearrange("p n t -> p (n t)"),
-            )
+        def planes(k, blocks):
+            cols = slice(P * blocks[0], P * (blocks[0] + len(blocks)))
+            nc.vector.quantize_mx(out=y_words[:, cols].bitcast(FP8X4), scales=y_scales[:, cols], in_=y_grouped[k][:])
             nc.sync.dma_start(out=out_words[:, cols], in_=y_words[:, cols].bitcast(I32))
 
-        def finish(b, terms, first):
-            planes(b, second_product(b, group_z(depth_max(b, terms, first))))
+        def halves(room):
+            half = room.shape[1] // 2
+            return [room[:, :half], room[:, half:]]
 
-        wide = [weighted_neighbours(gg_sb[i], 0, 2 * P, rooms[i // 2], S * (i % 2)) for i in range(TILES)]
-        first_max(0)
-        first_max(1)
-        finish(0, wide, 0)
-        finish(1, wide, P)
-        first_max(2)
-        late = [weighted_neighbours(gg_sb[i], 2 * P, 2 * P, gg_sb[last], S + 4 * P * i) for i in range(last)]
-        late.append(weighted_neighbours(gg_sb[last], 2 * P, 2 * P, tail_terms, 0))
-        first_max(3)
-        finish(2, late, 0)
-        finish(3, late, P)
+        free = keep.tile([P, S], F32, name="free_terms")
+        for i in range(TILES):
+            first_max(i)
+        for i in range(TILES):
+            second_round(i, [0, 1], halves(ggT[i][:] if i < 3 else free[:]))
+        second_round(3, [2, 3], halves(ggT[3][:]))
+        depth_max(0)
+        depth_max(1)
+        second_round(0, [2, 3], halves(mT[:, :H]))
+        second_round(1, [2, 3], halves(mT[:, H : 2 * H]))
+        quantise_z(0, [0, 1])
+        for b in range(2):
+            second_product(b, y_grouped[0][:, 512 * b : 512 * (b + 1)], nc.scalar.copy)
+        last_terms = z_grouped[0][:].bitcast(F32)
+        second_round(2, [2], halves(last_terms[:, : 2 * P]))
+        second_round(2, [3], halves(last_terms[:, 2 * P :]))
+        depth_max(2)
+        depth_max(3)
+        planes(0, [0, 1])
+        quantise_z(1, [2])
+        quantise_z(2, [3])
+        second_product(2, y_grouped[1][:], nc.scalar.copy)
+        second_product(3, y_grouped[2][:], nc.vector.tensor_copy)
+        planes(1, [2])
+        planes(2, [3])
 
         for q in range(4):
-            queue = nc.sync if q % 2 == 0 else nc.scalar
-            queue.dma_start(
+            nc.sync.dma_start(
                 out=out_2[0, 4 * q : 4 * q + 4, :].bitcast(I32),
                 in_=y_scales[32 * q : 32 * q + 4, :].bitcast(I32),
             )

@@ -31,7 +31,6 @@ def tile_picked_yjk_none_po_kernel(
     with ExitStack() as ctx:
         keep = ctx.enter_context(tc.tile_pool(name="keep", bufs=1))
         shared = ctx.enter_context(tc.tile_pool(name="shared", bufs=1))
-        ring = ctx.enter_context(tc.tile_pool(name="ring", bufs=2))
         psum = ctx.enter_context(tc.psum_pool(name="psum", bufs=1))
 
         def bank_tile(bank, name):
@@ -118,8 +117,8 @@ def tile_picked_yjk_none_po_kernel(
 
         def group_w1(i, o, copy):
             copy(
-                out=w1_grouped[i, o].rearrange("p (c e j) -> p c j e", e=4, j=4),
-                in_=w1_raw[i][o][:].rearrange("p j (c e) -> p c j e", e=4),
+                out=w1_grouped[i, o].rearrange("p (u c e j) -> p c j u e", u=2, e=2, j=4),
+                in_=w1_raw[i][o][:].rearrange("p j (c u e) -> p c j u e", u=2, e=2),
             )
 
         def quantise_w1(i, first, count, grouped, codes):
@@ -217,21 +216,14 @@ def tile_picked_yjk_none_po_kernel(
             second = place([P, S], F32, f"second_term{i}", None)
             first_round(i, [first[:], second[:]])
 
-        def pairs(ap):
-            return ap.rearrange("n (p u e) -> n u p e", u=2, e=2)
-
-        def sorted_pairs(ap):
-            return ap.rearrange("n (u p e) -> n u p e", u=2, e=2)
-
         def first_max(i):
             bank = bank_tile(5 + i % 2, f"hT{i}")
             for b in range(BLOCKS):
                 nc.tensor.transpose(bank[:, P * b : P * (b + 1)], h_sb[i][:, P * b : P * (b + 1)], ident[:])
-            sorted_out = mT[:].rearrange("n (b u p e) -> n u b p e", b=BLOCKS, u=2, e=2)[:, :, :, 32 * i : 32 * (i + 1), :]
             nc.vector.tensor_tensor(
-                sorted_out,
-                bank[:].rearrange("n (b p u e) -> n u b p e", b=BLOCKS, u=2, e=2),
-                ggT[i][:].rearrange("n (b p u e) -> n u b p e", b=BLOCKS, u=2, e=2),
+                mT[:].rearrange("n (g i c) -> n g i c", i=TILES, c=64)[:, :, i, :],
+                bank[:].rearrange("n (g c) -> n g c", c=64),
+                ggT[i][:].rearrange("n (g c) -> n g c", c=64),
                 MAX,
             )
 
@@ -240,8 +232,10 @@ def tile_picked_yjk_none_po_kernel(
         out_rows = out_0.rearrange("(p t) n -> p t n", t=4)
         out_words = out_1[0].rearrange("p n t -> p (n t)").bitcast(I32)
         zT = [keep.tile([P, H], BF16, name=f"zT{b}") for b in range(BLOCKS)]
-        z_grouped = [keep.tile([P, 4 * c], BF16, name=f"z_grouped{c}_{k}", align_bytes=64) for k, c in enumerate((2 * P, P, P))]
-        y_grouped = [keep.tile([P, 4 * c], BF16, name=f"y_grouped{c}_{k}", align_bytes=64) for k, c in enumerate((2 * P, P, P))]
+        z_room = shared.tile([P, 16 * P], BF16, name="z_room", align_bytes=64, offset=0)
+        z_grouped = [z_room[:, : 8 * P]]
+        z_grouped.extend(keep.tile([P, 4 * P], BF16, name=f"z_grouped{k}", align_bytes=64)[:] for k in range(2))
+        y_grouped = [keep.tile([P, 4 * c], BF16, name=f"y_grouped{k}", align_bytes=64) for k, c in enumerate((2 * P, 2 * P))]
         z_codes = keep.tile([P, S], U32, name="z_codes", align_bytes=64)
         z_scales = keep.tile([P, S], U8, name="z_scales", align_bytes=64)
         summed = {}
@@ -254,7 +248,12 @@ def tile_picked_yjk_none_po_kernel(
                 transposed_sum(summed[b][:, P * i : P * (i + 1)], terms, P * k)
 
         def depth_max(b):
-            nc.vector.tensor_tensor(sorted_pairs(zT[b][:]), pairs(summed[b][:]), sorted_pairs(mT[:, H * b : H * (b + 1)]), MAX)
+            nc.vector.tensor_tensor(
+                zT[b][:].rearrange("n (u i c) -> n u i c", u=2, c=64),
+                summed[b][:].rearrange("n (i u c) -> n u i c", u=2, c=64),
+                mT[:, H * b : H * (b + 1)].rearrange("n (u i c) -> n u i c", u=2, c=64),
+                MAX,
+            )
 
         def quantise_z(k, blocks):
             bank = bank_tile([7, 0, 7][k], f"z_back{k}")
@@ -265,13 +264,13 @@ def tile_picked_yjk_none_po_kernel(
                     at_bank = P * (count * u + j)
                     nc.tensor.transpose(bank[:, at_bank : at_bank + P], words[:, P * u : P * (u + 1)], ident[:])
             nc.scalar.copy(
-                out=z_grouped[k][:].bitcast(F32).rearrange("p (n u) -> p n u", u=2),
+                out=z_grouped[k].bitcast(F32).rearrange("p (n u) -> p n u", u=2),
                 in_=bank[:, : 2 * P * count].rearrange("p (u n) -> p n u", u=2),
             )
             cols = slice(P * blocks[0], P * (blocks[0] + count))
-            nc.vector.quantize_mx(out=z_codes[:, cols].bitcast(FP8X4), scales=z_scales[:, cols], in_=z_grouped[k][:])
+            nc.vector.quantize_mx(out=z_codes[:, cols].bitcast(FP8X4), scales=z_scales[:, cols], in_=z_grouped[k])
 
-        def second_product(b, rounded, round_copy):
+        def second_product(b, rounded, way):
             cols = slice(P * b, P * (b + 1))
             acc = bank_tile([4, 3, 5, 6][b], f"y_acc{b}")
             for t in range(4):
@@ -284,10 +283,13 @@ def tile_picked_yjk_none_po_kernel(
                     start=True,
                     stop=True,
                 )
-            round_copy(out=rounded.rearrange("p (n t) -> p n t", t=4), in_=acc[:].rearrange("p (t n) -> p n t", t=4))
-            y = ring.tile([P, 4, P], F32, name="y")
+            if way != "late":
+                copy = nc.scalar.copy if way == "scalar" else nc.vector.tensor_copy
+                copy(out=rounded.rearrange("p (n t) -> p n t", t=4), in_=acc[:].rearrange("p (t n) -> p n t", t=4))
+            y = keep.tile([P, 4, P], F32, name=f"y{b}")
             nc.scalar.copy(out=y[:], in_=acc[:].rearrange("p (t n) -> p t n", t=4))
             nc.sync.dma_start(out=out_rows[:, :, cols], in_=y[:])
+            return y
 
         def planes(k, blocks):
             cols = slice(P * blocks[0], P * (blocks[0] + len(blocks)))
@@ -307,11 +309,12 @@ def tile_picked_yjk_none_po_kernel(
         depth_max(0)
         depth_max(1)
         second_round(0, [2, 3], halves(mT[:, :H]))
-        second_round(1, [2, 3], halves(mT[:, H : 2 * H]))
         quantise_z(0, [0, 1])
+        late_term = shared.tile([P, 2 * P], F32, name="late_term", align_bytes=64, offset=0)
+        second_round(1, [2, 3], [mT[:, H : H + 2 * P], late_term[:]])
         for b in range(2):
-            second_product(b, y_grouped[0][:, 512 * b : 512 * (b + 1)], nc.scalar.copy)
-        last_terms = z_grouped[0][:].bitcast(F32)
+            second_product(b, y_grouped[0][:, 512 * b : 512 * (b + 1)], "scalar")
+        last_terms = shared.tile([P, S], F32, name="last_terms", align_bytes=64, offset=2048)
         second_round(2, [2], halves(last_terms[:, : 2 * P]))
         second_round(2, [3], halves(last_terms[:, 2 * P :]))
         depth_max(2)
@@ -319,10 +322,13 @@ def tile_picked_yjk_none_po_kernel(
         planes(0, [0, 1])
         quantise_z(1, [2])
         quantise_z(2, [3])
-        second_product(2, y_grouped[1][:], nc.scalar.copy)
-        second_product(3, y_grouped[2][:], nc.vector.tensor_copy)
-        planes(1, [2])
-        planes(2, [3])
+        y_late = second_product(2, y_grouped[1][:, :512], "late")
+        second_product(3, y_grouped[1][:, 512:], "vector")
+        nc.vector.tensor_copy(
+            out=y_grouped[1][:, :512].rearrange("p (c e t) -> p c t e", e=4, t=4),
+            in_=y_late[:].rearrange("p t (c e) -> p c t e", e=4),
+        )
+        planes(1, [2, 3])
 
         for q in range(4):
             nc.sync.dma_start(

@@ -13,6 +13,7 @@ FP8X4 = mybir.dt.float8_e4m3fn_x4
 FP4X4 = mybir.dt.float4_e2m1fn_x4
 MULT = mybir.AluOpType.mult
 MAX = mybir.AluOpType.max
+ADD = mybir.AluOpType.add
 
 P = 128
 K, T, S, H, N = 1024, 2048, 512, 512, 512
@@ -39,8 +40,9 @@ def tile_picked_yjk_none_po_kernel(
         offs_sb = keep.tile([P, S // 16], U16, name="offs_sb")
         pos_sb = [keep.tile([P, S // 16], U16, name=f"pos_sb{d}") for d in range(2)]
         x_table = []
-        xs_table = keep.tile([P, T], U8, name="xs_table")
         raw_at = 8 * T
+        xs_at = raw_at + 8 * 2048
+        xs_table = shared.tile([P, T], U8, name="xs_table", offset=xs_at, align_bytes=64)
         w1_raw = [[None, None] for i in range(TILES)]
         gate_rows = keep.tile([P, P], F32, name="gate_rows")
         gate_sb = [keep.tile([P, S], F32, name=f"gate_sb{d}") for d in range(2)]
@@ -49,45 +51,44 @@ def tile_picked_yjk_none_po_kernel(
         h_sb = [keep.tile([P, S + SPARE], F32, name=f"h_sb{i}", align_bytes=64) for i in range(TILES)]
         gg_sb = [keep.tile([P, S], F32, name=f"gg_sb{i}") for i in range(TILES)]
 
-        def load_w1(i, o):
-            offset = raw_at + 4096 * i + 2048 * o
-            w1_raw[i][o] = shared.tile([P, 4, P], F32, name=f"w1_raw{i}_{o}", offset=offset, align_bytes=64)
-            rows = w1[512 * o : 512 * (o + 1), P * i : P * (i + 1)]
-            nc.sync.dma_start(out=w1_raw[i][o][:], in_=rows.rearrange("(p j) c -> p j c", j=4))
+        def load_w1(first, count, o, offset):
+            raw = shared.tile([P, 4, P * count], F32, name=f"w1_raw{first}_{o}", offset=offset, align_bytes=64)
+            rows = w1[512 * o : 512 * (o + 1), P * first : P * (first + count)]
+            nc.sync.dma_start(out=raw[:], in_=rows.rearrange("(p j) c -> p j c", j=4))
+            for k in range(count):
+                w1_raw[first + k][o] = raw[:, :, P * k : P * (k + 1)]
 
         def load_x(o):
             x_table.append(shared.tile([P, T], I32, name=f"x_table{o}", offset=4 * T * o, align_bytes=64))
             nc.sync.dma_start(out=x_table[o][:], in_=x_words[o].rearrange("p n t -> p (n t)").bitcast(I32))
 
         nc.gpsimd.memset(xs_table[:].bitcast(I32), 0)
+        make_identity(nc, ident[:])
         nc.vector.memset(gate_rows[:], 0.0)
         w2s_raw = keep.tile([P, N], U8, name="w2s_raw")
         nc.vector.memset(w2s_raw[:].bitcast(I32), 0)
-        make_identity(nc, ident[:])
-        nc.gpsimd.memset(w2_sc[:].bitcast(I32), 0)
+        nc.vector.memset(w2_sc[:].bitcast(I32), 0)
         for i in range(TILES):
-            nc.gpsimd.memset(h_sb[i][:, S:], 0.0)
+            nc.vector.memset(h_sb[i][:, S:], 0.0)
 
         nc.sync.dma_start(offs_sb[:], offs)
-        w2_raw = keep.tile([P, 2 * N], U8, name="w2_raw")
-        nc.sync.dma_start(out=w2_raw[:].bitcast(I32), in_=w2_words[0].bitcast(I32))
-        load_w1(0, 0)
-        load_w1(0, 1)
+        for o in range(PASSES):
+            load_w1(0, 1, o, raw_at + 2048 * o)
         load_x(0)
+        nc.sync.dma_start(out=gate_rows[: 2 * BLOCKS, :], in_=gate[:, 0, :].rearrange("d (b c) -> d b c", c=P))
         for q in range(4):
             nc.sync.dma_start(
                 out=xs_table[32 * q : 32 * q + 4 * PASSES, :].bitcast(I32),
                 in_=x_scales[:, 4 * q : 4 * q + 4, :].bitcast(I32),
             )
-        nc.sync.dma_start(out=gate_rows[: 2 * BLOCKS, :], in_=gate[:, 0, :].rearrange("d (b c) -> d b c", c=P))
         load_x(1)
         nc.sync.dma_start(pos_sb[0][:], pos1)
         nc.sync.dma_start(pos_sb[1][:], pos2)
-        for i in range(1, TILES):
-            for o in range(PASSES):
-                load_w1(i, o)
-            if i == 1:
-                nc.sync.dma_start(out=w2s_raw[:16, :].bitcast(I32), in_=w2_scales[0].bitcast(I32))
+        w2_raw = keep.tile([P, 2 * N], U8, name="w2_raw")
+        nc.sync.dma_start(out=w2_raw[:].bitcast(I32), in_=w2_words[0].bitcast(I32))
+        nc.sync.dma_start(out=w2s_raw[:16, :].bitcast(I32), in_=w2_scales[0].bitcast(I32))
+        for o in range(PASSES):
+            load_w1(1, 3, o, raw_at + 4096 + 6144 * o)
 
         gate_cols = keep.tile([P, 2 * BLOCKS], F32, name="gate_cols")
         turned = bank_tile(2, "turned")
@@ -101,10 +102,6 @@ def tile_picked_yjk_none_po_kernel(
             nc.scalar.copy(out=gate_sb[d][:], in_=spread[:])
 
         at = 4 * T
-        codes_at = [None, None, None, None]
-        chain_at = at + 4096
-        grouped_at = [None, chain_at, chain_at, chain_at + 2048]
-        grouped_extent = [2, 4, 2, 2]
 
         def place(pool_tile_shape, dtype, name, offset):
             if offset is None:
@@ -118,7 +115,7 @@ def tile_picked_yjk_none_po_kernel(
         def group_w1(i, o, copy):
             copy(
                 out=w1_grouped[i, o].rearrange("p (u c e j) -> p c j u e", u=2, e=2, j=4),
-                in_=w1_raw[i][o][:].rearrange("p j (c u e) -> p c j u e", u=2, e=2),
+                in_=w1_raw[i][o].rearrange("p j (c u e) -> p c j u e", u=2, e=2),
             )
 
         def quantise_w1(i, first, count, grouped, codes):
@@ -129,21 +126,28 @@ def tile_picked_yjk_none_po_kernel(
                 in_=grouped,
             )
             for o in range(count):
-                w1_codes[i, first + o] = codes[:, P * o : P * (o + 1)]
+                w1_codes[i + (first + o) // PASSES, (first + o) % PASSES] = codes[:, P * o : P * (o + 1)]
 
         xs_picked = keep.tile([P, S], U8, name="xs_picked", align_bytes=64)
-        x_picked = [keep.tile([P, S], U32, name=f"x_picked{o}", align_bytes=64) for o in range(PASSES)]
-        w2_codes = keep.tile([P, 4, P, 2], U8, name="w2_codes", align_bytes=64)
-        nc.vector.tensor_copy(out=w2_codes[:], in_=w2_raw[:].rearrange("p (m t b) -> p t m b", t=4, b=2))
+        x_first = keep.tile([P, S], U32, name="x_first", align_bytes=64)
         early = place([P, PASSES * 512], BF16, "w1_grouped0", None)
         for o in range(PASSES):
             w1_grouped[0, o] = early[:, 512 * o : 512 * (o + 1)]
             group_w1(0, o, nc.vector.tensor_copy)
         quantise_w1(0, 0, PASSES, early[:], place([P, PASSES * P], U32, "w1_codes0", None))
-        nc.vector.tensor_copy(x_picked[0][:], x_table[0][:].bitcast(U32).indirect(offs_sb[:]))
+        nc.vector.tensor_copy(x_first[:], x_table[0][:].bitcast(U32).indirect(offs_sb[:]))
         nc.vector.tensor_copy(xs_picked[:], xs_table[:].indirect(offs_sb[:]))
-        nc.vector.tensor_copy(x_picked[1][:], x_table[1][:].bitcast(U32).indirect(offs_sb[:]))
-        w2s_dealt = shared.tile([P, N], U8, name="w2s_dealt", align_bytes=64, offset=at)
+        x_second = place([P, S], U32, "x_second", xs_at)
+        x_picked = [x_first, x_second]
+        half = S // 2
+        for k in range(2):
+            nc.vector.tensor_copy(
+                x_second[:, half * k : half * (k + 1)],
+                x_table[1][:].bitcast(U32).indirect(offs_sb[:, 16 * k : 16 * (k + 1)]),
+            )
+        w2_codes = place([P, 4, P, 2], U8, "w2_codes", at + 1024)
+        nc.vector.tensor_copy(out=w2_codes[:], in_=w2_raw[:].rearrange("p (m t b) -> p t m b", t=4, b=2))
+        w2s_dealt = place([P, N], U8, "w2s_dealt", at)
         nc.vector.tensor_copy(
             out=w2s_dealt[:].rearrange("p (t m) -> p t m", t=4), in_=w2s_raw[:].rearrange("p (m t) -> p t m", t=4)
         )
@@ -152,29 +156,21 @@ def tile_picked_yjk_none_po_kernel(
                 out=w2_sc[32 * q : 32 * q + 4, :].bitcast(I32), in_=w2s_dealt[4 * q : 4 * q + 4, :].bitcast(I32)
             )
 
-        def first_product(i):
-            acc = bank_tile(i % 2, f"acc{i}")
+        def first_product(i, bank, nodes):
+            acc = bank_tile(bank, f"acc{i}_{nodes.start}")
+            width = nodes.stop - nodes.start
             for o in range(PASSES):
                 cols = slice((i * PASSES + o) * P, (i * PASSES + o + 1) * P)
                 nc.tensor.matmul_mx(
-                    out=acc[:],
+                    out=acc[:, :width],
                     lhsT=w1_codes[i, o].bitcast(FP8X4),
                     lhsT_scale=w1_scales[:, cols],
-                    rhs=x_picked[o][:].bitcast(FP8X4),
-                    rhs_scale=xs_picked[4 * o : P, :],
+                    rhs=x_picked[o][:, nodes].bitcast(FP8X4),
+                    rhs_scale=xs_picked[4 * o : P, nodes],
                     start=(o == 0),
                     stop=(o == PASSES - 1),
                 )
-            nc.scalar.copy(out=h_sb[i][:, :S], in_=acc[:])
-
-        def hidden_tile(i, copy):
-            extent = place([P, grouped_extent[i] * 512], BF16, f"w1_grouped{i}", grouped_at[i])
-            grouped = extent[:, : PASSES * 512]
-            for o in range(PASSES):
-                w1_grouped[i, o] = grouped[:, 512 * o : 512 * (o + 1)]
-                group_w1(i, o, copy)
-            quantise_w1(i, 0, PASSES, grouped, place([P, PASSES * P], U32, f"w1_codes{i}", codes_at[i]))
-            first_product(i)
+            nc.scalar.copy(out=h_sb[i][:, nodes], in_=acc[:, :width])
 
         def weighted_neighbours(window, first, count, rooms):
             for d in range(2):
@@ -192,36 +188,47 @@ def tile_picked_yjk_none_po_kernel(
                 )
 
         mT = keep.tile([P, BLOCKS * H], F32, name="mT")
-        ggT = []
+        ggT = {}
 
         def first_round(i, terms):
             weighted_neighbours(h_sb[i], 0, S, terms)
-            bank = bank_tile([2, 0, 1, 2][i], f"first_sum{i}")
+            bank = bank_tile([None, 0, 1, 2][i], f"first_sum{i}")
             for b in range(BLOCKS):
                 transposed_sum(bank[:, P * b : P * (b + 1)], terms, P * b)
-            ggT.append(shared.tile([P, S], F32, name=f"ggT{i}", align_bytes=64, offset=raw_at + 3 * 4096 + 2048 * i))
+            ggT[i] = place([P, S], F32, f"ggT{i}", None)
             nc.scalar.copy(out=ggT[i][:], in_=bank[:])
             bank = bank_tile(3 + i % 2, f"back{i}")
             for b in range(BLOCKS):
                 nc.tensor.transpose(bank[:, P * b : P * (b + 1)], ggT[i][:, P * b : P * (b + 1)], ident[:])
             nc.scalar.copy(out=gg_sb[i][:], in_=bank[:])
 
-        first_product(0)
-        hidden_tile(1, nc.vector.tensor_copy)
-        hidden_tile(2, nc.scalar.copy)
-        hidden_tile(3, nc.scalar.copy)
-        terms_at = [None, chain_at, chain_at + 2048, None]
-        for i in range(TILES):
-            first = place([P, S], F32, f"first_term{i}", terms_at[i])
-            second = place([P, S], F32, f"second_term{i}", None)
-            first_round(i, [first[:], second[:]])
+        for k in range(2):
+            first_product(0, k, slice(half * k, half * (k + 1)))
+        grouped_at = at + 2048
+        next_grouped = place([P, PASSES * 512], BF16, "w1_grouped1", grouped_at)
+        last_grouped = place([P, 2 * PASSES * 512], BF16, "w1_grouped23", grouped_at + 2048)
+        for i in range(1, TILES):
+            for o in range(PASSES):
+                room = next_grouped if i == 1 else last_grouped
+                at_room = 512 * (PASSES * max(i - 2, 0) + o)
+                w1_grouped[i, o] = room[:, at_room : at_room + 512]
+        for i, o in ((1, 0), (2, 0), (1, 1), (3, 0), (2, 1), (3, 1)):
+            group_w1(i, o, nc.scalar.copy)
+        quantise_w1(1, 0, PASSES, next_grouped[:], place([P, PASSES * P], U32, "w1_codes1", None))
+        first_product(1, 2, slice(0, S))
+        quantise_w1(2, 0, 2 * PASSES, last_grouped[:], place([P, 2 * PASSES * P], U32, "w1_codes23", None))
+        first_product(2, 0, slice(0, S))
+        first_product(3, 1, slice(0, S))
+
+        def mT_part(i):
+            return mT[:].rearrange("n (g i c) -> n g i c", i=TILES, c=64)[:, :, i, :]
 
         def first_max(i):
-            bank = bank_tile(5 + i % 2, f"hT{i}")
+            bank = bank_tile([None, 6, 7, 5][i], f"hT{i}")
             for b in range(BLOCKS):
                 nc.tensor.transpose(bank[:, P * b : P * (b + 1)], h_sb[i][:, P * b : P * (b + 1)], ident[:])
             nc.vector.tensor_tensor(
-                mT[:].rearrange("n (g i c) -> n g i c", i=TILES, c=64)[:, :, i, :],
+                mT_part(i),
                 bank[:].rearrange("n (g c) -> n g c", c=64),
                 ggT[i][:].rearrange("n (g c) -> n g c", c=64),
                 MAX,
@@ -242,6 +249,9 @@ def tile_picked_yjk_none_po_kernel(
 
         def second_round(i, blocks, terms):
             weighted_neighbours(gg_sb[i], P * blocks[0], P * len(blocks), terms)
+            second_sums(i, blocks, terms)
+
+        def second_sums(i, blocks, terms):
             for k, b in enumerate(blocks):
                 if b not in summed:
                     summed[b] = bank_tile([4, 3, 1, 2][b], f"second_sum{b}")
@@ -255,8 +265,8 @@ def tile_picked_yjk_none_po_kernel(
                 MAX,
             )
 
-        def quantise_z(k, blocks):
-            bank = bank_tile([7, 0, 7][k], f"z_back{k}")
+        def turn_z(k, blocks):
+            bank = bank_tile([6, 7, 6][k], f"z_back{k}")
             count = len(blocks)
             for j, b in enumerate(blocks):
                 words = zT[b][:].bitcast(F32)
@@ -267,12 +277,14 @@ def tile_picked_yjk_none_po_kernel(
                 out=z_grouped[k].bitcast(F32).rearrange("p (n u) -> p n u", u=2),
                 in_=bank[:, : 2 * P * count].rearrange("p (u n) -> p n u", u=2),
             )
-            cols = slice(P * blocks[0], P * (blocks[0] + count))
+
+        def quantise_z(k, blocks):
+            cols = slice(P * blocks[0], P * (blocks[0] + len(blocks)))
             nc.vector.quantize_mx(out=z_codes[:, cols].bitcast(FP8X4), scales=z_scales[:, cols], in_=z_grouped[k])
 
         def second_product(b, rounded, way):
             cols = slice(P * b, P * (b + 1))
-            acc = bank_tile([4, 3, 5, 6][b], f"y_acc{b}")
+            acc = bank_tile([4, 3, 5, 0][b], f"y_acc{b}")
             for t in range(4):
                 nc.tensor.matmul_mx(
                     out=acc[:, P * t : P * (t + 1)],
@@ -300,14 +312,30 @@ def tile_picked_yjk_none_po_kernel(
             half = room.shape[1] // 2
             return [room[:, :half], room[:, half:]]
 
+        terms = [place([P, S], F32, "first_term0", None), place([P, S], F32, "second_term0", None)]
+        weighted_neighbours(h_sb[0], 0, S, [terms[0][:], terms[1][:]])
+        nc.vector.tensor_tensor(gg_sb[0][:], terms[0][:], terms[1][:], ADD)
+        larger = place([P, S], F32, "larger", grouped_at)
+        nc.vector.tensor_tensor(larger[:], h_sb[0][:, :S], gg_sb[0][:], MAX)
+        bank = bank_tile(5, "mT0")
+        for b in range(BLOCKS):
+            nc.tensor.transpose(bank[:, P * b : P * (b + 1)], larger[:, P * b : P * (b + 1)], ident[:])
+        nc.scalar.copy(out=mT_part(0), in_=bank[:].rearrange("n (g c) -> n g c", c=64))
+        early_terms = halves(place([P, S], F32, "early_terms", grouped_at + 2048)[:])
+        weighted_neighbours(gg_sb[0], 0, 2 * P, early_terms)
+        for i in range(1, TILES):
+            first = place([P, S], F32, f"first_term{i}", None)
+            second = place([P, S], F32, f"second_term{i}", None)
+            first_round(i, [first[:], second[:]])
+        second_sums(0, [0, 1], early_terms)
         free = keep.tile([P, S], F32, name="free_terms")
-        for i in range(TILES):
+        for i in range(1, TILES):
             first_max(i)
-        for i in range(TILES):
             second_round(i, [0, 1], halves(ggT[i][:] if i < 3 else free[:]))
         second_round(3, [2, 3], halves(ggT[3][:]))
         depth_max(0)
         depth_max(1)
+        turn_z(0, [0, 1])
         second_round(0, [2, 3], halves(mT[:, :H]))
         quantise_z(0, [0, 1])
         late_term = shared.tile([P, 2 * P], F32, name="late_term", align_bytes=64, offset=0)
@@ -318,7 +346,9 @@ def tile_picked_yjk_none_po_kernel(
         second_round(2, [2], halves(last_terms[:, : 2 * P]))
         second_round(2, [3], halves(last_terms[:, 2 * P :]))
         depth_max(2)
+        turn_z(1, [2])
         depth_max(3)
+        turn_z(2, [3])
         planes(0, [0, 1])
         quantise_z(1, [2])
         quantise_z(2, [3])

@@ -46,10 +46,12 @@ def tile_picked_yjk_none_po_kernel(
         w1_raw = [[None, None] for i in range(TILES)]
         gate_rows = keep.tile([P, P], F32, name="gate_rows")
         gate_sb = [keep.tile([P, S], F32, name=f"gate_sb{d}") for d in range(2)]
-        w2_sc = keep.tile([P, N], U8, name="w2_sc", align_bytes=64)
         ident = keep.tile([P, P], F32, name="ident")
-        h_sb = [keep.tile([P, S + SPARE], F32, name=f"h_sb{i}", align_bytes=64) for i in range(TILES)]
-        gg_sb = [keep.tile([P, S], F32, name=f"gg_sb{i}") for i in range(TILES)]
+        h_at = 8 * T + 9 * 2048
+        h_sb = [shared.tile([P, S + SPARE], F32, name="h_sb0", align_bytes=64, offset=h_at)]
+        h_sb.extend(keep.tile([P, S + SPARE], F32, name=f"h_sb{i}", align_bytes=64) for i in range(1, TILES))
+        gg_sb = [None]
+        gg_sb.extend(keep.tile([P, S], F32, name=f"gg_sb{i}") for i in range(1, TILES))
 
         def load_w1(first, count, o, offset):
             raw = shared.tile([P, 4, P * count], F32, name=f"w1_raw{first}_{o}", offset=offset, align_bytes=64)
@@ -64,14 +66,16 @@ def tile_picked_yjk_none_po_kernel(
 
         nc.gpsimd.memset(xs_table[:].bitcast(I32), 0)
         make_identity(nc, ident[:])
-        nc.vector.memset(gate_rows[:], 0.0)
         w2s_raw = keep.tile([P, N], U8, name="w2s_raw")
         nc.vector.memset(w2s_raw[:].bitcast(I32), 0)
-        nc.vector.memset(w2_sc[:].bitcast(I32), 0)
+        nc.vector.memset(gate_rows[:], 0.0)
         for i in range(TILES):
             nc.vector.memset(h_sb[i][:, S:], 0.0)
 
         nc.sync.dma_start(offs_sb[:], offs)
+        w2_raw = keep.tile([P, 2 * N], U8, name="w2_raw")
+        nc.sync.dma_start(out=w2_raw[:].bitcast(I32), in_=w2_words[0].bitcast(I32))
+        nc.sync.dma_start(out=w2s_raw[:16, :].bitcast(I32), in_=w2_scales[0].bitcast(I32))
         for o in range(PASSES):
             load_w1(0, 1, o, raw_at + 2048 * o)
         load_x(0)
@@ -84,11 +88,9 @@ def tile_picked_yjk_none_po_kernel(
         load_x(1)
         nc.sync.dma_start(pos_sb[0][:], pos1)
         nc.sync.dma_start(pos_sb[1][:], pos2)
-        w2_raw = keep.tile([P, 2 * N], U8, name="w2_raw")
-        nc.sync.dma_start(out=w2_raw[:].bitcast(I32), in_=w2_words[0].bitcast(I32))
-        nc.sync.dma_start(out=w2s_raw[:16, :].bitcast(I32), in_=w2_scales[0].bitcast(I32))
-        for o in range(PASSES):
-            load_w1(1, 3, o, raw_at + 4096 + 6144 * o)
+        load_w1(1, 3, 0, raw_at + 4096)
+        load_w1(1, 1, 1, raw_at + 4096 + 6144)
+        load_w1(2, 2, 1, raw_at + 4096 + 8192)
 
         gate_cols = keep.tile([P, 2 * BLOCKS], F32, name="gate_cols")
         turned = bank_tile(2, "turned")
@@ -130,6 +132,12 @@ def tile_picked_yjk_none_po_kernel(
 
         xs_picked = keep.tile([P, S], U8, name="xs_picked", align_bytes=64)
         x_first = keep.tile([P, S], U32, name="x_first", align_bytes=64)
+        w2_codes = place([P, 4, P, 2], U8, "w2_codes", None)
+        nc.vector.tensor_copy(out=w2_codes[:], in_=w2_raw[:].rearrange("p (m t b) -> p t m b", t=4, b=2))
+        w2s_dealt = place([P, N], U8, "w2s_dealt", None)
+        nc.vector.tensor_copy(
+            out=w2s_dealt[:].rearrange("p (t m) -> p t m", t=4), in_=w2s_raw[:].rearrange("p (m t) -> p t m", t=4)
+        )
         early = place([P, PASSES * 512], BF16, "w1_grouped0", None)
         for o in range(PASSES):
             w1_grouped[0, o] = early[:, 512 * o : 512 * (o + 1)]
@@ -145,18 +153,14 @@ def tile_picked_yjk_none_po_kernel(
                 x_second[:, half * k : half * (k + 1)],
                 x_table[1][:].bitcast(U32).indirect(offs_sb[:, 16 * k : 16 * (k + 1)]),
             )
-        w2_codes = place([P, 4, P, 2], U8, "w2_codes", at + 1024)
-        nc.vector.tensor_copy(out=w2_codes[:], in_=w2_raw[:].rearrange("p (m t b) -> p t m b", t=4, b=2))
-        w2s_dealt = place([P, N], U8, "w2s_dealt", at)
-        nc.vector.tensor_copy(
-            out=w2s_dealt[:].rearrange("p (t m) -> p t m", t=4), in_=w2s_raw[:].rearrange("p (m t) -> p t m", t=4)
-        )
+        w2_sc = place([P, N], U8, "w2_sc", at)
+        nc.gpsimd.memset(w2_sc[:].bitcast(I32), 0)
         for q in range(4):
             nc.sync.dma_start(
                 out=w2_sc[32 * q : 32 * q + 4, :].bitcast(I32), in_=w2s_dealt[4 * q : 4 * q + 4, :].bitcast(I32)
             )
 
-        def first_product(i, bank, nodes):
+        def first_product(i, bank, nodes, copy):
             acc = bank_tile(bank, f"acc{i}_{nodes.start}")
             width = nodes.stop - nodes.start
             for o in range(PASSES):
@@ -170,10 +174,10 @@ def tile_picked_yjk_none_po_kernel(
                     start=(o == 0),
                     stop=(o == PASSES - 1),
                 )
-            nc.scalar.copy(out=h_sb[i][:, nodes], in_=acc[:, :width])
+            copy(out=h_sb[i][:, nodes], in_=acc[:, :width])
 
-        def weighted_neighbours(window, first, count, rooms):
-            for d in range(2):
+        def weighted_neighbours(window, first, count, rooms, lists=(0, 1)):
+            for d in lists:
                 nc.vector.tensor_tensor(
                     rooms[d],
                     window[:].indirect(pos_sb[d][:, first // 16 : (first + count) // 16]),
@@ -187,7 +191,7 @@ def tile_picked_yjk_none_po_kernel(
                     out, terms[d][:, first : first + P], ident[:], start=(d == 0), stop=(d == 1), is_transpose=True
                 )
 
-        mT = keep.tile([P, BLOCKS * H], F32, name="mT")
+        mT = keep.tile([P, BLOCKS * H], F32, name="mT", align_bytes=64)
         ggT = {}
 
         def first_round(i, terms):
@@ -203,7 +207,7 @@ def tile_picked_yjk_none_po_kernel(
             nc.scalar.copy(out=gg_sb[i][:], in_=bank[:])
 
         for k in range(2):
-            first_product(0, k, slice(half * k, half * (k + 1)))
+            first_product(0, k, slice(half * k, half * (k + 1)), nc.vector.tensor_copy)
         grouped_at = at + 2048
         next_grouped = place([P, PASSES * 512], BF16, "w1_grouped1", grouped_at)
         last_grouped = place([P, 2 * PASSES * 512], BF16, "w1_grouped23", grouped_at + 2048)
@@ -212,21 +216,20 @@ def tile_picked_yjk_none_po_kernel(
                 room = next_grouped if i == 1 else last_grouped
                 at_room = 512 * (PASSES * max(i - 2, 0) + o)
                 w1_grouped[i, o] = room[:, at_room : at_room + 512]
-        for i, o in ((1, 0), (2, 0), (1, 1), (3, 0), (2, 1), (3, 1)):
+        for i, o in ((1, 0), (1, 1), (2, 0), (3, 0), (2, 1), (3, 1)):
             group_w1(i, o, nc.scalar.copy)
-        quantise_w1(1, 0, PASSES, next_grouped[:], place([P, PASSES * P], U32, "w1_codes1", None))
-        first_product(1, 2, slice(0, S))
-        quantise_w1(2, 0, 2 * PASSES, last_grouped[:], place([P, 2 * PASSES * P], U32, "w1_codes23", None))
-        first_product(2, 0, slice(0, S))
-        first_product(3, 1, slice(0, S))
+        hT = {}
+
+        def turn_h(i):
+            hT[i] = bank_tile(4 + i, f"hT{i}")
+            for b in range(BLOCKS):
+                nc.tensor.transpose(hT[i][:, P * b : P * (b + 1)], h_sb[i][:, P * b : P * (b + 1)], ident[:])
 
         def mT_part(i):
             return mT[:].rearrange("n (g i c) -> n g i c", i=TILES, c=64)[:, :, i, :]
 
         def first_max(i):
-            bank = bank_tile([None, 6, 7, 5][i], f"hT{i}")
-            for b in range(BLOCKS):
-                nc.tensor.transpose(bank[:, P * b : P * (b + 1)], h_sb[i][:, P * b : P * (b + 1)], ident[:])
+            bank = hT[i]
             nc.vector.tensor_tensor(
                 mT_part(i),
                 bank[:].rearrange("n (g c) -> n g c", c=64),
@@ -239,10 +242,10 @@ def tile_picked_yjk_none_po_kernel(
         out_rows = out_0.rearrange("(p t) n -> p t n", t=4)
         out_words = out_1[0].rearrange("p n t -> p (n t)").bitcast(I32)
         zT = [keep.tile([P, H], BF16, name=f"zT{b}") for b in range(BLOCKS)]
-        z_room = shared.tile([P, 16 * P], BF16, name="z_room", align_bytes=64, offset=0)
-        z_grouped = [z_room[:, : 8 * P]]
-        z_grouped.extend(keep.tile([P, 4 * P], BF16, name=f"z_grouped{k}", align_bytes=64)[:] for k in range(2))
-        y_grouped = [keep.tile([P, 4 * c], BF16, name=f"y_grouped{k}", align_bytes=64) for k, c in enumerate((2 * P, 2 * P))]
+        z_rooms = [place([P, 8 * P], BF16, "z_room0", 0), place([P, 8 * P], BF16, "z_room1", 2048)]
+        z_grouped = [room[:, : 4 * P] for room in z_rooms]
+        z_grouped.extend(place([P, 4 * P], BF16, f"z_grouped{b}", None)[:] for b in (2, 3))
+        y_grouped = [mT[:, 2 * H : 3 * H].bitcast(BF16), place([P, 8 * P], BF16, "y_grouped", None)[:]]
         z_codes = keep.tile([P, S], U32, name="z_codes", align_bytes=64)
         z_scales = keep.tile([P, S], U8, name="z_scales", align_bytes=64)
         summed = {}
@@ -265,22 +268,19 @@ def tile_picked_yjk_none_po_kernel(
                 MAX,
             )
 
-        def turn_z(k, blocks):
-            bank = bank_tile([6, 7, 6][k], f"z_back{k}")
-            count = len(blocks)
-            for j, b in enumerate(blocks):
-                words = zT[b][:].bitcast(F32)
-                for u in range(2):
-                    at_bank = P * (count * u + j)
-                    nc.tensor.transpose(bank[:, at_bank : at_bank + P], words[:, P * u : P * (u + 1)], ident[:])
+        def turn_z(b):
+            bank = bank_tile([6, 7, 3, 6][b], f"z_back{b}")
+            words = zT[b][:].bitcast(F32)
+            for u in range(2):
+                nc.tensor.transpose(bank[:, P * u : P * (u + 1)], words[:, P * u : P * (u + 1)], ident[:])
             nc.scalar.copy(
-                out=z_grouped[k].bitcast(F32).rearrange("p (n u) -> p n u", u=2),
-                in_=bank[:, : 2 * P * count].rearrange("p (u n) -> p n u", u=2),
+                out=z_grouped[b].bitcast(F32).rearrange("p (n u) -> p n u", u=2),
+                in_=bank[:, : 2 * P].rearrange("p (u n) -> p n u", u=2),
             )
 
-        def quantise_z(k, blocks):
-            cols = slice(P * blocks[0], P * (blocks[0] + len(blocks)))
-            nc.vector.quantize_mx(out=z_codes[:, cols].bitcast(FP8X4), scales=z_scales[:, cols], in_=z_grouped[k])
+        def quantise_z(b):
+            cols = slice(P * b, P * (b + 1))
+            nc.vector.quantize_mx(out=z_codes[:, cols].bitcast(FP8X4), scales=z_scales[:, cols], in_=z_grouped[b])
 
         def second_product(b, rounded, way):
             cols = slice(P * b, P * (b + 1))
@@ -295,37 +295,57 @@ def tile_picked_yjk_none_po_kernel(
                     start=True,
                     stop=True,
                 )
-            if way != "late":
-                copy = nc.scalar.copy if way == "scalar" else nc.vector.tensor_copy
-                copy(out=rounded.rearrange("p (n t) -> p n t", t=4), in_=acc[:].rearrange("p (t n) -> p n t", t=4))
+            if way == "vector first":
+                nc.vector.tensor_copy(
+                    out=rounded.rearrange("p (n t) -> p n t", t=4), in_=acc[:].rearrange("p (t n) -> p n t", t=4)
+                )
             y = keep.tile([P, 4, P], F32, name=f"y{b}")
             nc.scalar.copy(out=y[:], in_=acc[:].rearrange("p (t n) -> p t n", t=4))
             nc.sync.dma_start(out=out_rows[:, :, cols], in_=y[:])
+            if way == "scalar":
+                nc.scalar.copy(
+                    out=rounded.rearrange("p (n t) -> p n t", t=4), in_=acc[:].rearrange("p (t n) -> p n t", t=4)
+                )
             return y
+
+        def round_y(y, rounded):
+            nc.vector.tensor_copy(
+                out=rounded.rearrange("p (c e t) -> p c t e", e=4, t=4),
+                in_=y[:].rearrange("p t (c e) -> p c t e", e=4),
+            )
 
         def planes(k, blocks):
             cols = slice(P * blocks[0], P * (blocks[0] + len(blocks)))
-            nc.vector.quantize_mx(out=y_words[:, cols].bitcast(FP8X4), scales=y_scales[:, cols], in_=y_grouped[k][:])
+            nc.vector.quantize_mx(out=y_words[:, cols].bitcast(FP8X4), scales=y_scales[:, cols], in_=y_grouped[k])
             nc.sync.dma_start(out=out_words[:, cols], in_=y_words[:, cols].bitcast(I32))
 
         def halves(room):
             half = room.shape[1] // 2
             return [room[:, :half], room[:, half:]]
 
-        terms = [place([P, S], F32, "first_term0", None), place([P, S], F32, "second_term0", None)]
+        terms = [place([P, S], F32, f"term0_{d}", 4096 + 2048 * d) for d in range(2)]
         weighted_neighbours(h_sb[0], 0, S, [terms[0][:], terms[1][:]])
+        quantise_w1(1, 0, PASSES, next_grouped[:], place([P, PASSES * P], U32, "w1_codes1", None))
+        first_product(1, 2, slice(0, S), nc.scalar.copy)
+        gg_sb[0] = place([P, S], F32, "gg_sb0", grouped_at)
         nc.vector.tensor_tensor(gg_sb[0][:], terms[0][:], terms[1][:], ADD)
-        larger = place([P, S], F32, "larger", grouped_at)
+        larger = place([P, S], F32, "larger", None)
         nc.vector.tensor_tensor(larger[:], h_sb[0][:, :S], gg_sb[0][:], MAX)
-        bank = bank_tile(5, "mT0")
+        bank = bank_tile(3, "mT0")
         for b in range(BLOCKS):
             nc.tensor.transpose(bank[:, P * b : P * (b + 1)], larger[:, P * b : P * (b + 1)], ident[:])
         nc.scalar.copy(out=mT_part(0), in_=bank[:].rearrange("n (g c) -> n g c", c=64))
-        early_terms = halves(place([P, S], F32, "early_terms", grouped_at + 2048)[:])
-        weighted_neighbours(gg_sb[0], 0, 2 * P, early_terms)
+        early_terms = halves(place([P, S], F32, "early_terms", None)[:])
+        weighted_neighbours(gg_sb[0], 0, 2 * P, early_terms, (0,))
+        quantise_w1(2, 0, 2 * PASSES, last_grouped[:], place([P, 2 * PASSES * P], U32, "w1_codes23", h_at))
+        weighted_neighbours(gg_sb[0], 0, 2 * P, early_terms, (1,))
+        for i in (2, 3):
+            first_product(i, i % 2, slice(0, S), nc.scalar.copy)
         for i in range(1, TILES):
-            first = place([P, S], F32, f"first_term{i}", None)
-            second = place([P, S], F32, f"second_term{i}", None)
+            turn_h(i)
+        for i in range(1, TILES):
+            first = place([P, S], F32, f"first_term{i}", grouped_at + 2048 if i == 1 else None)
+            second = place([P, S], F32, f"second_term{i}", grouped_at + 4096 if i == 1 else None)
             first_round(i, [first[:], second[:]])
         second_sums(0, [0, 1], early_terms)
         free = keep.tile([P, S], F32, name="free_terms")
@@ -333,35 +353,34 @@ def tile_picked_yjk_none_po_kernel(
             first_max(i)
             second_round(i, [0, 1], halves(ggT[i][:] if i < 3 else free[:]))
         second_round(3, [2, 3], halves(ggT[3][:]))
-        depth_max(0)
-        depth_max(1)
-        turn_z(0, [0, 1])
-        second_round(0, [2, 3], halves(mT[:, :H]))
-        quantise_z(0, [0, 1])
-        late_term = shared.tile([P, 2 * P], F32, name="late_term", align_bytes=64, offset=0)
-        second_round(1, [2, 3], [mT[:, H : H + 2 * P], late_term[:]])
         for b in range(2):
-            second_product(b, y_grouped[0][:, 512 * b : 512 * (b + 1)], "scalar")
-        last_terms = shared.tile([P, S], F32, name="last_terms", align_bytes=64, offset=2048)
+            depth_max(b)
+            turn_z(b)
+        second_round(0, [2, 3], halves(mT[:, :H]))
+        quantise_z(0)
+        y_early = [second_product(0, None, "late")]
+        late_terms = [mT[:, H : H + 2 * P], place([P, 2 * P], F32, "late_term", 0)[:]]
+        quantise_z(1)
+        y_early.append(second_product(1, None, "late"))
+        second_round(1, [2, 3], late_terms)
+        last_terms = place([P, S], F32, "last_terms", 2048)
         second_round(2, [2], halves(last_terms[:, : 2 * P]))
         second_round(2, [3], halves(last_terms[:, 2 * P :]))
-        depth_max(2)
-        turn_z(1, [2])
-        depth_max(3)
-        turn_z(2, [3])
+        for b in (2, 3):
+            depth_max(b)
+            turn_z(b)
+        round_y(y_early[0], y_grouped[0][:, :512])
+        quantise_z(2)
+        second_product(2, y_grouped[1][:, :512], "scalar")
+        round_y(y_early[1], y_grouped[0][:, 512:])
+        quantise_z(3)
         planes(0, [0, 1])
-        quantise_z(1, [2])
-        quantise_z(2, [3])
-        y_late = second_product(2, y_grouped[1][:, :512], "late")
-        second_product(3, y_grouped[1][:, 512:], "vector")
-        nc.vector.tensor_copy(
-            out=y_grouped[1][:, :512].rearrange("p (c e t) -> p c t e", e=4, t=4),
-            in_=y_late[:].rearrange("p t (c e) -> p c t e", e=4),
-        )
+        second_product(3, y_grouped[1][:, 512:], "vector first")
         planes(1, [2, 3])
 
         for q in range(4):
-            nc.sync.dma_start(
+            queue = nc.sync if q % 2 == 0 else nc.scalar
+            queue.dma_start(
                 out=out_2[0, 4 * q : 4 * q + 4, :].bitcast(I32),
                 in_=y_scales[32 * q : 32 * q + 4, :].bitcast(I32),
             )

@@ -348,24 +348,25 @@ def tile_picked_yjk_none_po_kernel(
             second = place([P, S], F32, f"second_term{i}", grouped_at + 4096 if i == 1 else None)
             first_round(i, [first[:], second[:]])
         second_sums(0, [0, 1], early_terms)
+        filler_terms = halves(h_sb[2][:, :S])
+        weighted_neighbours(gg_sb[0], 2 * P, 2 * P, filler_terms)
         free = keep.tile([P, S], F32, name="free_terms")
         for i in range(1, TILES):
             first_max(i)
             second_round(i, [0, 1], halves(ggT[i][:] if i < 3 else free[:]))
         second_round(3, [2, 3], halves(ggT[3][:]))
+        second_sums(0, [2, 3], filler_terms)
         for b in range(2):
             depth_max(b)
             turn_z(b)
-        second_round(0, [2, 3], halves(mT[:, :H]))
+        second_round(1, [2, 3], [mT[:, : 2 * P], mT[:, H : H + 2 * P]])
         quantise_z(0)
         y_early = [second_product(0, None, "late")]
-        late_terms = [mT[:, H : H + 2 * P], place([P, 2 * P], F32, "late_term", 0)[:]]
         quantise_z(1)
         y_early.append(second_product(1, None, "late"))
-        second_round(1, [2, 3], late_terms)
-        last_terms = place([P, S], F32, "last_terms", 2048)
-        second_round(2, [2], halves(last_terms[:, : 2 * P]))
-        second_round(2, [3], halves(last_terms[:, 2 * P :]))
+        last_terms = place([P, 3 * P], F32, "last_terms", 0)
+        second_round(2, [2], [mT[:, H + 2 * P : H + 3 * P], last_terms[:, :P]])
+        second_round(2, [3], halves(last_terms[:, P:]))
         for b in (2, 3):
             depth_max(b)
             turn_z(b)

@@ -191,7 +191,7 @@ def tile_picked_yjk_none_po_kernel(
                     out, terms[d][:, first : first + P], ident[:], start=(d == 0), stop=(d == 1), is_transpose=True
                 )
 
-        mT = keep.tile([P, BLOCKS * H], F32, name="mT", align_bytes=64)
+        mT = keep.tile([P, BLOCKS * H], BF16, name="mT", align_bytes=64)
         ggT = {}
 
         def first_round(i, terms):
@@ -221,19 +221,22 @@ def tile_picked_yjk_none_po_kernel(
         hT = {}
 
         def turn_h(i):
-            hT[i] = bank_tile(4 + i, f"hT{i}")
+            bank = bank_tile(4 + i, f"hT{i}")
             for b in range(BLOCKS):
-                nc.tensor.transpose(hT[i][:, P * b : P * (b + 1)], h_sb[i][:, P * b : P * (b + 1)], ident[:])
+                nc.tensor.transpose(bank[:, P * b : P * (b + 1)], h_sb[i][:, P * b : P * (b + 1)], ident[:])
+            hT[i] = place([P, S], BF16, f"hT_rounded{i}", None)
+            nc.scalar.copy(out=hT[i][:], in_=bank[:])
 
         def mT_part(i):
             return mT[:].rearrange("n (g i c) -> n g i c", i=TILES, c=64)[:, :, i, :]
 
         def first_max(i):
-            bank = hT[i]
+            rounded = place([P, S], BF16, f"ggT_rounded{i}", None)
+            nc.scalar.copy(out=rounded[:], in_=ggT[i][:])
             nc.vector.tensor_tensor(
                 mT_part(i),
-                bank[:].rearrange("n (g c) -> n g c", c=64),
-                ggT[i][:].rearrange("n (g c) -> n g c", c=64),
+                hT[i][:].rearrange("n (g c) -> n g c", c=64),
+                rounded[:].rearrange("n (g c) -> n g c", c=64),
                 MAX,
             )
 
@@ -245,7 +248,7 @@ def tile_picked_yjk_none_po_kernel(
         z_rooms = [place([P, 8 * P], BF16, "z_room0", 0), place([P, 8 * P], BF16, "z_room1", 2048)]
         z_grouped = [room[:, : 4 * P] for room in z_rooms]
         z_grouped.extend(place([P, 4 * P], BF16, f"z_grouped{b}", None)[:] for b in (2, 3))
-        y_grouped = [mT[:, 2 * H : 3 * H].bitcast(BF16), place([P, 8 * P], BF16, "y_grouped", None)[:]]
+        y_grouped = [mT[:, 2 * H :], place([P, 8 * P], BF16, "y_grouped", None)[:]]
         z_codes = keep.tile([P, S], U32, name="z_codes", align_bytes=64)
         z_scales = keep.tile([P, S], U8, name="z_scales", align_bytes=64)
         summed = {}
@@ -350,22 +353,22 @@ def tile_picked_yjk_none_po_kernel(
         second_sums(0, [0, 1], early_terms)
         filler_terms = halves(h_sb[2][:, :S])
         weighted_neighbours(gg_sb[0], 2 * P, 2 * P, filler_terms)
-        free = keep.tile([P, S], F32, name="free_terms")
+        for i in range(1, TILES):
+            second_round(i, [0, 1], halves(place([P, S], F32, f"second_terms{i}", None)[:]))
+        second_round(3, [2, 3], halves(place([P, S], F32, "third_terms", None)[:]))
+        second_sums(0, [2, 3], filler_terms)
         for i in range(1, TILES):
             first_max(i)
-            second_round(i, [0, 1], halves(ggT[i][:] if i < 3 else free[:]))
-        second_round(3, [2, 3], halves(ggT[3][:]))
-        second_sums(0, [2, 3], filler_terms)
         for b in range(2):
             depth_max(b)
             turn_z(b)
-        second_round(1, [2, 3], [mT[:, : 2 * P], mT[:, H : H + 2 * P]])
+        second_round(1, [2, 3], [mT[:, :H].bitcast(F32), mT[:, H : 2 * H].bitcast(F32)])
         quantise_z(0)
         y_early = [second_product(0, None, "late")]
         quantise_z(1)
         y_early.append(second_product(1, None, "late"))
         last_terms = place([P, 3 * P], F32, "last_terms", 0)
-        second_round(2, [2], [mT[:, H + 2 * P : H + 3 * P], last_terms[:, :P]])
+        second_round(2, [2], [zT[0][:].bitcast(F32)[:, :P], last_terms[:, :P]])
         second_round(2, [3], halves(last_terms[:, P:]))
         for b in (2, 3):
             depth_max(b)

@@ -154,7 +154,7 @@ def tile_picked_yjk_none_po_kernel(
                 x_table[1][:].bitcast(U32).indirect(offs_sb[:, 16 * k : 16 * (k + 1)]),
             )
         w2_sc = place([P, N], U8, "w2_sc", at)
-        nc.gpsimd.memset(w2_sc[:].bitcast(I32), 0)
+        nc.vector.memset(w2_sc[:].bitcast(I32), 0)
         for q in range(4):
             nc.sync.dma_start(
                 out=w2_sc[32 * q : 32 * q + 4, :].bitcast(I32), in_=w2s_dealt[4 * q : 4 * q + 4, :].bitcast(I32)

@@ -53,10 +53,10 @@ def tile_picked_yjk_none_po_kernel(
         gg_sb = [None]
         gg_sb.extend(keep.tile([P, S], F32, name=f"gg_sb{i}") for i in range(1, TILES))
 
-        def load_w1(first, count, o, offset):
+        def load_w1(first, count, o, offset, queue):
             raw = shared.tile([P, 4, P * count], F32, name=f"w1_raw{first}_{o}", offset=offset, align_bytes=64)
             rows = w1[512 * o : 512 * (o + 1), P * first : P * (first + count)]
-            nc.sync.dma_start(out=raw[:], in_=rows.rearrange("(p j) c -> p j c", j=4))
+            queue.dma_start(out=raw[:], in_=rows.rearrange("(p j) c -> p j c", j=4))
             for k in range(count):
                 w1_raw[first + k][o] = raw[:, :, P * k : P * (k + 1)]
 
@@ -77,7 +77,7 @@ def tile_picked_yjk_none_po_kernel(
         nc.sync.dma_start(out=w2_raw[:].bitcast(I32), in_=w2_words[0].bitcast(I32))
         nc.sync.dma_start(out=w2s_raw[:16, :].bitcast(I32), in_=w2_scales[0].bitcast(I32))
         for o in range(PASSES):
-            load_w1(0, 1, o, raw_at + 2048 * o)
+            load_w1(0, 1, o, raw_at + 2048 * o, nc.scalar)
         load_x(0)
         nc.sync.dma_start(out=gate_rows[: 2 * BLOCKS, :], in_=gate[:, 0, :].rearrange("d (b c) -> d b c", c=P))
         for q in range(4):
@@ -88,9 +88,9 @@ def tile_picked_yjk_none_po_kernel(
         load_x(1)
         nc.sync.dma_start(pos_sb[0][:], pos1)
         nc.sync.dma_start(pos_sb[1][:], pos2)
-        load_w1(1, 3, 0, raw_at + 4096)
-        load_w1(1, 1, 1, raw_at + 4096 + 6144)
-        load_w1(2, 2, 1, raw_at + 4096 + 8192)
+        load_w1(1, 3, 0, raw_at + 4096, nc.sync)
+        load_w1(1, 1, 1, raw_at + 4096 + 6144, nc.sync)
+        load_w1(2, 2, 1, raw_at + 4096 + 8192, nc.sync)
 
         gate_cols = keep.tile([P, 2 * BLOCKS], F32, name="gate_cols")
         turned = bank_tile(2, "turned")

@@ -11,6 +11,7 @@ U16 = mybir.dt.uint16
 U8 = mybir.dt.uint8
 FP8X4 = mybir.dt.float8_e4m3fn_x4
 FP4X4 = mybir.dt.float4_e2m1fn_x4
+COPY = mybir.ActivationFunctionType.Copy
 MULT = mybir.AluOpType.mult
 MAX = mybir.AluOpType.max
 ADD = mybir.AluOpType.add
@@ -47,11 +48,9 @@ def tile_picked_yjk_none_po_kernel(
         gate_rows = keep.tile([P, P], F32, name="gate_rows")
         gate_sb = [keep.tile([P, S], F32, name=f"gate_sb{d}") for d in range(2)]
         ident = keep.tile([P, P], F32, name="ident")
-        h_at = 8 * T + 9 * 2048
-        h_sb = [shared.tile([P, S + SPARE], F32, name="h_sb0", align_bytes=64, offset=h_at)]
-        h_sb.extend(keep.tile([P, S + SPARE], F32, name=f"h_sb{i}", align_bytes=64) for i in range(1, TILES))
-        gg_sb = [None]
-        gg_sb.extend(keep.tile([P, S], F32, name=f"gg_sb{i}") for i in range(1, TILES))
+        ident_bf = keep.tile([P, P], BF16, name="ident_bf")
+        h_sb = [keep.tile([P, S + SPARE], F32, name=f"h_sb{i}", align_bytes=64) for i in range(TILES)]
+        gg_sb = [keep.tile([P, S + SPARE], F32, name=f"gg_sb{i}", align_bytes=64) for i in range(TILES)]
 
         def load_w1(first, count, o, offset, queue):
             raw = shared.tile([P, 4, P * count], F32, name=f"w1_raw{first}_{o}", offset=offset, align_bytes=64)
@@ -71,6 +70,8 @@ def tile_picked_yjk_none_po_kernel(
         nc.vector.memset(gate_rows[:], 0.0)
         for i in range(TILES):
             nc.vector.memset(h_sb[i][:, S:], 0.0)
+            nc.vector.memset(gg_sb[i][:, S:], 0.0)
+        nc.vector.tensor_copy(out=ident_bf[:], in_=ident[:])
 
         nc.sync.dma_start(offs_sb[:], offs)
         w2_raw = keep.tile([P, 2 * N], U8, name="w2_raw")
@@ -88,14 +89,15 @@ def tile_picked_yjk_none_po_kernel(
         load_x(1)
         nc.sync.dma_start(pos_sb[0][:], pos1)
         nc.sync.dma_start(pos_sb[1][:], pos2)
-        load_w1(1, 3, 0, raw_at + 4096, nc.sync)
-        load_w1(1, 1, 1, raw_at + 4096 + 6144, nc.sync)
-        load_w1(2, 2, 1, raw_at + 4096 + 8192, nc.sync)
+        for o in range(PASSES):
+            load_w1(1, 1, o, raw_at + 4096 + 6144 * o, nc.sync)
+        for o in range(PASSES):
+            load_w1(2, 2, o, raw_at + 6144 + 6144 * o, nc.sync)
 
         gate_cols = keep.tile([P, 2 * BLOCKS], F32, name="gate_cols")
         turned = bank_tile(2, "turned")
         nc.tensor.transpose(turned[:, :P], gate_rows[:], ident[:])
-        nc.scalar.copy(out=gate_cols[:], in_=turned[:, : 2 * BLOCKS])
+        nc.scalar.activation(gate_cols[:], turned[:, : 2 * BLOCKS], COPY)
         for d in range(2):
             spread = bank_tile(d, f"spread{d}")
             for b in range(BLOCKS):
@@ -105,7 +107,23 @@ def tile_picked_yjk_none_po_kernel(
 
         at = 4 * T
 
+        rooms = {
+            "w1_codes1": 27,
+            "plain0_0_0": 27,
+            "first0_1": 10,
+            "larger0_0": 14.5,
+            "first1_1": 12.5,
+            "first1_0": 15.5,
+            "first3_1": 36,
+            "ee0_0": 36,
+            "ee0_1": 36.5,
+            "ee1_0": 37,
+            "ee1_1": 37.5,
+        }
+
         def place(pool_tile_shape, dtype, name, offset):
+            if name in rooms:
+                offset = int(1024 * rooms[name])
             if offset is None:
                 return keep.tile(pool_tile_shape, dtype, name=name, align_bytes=64)
             return shared.tile(pool_tile_shape, dtype, name=name, align_bytes=64, offset=offset)
@@ -176,67 +194,113 @@ def tile_picked_yjk_none_po_kernel(
                 )
             copy(out=h_sb[i][:, nodes], in_=acc[:, :width])
 
-        def weighted_neighbours(window, first, count, rooms, lists=(0, 1)):
-            for d in lists:
-                nc.vector.tensor_tensor(
-                    rooms[d],
-                    window[:].indirect(pos_sb[d][:, first // 16 : (first + count) // 16]),
-                    gate_sb[d][:, first : first + count],
-                    MULT,
-                )
-
-        def transposed_sum(out, terms, first):
-            for d in range(2):
-                nc.tensor.matmul(
-                    out, terms[d][:, first : first + P], ident[:], start=(d == 0), stop=(d == 1), is_transpose=True
-                )
-
-        mT = keep.tile([P, BLOCKS * H], BF16, name="mT", align_bytes=64)
-        ggT = {}
-
-        def first_round(i, terms):
-            weighted_neighbours(h_sb[i], 0, S, terms)
-            bank = bank_tile([None, 0, 1, 2][i], f"first_sum{i}")
-            for b in range(BLOCKS):
-                transposed_sum(bank[:, P * b : P * (b + 1)], terms, P * b)
-            ggT[i] = place([P, S], F32, f"ggT{i}", None)
-            nc.scalar.copy(out=ggT[i][:], in_=bank[:])
-            bank = bank_tile(3 + i % 2, f"back{i}")
-            for b in range(BLOCKS):
-                nc.tensor.transpose(bank[:, P * b : P * (b + 1)], ggT[i][:, P * b : P * (b + 1)], ident[:])
-            nc.scalar.copy(out=gg_sb[i][:], in_=bank[:])
-
         for k in range(2):
-            first_product(0, k, slice(half * k, half * (k + 1)), nc.vector.tensor_copy)
+            first_product(0, k, slice(half * k, half * (k + 1)), [nc.scalar.copy, nc.vector.tensor_copy][k])
         grouped_at = at + 2048
-        next_grouped = place([P, PASSES * 512], BF16, "w1_grouped1", grouped_at)
-        last_grouped = place([P, 2 * PASSES * 512], BF16, "w1_grouped23", grouped_at + 2048)
+        grouped = {}
         for i in range(1, TILES):
+            grouped[i] = place([P, PASSES * 512], BF16, f"w1_grouped{i}", grouped_at + 2048 * (i - 1))
             for o in range(PASSES):
-                room = next_grouped if i == 1 else last_grouped
-                at_room = 512 * (PASSES * max(i - 2, 0) + o)
-                w1_grouped[i, o] = room[:, at_room : at_room + 512]
-        for i, o in ((1, 0), (1, 1), (2, 0), (3, 0), (2, 1), (3, 1)):
-            group_w1(i, o, nc.scalar.copy)
-        hT = {}
+                w1_grouped[i, o] = grouped[i][:, 512 * o : 512 * (o + 1)]
+                group_w1(i, o, nc.scalar.copy)
 
-        def turn_h(i):
-            bank = bank_tile(4 + i, f"hT{i}")
-            for b in range(BLOCKS):
-                nc.tensor.transpose(bank[:, P * b : P * (b + 1)], h_sb[i][:, P * b : P * (b + 1)], ident[:])
-            hT[i] = place([P, S], BF16, f"hT_rounded{i}", None)
-            nc.scalar.copy(out=hT[i][:], in_=bank[:])
+        def next_tile(i, bank):
+            quantise_w1(i, 0, PASSES, grouped[i][:], place([P, PASSES * P], U32, f"w1_codes{i}", None))
+            first_product(i, bank, slice(0, S), nc.scalar.copy)
 
-        def mT_part(i):
-            return mT[:].rearrange("n (g i c) -> n g i c", i=TILES, c=64)[:, :, i, :]
+        def offsets(d, blocks):
+            return pos_sb[d][:, 8 * blocks[0] : 8 * (blocks[0] + len(blocks))]
 
-        def first_max(i):
-            rounded = place([P, S], BF16, f"ggT_rounded{i}", None)
-            nc.scalar.copy(out=rounded[:], in_=ggT[i][:])
+        def nodes_of(blocks):
+            return slice(P * blocks[0], P * (blocks[0] + len(blocks)))
+
+        def weighted(window, d, blocks, name):
+            term = place([P, P * len(blocks)], F32, name, None)
+            nc.vector.tensor_tensor(term[:], window[:].indirect(offsets(d, blocks)), gate_sb[d][:, nodes_of(blocks)], MULT)
+            return term
+
+        def turned_blocks(bank, source, count, identity):
+            for k in range(count):
+                nc.tensor.transpose(bank[:, P * k : P * (k + 1)], source[:, P * k : P * (k + 1)], identity[:])
+
+        ALL = [0, 1, 2, 3]
+        HALVES = [[0, 1], [2, 3]]
+        zT = [keep.tile([P, 2 * H], BF16, name=f"zT{k}") for k in range(2)]
+        mT = {}
+        scaled = {}
+        ee = {}
+
+        def z_part(i, k):
+            return zT[k][:].rearrange("n (g i c) -> n g i c", i=TILES, c=64)[:, :, i, :]
+
+        def first_max(i, blocks, bank):
+            larger = place([P, P * len(blocks)], BF16, f"larger{i}_{blocks[0]}", None)
+            nc.vector.tensor_tensor(larger[:], h_sb[i][:, nodes_of(blocks)], gg_sb[i][:, nodes_of(blocks)], MAX)
+            turned_m = psum.tile([P, 512], BF16, name=f"mT{i}_{blocks[0]}", offset=2048 * bank)
+            turned_blocks(turned_m, larger, len(blocks), ident_bf)
+            for j, b in enumerate(blocks):
+                mT[i, b] = (turned_m, P * j)
+
+        turned_terms = {}
+
+        def plain_gather(key, window, d, blocks, bank, term=None):
+            if term is None:
+                term = place([P, P * len(blocks)], F32, f"plain{key}_{blocks[0]}_{d}", None)[:]
+            nc.scalar.activation(term, window[:].indirect(offsets(d, blocks)), COPY)
+            turned_term = bank_tile(bank, f"plainT{key}_{blocks[0]}_{d}")
+            turned_blocks(turned_term, term, len(blocks), ident)
+            for j, b in enumerate(blocks):
+                turned_terms[key, d, b] = turned_term[:, P * j : P * (j + 1)]
+
+        def scale_first(key, blocks):
+            room = place([P, P * len(blocks)], F32, f"scaled{key}_{blocks[0]}", None)
+            for j, b in enumerate(blocks):
+                scaled[key, b] = room[:, P * j : P * (j + 1)]
+                nc.scalar.activation(scaled[key, b], turned_terms[key, 0, b], COPY, scale=gate_cols[:, b : b + 1])
+
+        def scale_and_add(key, blocks, out):
+            for j, b in enumerate(blocks):
+                nc.vector.scalar_tensor_tensor(
+                    out[:, P * j : P * (j + 1)],
+                    turned_terms[key, 1, b],
+                    gate_cols[:, BLOCKS + b : BLOCKS + b + 1],
+                    scaled[key, b],
+                    MULT,
+                    ADD,
+                )
+
+        def second_sum(i, k):
+            ee[i, k] = place([P, 2 * P], BF16, f"ee{i}_{k}", None)
+            scale_and_add(i, HALVES[k], ee[i, k])
+
+        def fused_sum(terms, count, bank, name):
+            summed = bank_tile(bank, name)
+            for j in range(count):
+                for d in range(2):
+                    nc.tensor.matmul(
+                        summed[:, P * j : P * (j + 1)],
+                        terms[d][:, P * j : P * (j + 1)],
+                        ident[:],
+                        start=(d == 0),
+                        stop=(d == 1),
+                        is_transpose=True,
+                    )
+            return summed
+
+        def fused_max(i, k, summed, larger):
             nc.vector.tensor_tensor(
-                mT_part(i),
-                hT[i][:].rearrange("n (g c) -> n g c", c=64),
-                rounded[:].rearrange("n (g c) -> n g c", c=64),
+                z_part(i, k),
+                summed.rearrange("n (g c) -> n g c", c=64),
+                larger.rearrange("n (g c) -> n g c", c=64),
+                MAX,
+            )
+
+        def depth_max(i, k):
+            bank, start = mT[i, HALVES[k][0]]
+            nc.vector.tensor_tensor(
+                z_part(i, k),
+                bank[:, start : start + 2 * P].rearrange("n (g c) -> n g c", c=64),
+                ee[i, k][:].rearrange("n (g c) -> n g c", c=64),
                 MAX,
             )
 
@@ -244,38 +308,17 @@ def tile_picked_yjk_none_po_kernel(
         y_scales = keep.tile([P, S], U8, name="y_scales", align_bytes=64)
         out_rows = out_0.rearrange("(p t) n -> p t n", t=4)
         out_words = out_1[0].rearrange("p n t -> p (n t)").bitcast(I32)
-        zT = [keep.tile([P, H], BF16, name=f"zT{b}") for b in range(BLOCKS)]
-        z_rooms = [place([P, 8 * P], BF16, "z_room0", 0), place([P, 8 * P], BF16, "z_room1", 2048)]
-        z_grouped = [room[:, : 4 * P] for room in z_rooms]
-        z_grouped.extend(place([P, 4 * P], BF16, f"z_grouped{b}", None)[:] for b in (2, 3))
-        y_grouped = [mT[:, 2 * H :], place([P, 8 * P], BF16, "y_grouped", None)[:]]
+        z_grouped = [place([P, 4 * P], BF16, f"z_grouped{b}", None)[:] for b in ALL]
+        y_grouped = [place([P, 8 * P], BF16, f"y_grouped{k}", None)[:] for k in range(2)]
         z_codes = keep.tile([P, S], U32, name="z_codes", align_bytes=64)
         z_scales = keep.tile([P, S], U8, name="z_scales", align_bytes=64)
-        summed = {}
 
-        def second_round(i, blocks, terms):
-            weighted_neighbours(gg_sb[i], P * blocks[0], P * len(blocks), terms)
-            second_sums(i, blocks, terms)
-
-        def second_sums(i, blocks, terms):
-            for k, b in enumerate(blocks):
-                if b not in summed:
-                    summed[b] = bank_tile([4, 3, 1, 2][b], f"second_sum{b}")
-                transposed_sum(summed[b][:, P * i : P * (i + 1)], terms, P * k)
-
-        def depth_max(b):
-            nc.vector.tensor_tensor(
-                zT[b][:].rearrange("n (u i c) -> n u i c", u=2, c=64),
-                summed[b][:].rearrange("n (i u c) -> n u i c", u=2, c=64),
-                mT[:, H * b : H * (b + 1)].rearrange("n (u i c) -> n u i c", u=2, c=64),
-                MAX,
-            )
-
-        def turn_z(b):
-            bank = bank_tile([6, 7, 3, 6][b], f"z_back{b}")
-            words = zT[b][:].bitcast(F32)
+        def turn_z(b, bank):
+            bank = bank_tile(bank, f"z_back{b}")
+            words = zT[b // 2][:].bitcast(F32)
             for u in range(2):
-                nc.tensor.transpose(bank[:, P * u : P * (u + 1)], words[:, P * u : P * (u + 1)], ident[:])
+                at_word = P * (2 * (b % 2) + u)
+                nc.tensor.transpose(bank[:, P * u : P * (u + 1)], words[:, at_word : at_word + P], ident[:])
             nc.scalar.copy(
                 out=z_grouped[b].bitcast(F32).rearrange("p (n u) -> p n u", u=2),
                 in_=bank[:, : 2 * P].rearrange("p (u n) -> p n u", u=2),
@@ -285,9 +328,10 @@ def tile_picked_yjk_none_po_kernel(
             cols = slice(P * b, P * (b + 1))
             nc.vector.quantize_mx(out=z_codes[:, cols].bitcast(FP8X4), scales=z_scales[:, cols], in_=z_grouped[b])
 
-        def second_product(b, rounded, way):
+        def second_product(b, bank, way):
             cols = slice(P * b, P * (b + 1))
-            acc = bank_tile([4, 3, 5, 0][b], f"y_acc{b}")
+            rounded = y_grouped[b // 2][:, 512 * (b % 2) : 512 * (b % 2 + 1)]
+            acc = bank_tile(bank, f"y_acc{b}")
             for t in range(4):
                 nc.tensor.matmul_mx(
                     out=acc[:, P * t : P * (t + 1)],
@@ -311,76 +355,82 @@ def tile_picked_yjk_none_po_kernel(
                 )
             return y
 
-        def round_y(y, rounded):
+        def round_y(b, y):
             nc.vector.tensor_copy(
-                out=rounded.rearrange("p (c e t) -> p c t e", e=4, t=4),
+                out=y_grouped[b // 2][:, 512 * (b % 2) : 512 * (b % 2 + 1)].rearrange("p (c e t) -> p c t e", e=4, t=4),
                 in_=y[:].rearrange("p t (c e) -> p c t e", e=4),
             )
 
-        def planes(k, blocks):
-            cols = slice(P * blocks[0], P * (blocks[0] + len(blocks)))
+        def planes(k):
+            cols = nodes_of(HALVES[k])
             nc.vector.quantize_mx(out=y_words[:, cols].bitcast(FP8X4), scales=y_scales[:, cols], in_=y_grouped[k])
             nc.sync.dma_start(out=out_words[:, cols], in_=y_words[:, cols].bitcast(I32))
 
-        def halves(room):
-            half = room.shape[1] // 2
-            return [room[:, :half], room[:, half:]]
+        def first_sum(i, terms):
+            nc.vector.tensor_tensor(gg_sb[i][:, :S], terms[0][:], terms[1][:], ADD)
 
-        terms = [place([P, S], F32, f"term0_{d}", 4096 + 2048 * d) for d in range(2)]
-        weighted_neighbours(h_sb[0], 0, S, [terms[0][:], terms[1][:]])
-        quantise_w1(1, 0, PASSES, next_grouped[:], place([P, PASSES * P], U32, "w1_codes1", None))
-        first_product(1, 2, slice(0, S), nc.scalar.copy)
-        gg_sb[0] = place([P, S], F32, "gg_sb0", grouped_at)
-        nc.vector.tensor_tensor(gg_sb[0][:], terms[0][:], terms[1][:], ADD)
-        larger = place([P, S], F32, "larger", None)
-        nc.vector.tensor_tensor(larger[:], h_sb[0][:, :S], gg_sb[0][:], MAX)
-        bank = bank_tile(3, "mT0")
-        for b in range(BLOCKS):
-            nc.tensor.transpose(bank[:, P * b : P * (b + 1)], larger[:, P * b : P * (b + 1)], ident[:])
-        nc.scalar.copy(out=mT_part(0), in_=bank[:].rearrange("n (g c) -> n g c", c=64))
-        early_terms = halves(place([P, S], F32, "early_terms", None)[:])
-        weighted_neighbours(gg_sb[0], 0, 2 * P, early_terms, (0,))
-        quantise_w1(2, 0, 2 * PASSES, last_grouped[:], place([P, 2 * PASSES * P], U32, "w1_codes23", h_at))
-        weighted_neighbours(gg_sb[0], 0, 2 * P, early_terms, (1,))
-        for i in (2, 3):
-            first_product(i, i % 2, slice(0, S), nc.scalar.copy)
-        for i in range(1, TILES):
-            turn_h(i)
-        for i in range(1, TILES):
-            first = place([P, S], F32, f"first_term{i}", grouped_at + 2048 if i == 1 else None)
-            second = place([P, S], F32, f"second_term{i}", grouped_at + 4096 if i == 1 else None)
-            first_round(i, [first[:], second[:]])
-        second_sums(0, [0, 1], early_terms)
-        filler_terms = halves(h_sb[2][:, :S])
-        weighted_neighbours(gg_sb[0], 2 * P, 2 * P, filler_terms)
-        for i in range(1, TILES):
-            second_round(i, [0, 1], halves(place([P, S], F32, f"second_terms{i}", None)[:]))
-        second_round(3, [2, 3], halves(place([P, S], F32, "third_terms", None)[:]))
-        second_sums(0, [2, 3], filler_terms)
-        for i in range(1, TILES):
-            first_max(i)
-        for b in range(2):
-            depth_max(b)
-            turn_z(b)
-        second_round(1, [2, 3], [mT[:, :H].bitcast(F32), mT[:, H : 2 * H].bitcast(F32)])
+        terms = [weighted(h_sb[0], 0, ALL, "first0_0")]
+        next_tile(1, 2)
+        terms.append(weighted(h_sb[0], 1, ALL, "first0_1"))
+        first_sum(0, terms)
+        next_tile(2, 0)
+        next_tile(3, 1)
+        plain_gather(0, gg_sb[0], 0, ALL, 3)
+        plain_gather(0, gg_sb[0], 1, ALL, 4)
+        scale_first(0, ALL)
+        terms = [weighted(h_sb[1], d, ALL, f"first1_{d}") for d in range(2)]
+        first_max(0, ALL, 6)
+        first_sum(1, terms)
+        plain_gather(1, gg_sb[1], 0, ALL, 3)
+        plain_gather(1, gg_sb[1], 1, ALL, 5)
+        scale_first(1, ALL)
+        terms = [weighted(h_sb[2], d, ALL, f"first2_{d}") for d in range(2)]
+        first_max(1, ALL, 7)
+        first_sum(2, terms)
+        plain_gather(2, gg_sb[2], 0, ALL, 3)
+        plain_gather(2, gg_sb[2], 1, ALL, 2)
+        scale_first(2, ALL)
+        terms = [weighted(h_sb[3], d, ALL, f"first3_{d}") for d in range(2)]
+        first_max(2, ALL, 0)
+        first_sum(3, terms)
+        for k in range(2):
+            second_sum(0, k)
+        for k in range(2):
+            depth_max(0, k)
+        for k in range(2):
+            plain_gather(3, gg_sb[3], 0, HALVES[k], [3, 1][k])
+            plain_gather(3, gg_sb[3], 1, HALVES[k], [4, 6][k])
+            scale_first(3, HALVES[k])
+        second_sum(1, 0)
+        second_sum(2, 0)
+        second_sum(1, 1)
+        first_max(3, ALL, 5)
+        depth_max(1, 0)
+        depth_max(2, 0)
+        second_sum(3, 0)
+        second_sum(2, 1)
+        depth_max(3, 0)
+        turn_z(0, 3)
+        turn_z(1, 4)
+        depth_max(1, 1)
+        depth_max(2, 1)
+        second_sum(3, 1)
         quantise_z(0)
-        y_early = [second_product(0, None, "late")]
+        y_done = [second_product(0, 3, "late")]
+        depth_max(3, 1)
+        turn_z(2, 0)
+        turn_z(3, 2)
         quantise_z(1)
-        y_early.append(second_product(1, None, "late"))
-        last_terms = place([P, 3 * P], F32, "last_terms", 0)
-        second_round(2, [2], [zT[0][:].bitcast(F32)[:, :P], last_terms[:, :P]])
-        second_round(2, [3], halves(last_terms[:, P:]))
-        for b in (2, 3):
-            depth_max(b)
-            turn_z(b)
-        round_y(y_early[0], y_grouped[0][:, :512])
+        y_done.append(second_product(1, 4, "late"))
         quantise_z(2)
-        second_product(2, y_grouped[1][:, :512], "scalar")
-        round_y(y_early[1], y_grouped[0][:, 512:])
+        y_done.append(second_product(2, 5, "late"))
+        round_y(0, y_done[0])
         quantise_z(3)
-        planes(0, [0, 1])
-        second_product(3, y_grouped[1][:, 512:], "vector first")
-        planes(1, [2, 3])
+        round_y(1, y_done[1])
+        round_y(2, y_done[2])
+        planes(0)
+        second_product(3, 6, "vector first")
+        planes(1)
 
         for q in range(4):
             queue = nc.sync if q % 2 == 0 else nc.scalar

@@ -49,8 +49,10 @@ def tile_picked_yjk_none_po_kernel(
         gate_sb = [keep.tile([P, S], F32, name=f"gate_sb{d}") for d in range(2)]
         ident = keep.tile([P, P], F32, name="ident")
         ident_bf = keep.tile([P, P], BF16, name="ident_bf")
-        h_sb = [keep.tile([P, S + SPARE], F32, name=f"h_sb{i}", align_bytes=64) for i in range(TILES)]
-        gg_sb = [keep.tile([P, S + SPARE], F32, name=f"gg_sb{i}", align_bytes=64) for i in range(TILES)]
+        h_sb = [keep.tile([P, S + SPARE], F32, name=f"h_sb{i}", align_bytes=64) for i in (0, 2, 3)]
+        h_sb.insert(1, shared.tile([P, S + SPARE], F32, name="h_sb1", align_bytes=64, offset=int(29.5 * 1024)))
+        gg_sb = [shared.tile([P, S + SPARE], F32, name="gg_sb0", align_bytes=64, offset=int(44.5 * 1024))]
+        gg_sb.extend(keep.tile([P, S + SPARE], F32, name=f"gg_sb{i}", align_bytes=64) for i in range(1, TILES))
 
         def load_w1(first, count, o, offset, queue):
             raw = shared.tile([P, 4, P * count], F32, name=f"w1_raw{first}_{o}", offset=offset, align_bytes=64)
@@ -68,8 +70,9 @@ def tile_picked_yjk_none_po_kernel(
         w2s_raw = keep.tile([P, N], U8, name="w2s_raw")
         nc.vector.memset(w2s_raw[:].bitcast(I32), 0)
         nc.vector.memset(gate_rows[:], 0.0)
-        for i in range(TILES):
+        for i in (0, 2, 3):
             nc.vector.memset(h_sb[i][:, S:], 0.0)
+        for i in range(1, TILES):
             nc.vector.memset(gg_sb[i][:, S:], 0.0)
         nc.vector.tensor_copy(out=ident_bf[:], in_=ident[:])
 
@@ -110,15 +113,19 @@ def tile_picked_yjk_none_po_kernel(
         rooms = {
             "w1_codes1": 27,
             "plain0_0_0": 27,
-            "first0_1": 10,
-            "larger0_0": 14.5,
-            "first1_1": 12.5,
-            "first1_0": 15.5,
             "first3_1": 36,
             "ee0_0": 36,
             "ee0_1": 36.5,
             "ee1_0": 37,
             "ee1_1": 37.5,
+            "w1_codes0": 48,
+            "w1_grouped2": 46.5,
+            "w1_grouped3": 48.5,
+            "first1_1": 47,
+            "larger0_0": 49,
+            "first1_0": 50,
+            "first0_0": 9,
+            "first0_1": 11,
         }
 
         def place(pool_tile_shape, dtype, name, offset):
@@ -163,13 +170,16 @@ def tile_picked_yjk_none_po_kernel(
         quantise_w1(0, 0, PASSES, early[:], place([P, PASSES * P], U32, "w1_codes0", None))
         nc.vector.tensor_copy(x_first[:], x_table[0][:].bitcast(U32).indirect(offs_sb[:]))
         nc.vector.tensor_copy(xs_picked[:], xs_table[:].indirect(offs_sb[:]))
-        x_second = place([P, S], U32, "x_second", xs_at)
-        x_picked = [x_first, x_second]
-        half = S // 2
-        for k in range(2):
+        PIECES = [slice(0, 256), slice(256, 512)]
+        PIECE_BANKS = [0, 1]
+        PIECE_COPIES = [nc.scalar.copy] * 2
+        x_second = []
+        for nodes in PIECES:
+            width = nodes.stop - nodes.start
+            x_second.append(place([P, width], U32, f"x_second{nodes.start}", xs_at + 4 * nodes.start))
             nc.vector.tensor_copy(
-                x_second[:, half * k : half * (k + 1)],
-                x_table[1][:].bitcast(U32).indirect(offs_sb[:, 16 * k : 16 * (k + 1)]),
+                x_second[-1][:],
+                x_table[1][:].bitcast(U32).indirect(offs_sb[:, nodes.start // 16 : nodes.stop // 16]),
             )
         w2_sc = place([P, N], U8, "w2_sc", at)
         nc.vector.memset(w2_sc[:].bitcast(I32), 0)
@@ -178,31 +188,42 @@ def tile_picked_yjk_none_po_kernel(
                 out=w2_sc[32 * q : 32 * q + 4, :].bitcast(I32), in_=w2s_dealt[4 * q : 4 * q + 4, :].bitcast(I32)
             )
 
-        def first_product(i, bank, nodes, copy):
-            acc = bank_tile(bank, f"acc{i}_{nodes.start}")
-            width = nodes.stop - nodes.start
-            for o in range(PASSES):
-                cols = slice((i * PASSES + o) * P, (i * PASSES + o + 1) * P)
-                nc.tensor.matmul_mx(
-                    out=acc[:, :width],
-                    lhsT=w1_codes[i, o].bitcast(FP8X4),
-                    lhsT_scale=w1_scales[:, cols],
-                    rhs=x_picked[o][:, nodes].bitcast(FP8X4),
-                    rhs_scale=xs_picked[4 * o : P, nodes],
-                    start=(o == 0),
-                    stop=(o == PASSES - 1),
-                )
-            copy(out=h_sb[i][:, nodes], in_=acc[:, :width])
+        def first_pass(i, o, acc, nodes, words):
+            cols = slice((i * PASSES + o) * P, (i * PASSES + o + 1) * P)
+            nc.tensor.matmul_mx(
+                out=acc,
+                lhsT=w1_codes[i, o].bitcast(FP8X4),
+                lhsT_scale=w1_scales[:, cols],
+                rhs=words.bitcast(FP8X4),
+                rhs_scale=xs_picked[4 * o : P, nodes],
+                start=(o == 0),
+                stop=(o == PASSES - 1 and (i == 0 or nodes.stop == S)),
+            )
 
-        for k in range(2):
-            first_product(0, k, slice(half * k, half * (k + 1)), [nc.scalar.copy, nc.vector.tensor_copy][k])
+        def first_product(i, bank, nodes, copy):
+            acc = bank_tile(bank, f"acc{i}")
+            first_pass(i, 0, acc[:], nodes, x_first[:])
+            for piece, words in zip(PIECES, x_second):
+                first_pass(i, 1, acc[:, piece], piece, words[:])
+            copy(out=h_sb[i][:, nodes], in_=acc[:])
+
+        accs = [bank_tile(bank, f"acc0_{bank}") for bank in PIECE_BANKS]
+        for acc, nodes in zip(accs, PIECES):
+            first_pass(0, 0, acc[:, : nodes.stop - nodes.start], nodes, x_first[:, nodes])
+        for acc, nodes, words in zip(accs, PIECES, x_second):
+            first_pass(0, 1, acc[:, : nodes.stop - nodes.start], nodes, words[:])
+        for acc, nodes, copy in zip(accs, PIECES, PIECE_COPIES):
+            copy(out=h_sb[0][:, nodes], in_=acc[:, : nodes.stop - nodes.start])
         grouped_at = at + 2048
         grouped = {}
         for i in range(1, TILES):
             grouped[i] = place([P, PASSES * 512], BF16, f"w1_grouped{i}", grouped_at + 2048 * (i - 1))
             for o in range(PASSES):
                 w1_grouped[i, o] = grouped[i][:, 512 * o : 512 * (o + 1)]
-                group_w1(i, o, nc.scalar.copy)
+
+        def cast_tile(i, copy):
+            for o in range(PASSES):
+                group_w1(i, o, copy)
 
         def next_tile(i, bank):
             quantise_w1(i, 0, PASSES, grouped[i][:], place([P, PASSES * P], U32, f"w1_codes{i}", None))
@@ -369,11 +390,17 @@ def tile_picked_yjk_none_po_kernel(
         def first_sum(i, terms):
             nc.vector.tensor_tensor(gg_sb[i][:, :S], terms[0][:], terms[1][:], ADD)
 
-        terms = [weighted(h_sb[0], 0, ALL, "first0_0")]
-        next_tile(1, 2)
-        terms.append(weighted(h_sb[0], 1, ALL, "first0_1"))
-        first_sum(0, terms)
+        cast_tile(1, nc.vector.tensor_copy)
+        quantise_w1(1, 0, PASSES, grouped[1][:], place([P, PASSES * P], U32, "w1_codes1", None))
+        for o in range(PASSES):
+            for i in (2, 3):
+                group_w1(i, o, nc.scalar.copy)
+        first_product(1, 2, slice(0, S), nc.scalar.copy)
+        terms = [weighted(h_sb[0], d, ALL, f"first0_{d}") for d in range(2)]
         next_tile(2, 0)
+        nc.vector.memset(gg_sb[0][:, S:], 0.0)
+        first_sum(0, terms)
+        nc.vector.memset(h_sb[1][:, S:], 0.0)
         next_tile(3, 1)
         plain_gather(0, gg_sb[0], 0, ALL, 3)
         plain_gather(0, gg_sb[0], 1, ALL, 4)

@@ -334,13 +334,13 @@ def tile_picked_yjk_none_po_kernel(
         z_codes = keep.tile([P, S], U32, name="z_codes", align_bytes=64)
         z_scales = keep.tile([P, S], U8, name="z_scales", align_bytes=64)
 
-        def turn_z(b, bank):
+        def turn_z(b, bank, copy=nc.scalar.copy):
             bank = bank_tile(bank, f"z_back{b}")
             words = zT[b // 2][:].bitcast(F32)
             for u in range(2):
                 at_word = P * (2 * (b % 2) + u)
                 nc.tensor.transpose(bank[:, P * u : P * (u + 1)], words[:, at_word : at_word + P], ident[:])
-            nc.scalar.copy(
+            copy(
                 out=z_grouped[b].bitcast(F32).rearrange("p (n u) -> p n u", u=2),
                 in_=bank[:, : 2 * P].rearrange("p (u n) -> p n u", u=2),
             )
@@ -446,7 +446,7 @@ def tile_picked_yjk_none_po_kernel(
         y_done = [second_product(0, 3, "late")]
         depth_max(3, 1)
         turn_z(2, 0)
-        turn_z(3, 2)
+        turn_z(3, 2, nc.vector.tensor_copy)
         quantise_z(1)
         y_done.append(second_product(1, 4, "late"))
         quantise_z(2)

@@ -442,15 +442,15 @@ def tile_picked_yjk_none_po_kernel(
         depth_max(1, 1)
         depth_max(2, 1)
         second_sum(3, 1)
-        quantise_z(0)
-        y_done = [second_product(0, 3, "late")]
         depth_max(3, 1)
         turn_z(2, 0)
-        turn_z(3, 2, nc.vector.tensor_copy)
+        turn_z(3, 2)
+        quantise_z(0)
+        y_done = [second_product(0, 5, "late")]
         quantise_z(1)
         y_done.append(second_product(1, 4, "late"))
         quantise_z(2)
-        y_done.append(second_product(2, 5, "late"))
+        y_done.append(second_product(2, 3, "late"))
         round_y(0, y_done[0])
         quantise_z(3)
         round_y(1, y_done[1])

@@ -382,10 +382,14 @@ def tile_picked_yjk_none_po_kernel(
                 in_=y[:].rearrange("p t (c e) -> p c t e", e=4),
             )
 
-        def planes(k):
-            cols = nodes_of(HALVES[k])
-            nc.vector.quantize_mx(out=y_words[:, cols].bitcast(FP8X4), scales=y_scales[:, cols], in_=y_grouped[k])
-            nc.sync.dma_start(out=out_words[:, cols], in_=y_words[:, cols].bitcast(I32))
+        def planes(blocks):
+            cols = nodes_of(blocks)
+            start = 512 * (blocks[0] % 2)
+            nc.vector.quantize_mx(
+                out=y_words[:, cols].bitcast(FP8X4),
+                scales=y_scales[:, cols],
+                in_=y_grouped[blocks[0] // 2][:, start : start + 512 * len(blocks)],
+            )
 
         def first_sum(i, terms):
             nc.vector.tensor_tensor(gg_sb[i][:, :S], terms[0][:], terms[1][:], ADD)
@@ -455,10 +459,11 @@ def tile_picked_yjk_none_po_kernel(
         quantise_z(3)
         round_y(1, y_done[1])
         round_y(2, y_done[2])
-        planes(0)
+        planes([0, 1])
         second_product(3, 6, "vector first")
-        planes(1)
+        planes([2, 3])
 
+        nc.sync.dma_start(out=out_words, in_=y_words[:].bitcast(I32))
         for q in range(4):
             queue = nc.sync if q % 2 == 0 else nc.scalar
             queue.dma_start(

@@ -21,7 +21,9 @@ K, T, S, H, N = 1024, 2048, 512, 512, 512
 PASSES = K // 512
 TILES = H // P
 BLOCKS = S // P
+HALF = S // 2
 SPARE = 16
+BYTES_OF = {F32: 4, I32: 4, U32: 4, BF16: 2, U8: 1}
 
 FLOPS = 2 * K * H * S + 2 * H * N * S
 
@@ -35,53 +37,61 @@ def tile_picked_yjk_none_po_kernel(
         shared = ctx.enter_context(tc.tile_pool(name="shared", bufs=1))
         psum = ctx.enter_context(tc.psum_pool(name="psum", bufs=1))
 
-        def bank_tile(bank, name):
-            return psum.tile([P, 512], F32, name=name, offset=2048 * bank)
+        def bank_tile(bank, name, dtype=F32):
+            return psum.tile([P, 2048 // BYTES_OF[dtype]], dtype, name=name, offset=2048 * bank)
+
+        def own(shape, dtype, name):
+            return keep.tile(shape, dtype, name=name, align_bytes=64)
+
+        starts = {"end": 0}
+
+        def first_tenant(shape, dtype, name, room):
+            starts[name] = starts["end"]
+            starts["end"] = starts[name] + room
+            return shared.tile(shape, dtype, name=name, align_bytes=64, offset=starts[name])
+
+        def middle_tenant(shape, dtype, name, before, room):
+            starts["end"] = starts["end"] + before
+            return first_tenant(shape, dtype, name, room)
+
+        def tenant(older, shape, dtype, name, shift=0):
+            starts[name] = starts[older] + shift
+            return shared.tile(shape, dtype, name=name, align_bytes=64, offset=starts[name])
 
         offs_sb = keep.tile([P, S // 16], U16, name="offs_sb")
         pos_sb = [keep.tile([P, S // 16], U16, name=f"pos_sb{d}") for d in range(2)]
-        x_table = []
-        raw_at = 8 * T
-        xs_at = raw_at + 8 * 2048
-        xs_table = shared.tile([P, T], U8, name="xs_table", offset=xs_at, align_bytes=64)
-        w1_raw = [[None, None] for i in range(TILES)]
-        gate_rows = keep.tile([P, P], F32, name="gate_rows")
-        gate_sb = [keep.tile([P, S], F32, name=f"gate_sb{d}") for d in range(2)]
-        ident = keep.tile([P, P], F32, name="ident")
-        ident_bf = keep.tile([P, P], BF16, name="ident_bf")
-        h_sb = [keep.tile([P, S + SPARE], F32, name=f"h_sb{i}", align_bytes=64) for i in (0, 2, 3)]
-        h_sb.insert(1, shared.tile([P, S + SPARE], F32, name="h_sb1", align_bytes=64, offset=int(29.5 * 1024)))
-        gg_sb = [shared.tile([P, S + SPARE], F32, name="gg_sb0", align_bytes=64, offset=int(44.5 * 1024))]
-        gg_sb.extend(keep.tile([P, S + SPARE], F32, name=f"gg_sb{i}", align_bytes=64) for i in range(1, TILES))
+        x_table = [first_tenant([P, T], I32, f"x_table{o}", 4 * T) for o in range(PASSES)]
+        xs_table = first_tenant([P, T], U8, "xs_table", T)
+        gate_rows = own([P, P], F32, "gate_rows")
+        gate_sb = [own([P, S], F32, f"gate_sb{d}") for d in range(2)]
+        ident = own([P, P], F32, "ident")
+        ident_bf = own([P, P], BF16, "ident_bf")
+        h_sb = {i: own([P, S + SPARE], F32, f"h_sb{i}") for i in (0, 2, 3)}
+        w1_raw = {}
 
-        def load_w1(first, count, o, offset, queue):
-            raw = shared.tile([P, 4, P * count], F32, name=f"w1_raw{first}_{o}", offset=offset, align_bytes=64)
-            rows = w1[512 * o : 512 * (o + 1), P * first : P * (first + count)]
-            queue.dma_start(out=raw[:], in_=rows.rearrange("(p j) c -> p j c", j=4))
-            for k in range(count):
-                w1_raw[first + k][o] = raw[:, :, P * k : P * (k + 1)]
+        def load_w1(i, o, queue):
+            w1_raw[i, o] = middle_tenant([P, 4, P], F32, f"w1_raw{i}_{o}", 1024, 4 * (S + SPARE) + 1024)
+            rows = w1[512 * o : 512 * (o + 1), P * i : P * (i + 1)]
+            queue.dma_start(out=w1_raw[i, o][:], in_=rows.rearrange("(p j) c -> p j c", j=4))
 
         def load_x(o):
-            x_table.append(shared.tile([P, T], I32, name=f"x_table{o}", offset=4 * T * o, align_bytes=64))
             nc.sync.dma_start(out=x_table[o][:], in_=x_words[o].rearrange("p n t -> p (n t)").bitcast(I32))
 
         nc.gpsimd.memset(xs_table[:].bitcast(I32), 0)
         make_identity(nc, ident[:])
-        w2s_raw = keep.tile([P, N], U8, name="w2s_raw")
+        w2s_raw = own([P, N], U8, "w2s_raw")
         nc.vector.memset(w2s_raw[:].bitcast(I32), 0)
         nc.vector.memset(gate_rows[:], 0.0)
         for i in (0, 2, 3):
             nc.vector.memset(h_sb[i][:, S:], 0.0)
-        for i in range(1, TILES):
-            nc.vector.memset(gg_sb[i][:, S:], 0.0)
         nc.vector.tensor_copy(out=ident_bf[:], in_=ident[:])
 
         nc.sync.dma_start(offs_sb[:], offs)
-        w2_raw = keep.tile([P, 2 * N], U8, name="w2_raw")
+        w2_raw = own([P, 2 * N], U8, "w2_raw")
         nc.sync.dma_start(out=w2_raw[:].bitcast(I32), in_=w2_words[0].bitcast(I32))
         nc.sync.dma_start(out=w2s_raw[:16, :].bitcast(I32), in_=w2_scales[0].bitcast(I32))
         for o in range(PASSES):
-            load_w1(0, 1, o, raw_at + 2048 * o, nc.scalar)
+            load_w1(0, o, nc.scalar)
         load_x(0)
         nc.sync.dma_start(out=gate_rows[: 2 * BLOCKS, :], in_=gate[:, 0, :].rearrange("d (b c) -> d b c", c=P))
         for q in range(4):
@@ -90,14 +100,15 @@ def tile_picked_yjk_none_po_kernel(
                 in_=x_scales[:, 4 * q : 4 * q + 4, :].bitcast(I32),
             )
         load_x(1)
+        for o in range(PASSES):
+            load_w1(1, o, nc.sync)
         nc.sync.dma_start(pos_sb[0][:], pos1)
         nc.sync.dma_start(pos_sb[1][:], pos2)
-        for o in range(PASSES):
-            load_w1(1, 1, o, raw_at + 4096 + 6144 * o, nc.sync)
-        for o in range(PASSES):
-            load_w1(2, 2, o, raw_at + 6144 + 6144 * o, nc.sync)
+        for i in (2, 3):
+            for o in range(PASSES):
+                load_w1(i, o, nc.sync)
 
-        gate_cols = keep.tile([P, 2 * BLOCKS], F32, name="gate_cols")
+        gate_cols = own([P, 2 * BLOCKS], F32, "gate_cols")
         turned = bank_tile(2, "turned")
         nc.tensor.transpose(turned[:, :P], gate_rows[:], ident[:])
         nc.scalar.activation(gate_cols[:], turned[:, : 2 * BLOCKS], COPY)
@@ -108,361 +119,366 @@ def tile_picked_yjk_none_po_kernel(
                 nc.tensor.transpose(spread[:, P * b : P * (b + 1)], gate_cols[:, j : j + 1].to_broadcast([P, P]), ident[:])
             nc.scalar.copy(out=gate_sb[d][:], in_=spread[:])
 
-        at = 4 * T
-
-        rooms = {
-            "w1_codes1": 27,
-            "plain0_0_0": 27,
-            "first3_1": 36,
-            "ee0_0": 36,
-            "ee0_1": 36.5,
-            "ee1_0": 37,
-            "ee1_1": 37.5,
-            "w1_codes0": 48,
-            "w1_grouped2": 46.5,
-            "w1_grouped3": 48.5,
-            "first1_1": 47,
-            "larger0_0": 49,
-            "first1_0": 50,
-            "first0_0": 9,
-            "first0_1": 11,
-        }
-
-        def place(pool_tile_shape, dtype, name, offset):
-            if name in rooms:
-                offset = int(1024 * rooms[name])
-            if offset is None:
-                return keep.tile(pool_tile_shape, dtype, name=name, align_bytes=64)
-            return shared.tile(pool_tile_shape, dtype, name=name, align_bytes=64, offset=offset)
-
-        w1_scales = keep.tile([P, TILES * PASSES * P], U8, name="w1_scales", align_bytes=64)
+        w1_scales = own([P, TILES * PASSES * P], U8, "w1_scales")
         w1_codes = {}
         w1_grouped = {}
 
-        def group_w1(i, o, copy):
+        def cast_w1(i, o, copy):
             copy(
-                out=w1_grouped[i, o].rearrange("p (u c e j) -> p c j u e", u=2, e=2, j=4),
-                in_=w1_raw[i][o].rearrange("p j (c u e) -> p c j u e", u=2, e=2),
+                out=w1_grouped[i][:, 512 * o : 512 * (o + 1)].rearrange("p (u c e j) -> p c j u e", u=2, e=2, j=4),
+                in_=w1_raw[i, o][:].rearrange("p j (c u e) -> p c j u e", u=2, e=2),
             )
 
-        def quantise_w1(i, first, count, grouped, codes):
-            cols = slice((i * PASSES + first) * P, (i * PASSES + first + count) * P)
+        def scale_cols(i, o, count=1):
+            return slice((i * PASSES + o) * P, (i * PASSES + o + count) * P)
+
+        def quantise_w1(i):
             nc.vector.quantize_mx(
-                out=codes[:].bitcast(FP8X4),
-                scales=w1_scales[:, cols],
-                in_=grouped,
+                out=w1_codes[i][:].bitcast(FP8X4), scales=w1_scales[:, scale_cols(i, 0, PASSES)], in_=w1_grouped[i][:]
             )
-            for o in range(count):
-                w1_codes[i + (first + o) // PASSES, (first + o) % PASSES] = codes[:, P * o : P * (o + 1)]
 
-        xs_picked = keep.tile([P, S], U8, name="xs_picked", align_bytes=64)
-        x_first = keep.tile([P, S], U32, name="x_first", align_bytes=64)
-        w2_codes = place([P, 4, P, 2], U8, "w2_codes", None)
+        xs_picked = own([P, S], U8, "xs_picked")
+        x_first = own([P, S], U32, "x_first")
+        w2_codes = own([P, 4, P, 2], U8, "w2_codes")
         nc.vector.tensor_copy(out=w2_codes[:], in_=w2_raw[:].rearrange("p (m t b) -> p t m b", t=4, b=2))
-        w2s_dealt = place([P, N], U8, "w2s_dealt", None)
+        w2s_dealt = own([P, N], U8, "w2s_dealt")
         nc.vector.tensor_copy(
             out=w2s_dealt[:].rearrange("p (t m) -> p t m", t=4), in_=w2s_raw[:].rearrange("p (m t) -> p t m", t=4)
         )
-        early = place([P, PASSES * 512], BF16, "w1_grouped0", None)
+        w1_grouped[0] = own([P, PASSES * 512], BF16, "w1_grouped0")
+        w1_codes[0] = first_tenant([P, PASSES * P], U32, "w1_codes0", 2048)
         for o in range(PASSES):
-            w1_grouped[0, o] = early[:, 512 * o : 512 * (o + 1)]
-            group_w1(0, o, nc.vector.tensor_copy)
-        quantise_w1(0, 0, PASSES, early[:], place([P, PASSES * P], U32, "w1_codes0", None))
+            cast_w1(0, o, nc.vector.tensor_copy)
+        quantise_w1(0)
         nc.vector.tensor_copy(x_first[:], x_table[0][:].bitcast(U32).indirect(offs_sb[:]))
         nc.vector.tensor_copy(xs_picked[:], xs_table[:].indirect(offs_sb[:]))
-        PIECES = [slice(0, 256), slice(256, 512)]
-        PIECE_BANKS = [0, 1]
-        PIECE_COPIES = [nc.scalar.copy] * 2
-        x_second = []
-        for nodes in PIECES:
-            width = nodes.stop - nodes.start
-            x_second.append(place([P, width], U32, f"x_second{nodes.start}", xs_at + 4 * nodes.start))
-            nc.vector.tensor_copy(
-                x_second[-1][:],
-                x_table[1][:].bitcast(U32).indirect(offs_sb[:, nodes.start // 16 : nodes.stop // 16]),
-            )
-        w2_sc = place([P, N], U8, "w2_sc", at)
-        nc.vector.memset(w2_sc[:].bitcast(I32), 0)
-        for q in range(4):
-            nc.sync.dma_start(
-                out=w2_sc[32 * q : 32 * q + 4, :].bitcast(I32), in_=w2s_dealt[4 * q : 4 * q + 4, :].bitcast(I32)
-            )
 
-        def first_pass(i, o, acc, nodes, words):
-            cols = slice((i * PASSES + o) * P, (i * PASSES + o + 1) * P)
+        def half(k):
+            return slice(HALF * k, HALF * (k + 1))
+
+        def list_half(tile, k):
+            return tile[:, HALF // 16 * k : HALF // 16 * (k + 1)]
+
+        x_second = []
+        for k in range(2):
+            x_second.append(tenant("xs_table", [P, HALF], U32, f"x_second{k}", 4 * HALF * k))
+            nc.vector.tensor_copy(x_second[k][:], x_table[1][:].bitcast(U32).indirect(list_half(offs_sb, k)))
+
+        def first_pass(i, o, acc, nodes, words, stop):
             nc.tensor.matmul_mx(
                 out=acc,
-                lhsT=w1_codes[i, o].bitcast(FP8X4),
-                lhsT_scale=w1_scales[:, cols],
+                lhsT=w1_codes[i][:, P * o : P * (o + 1)].bitcast(FP8X4),
+                lhsT_scale=w1_scales[:, scale_cols(i, o)],
                 rhs=words.bitcast(FP8X4),
                 rhs_scale=xs_picked[4 * o : P, nodes],
                 start=(o == 0),
-                stop=(o == PASSES - 1 and (i == 0 or nodes.stop == S)),
+                stop=stop,
             )
 
-        def first_product(i, bank, nodes, copy):
-            acc = bank_tile(bank, f"acc{i}")
-            first_pass(i, 0, acc[:], nodes, x_first[:])
-            for piece, words in zip(PIECES, x_second):
-                first_pass(i, 1, acc[:, piece], piece, words[:])
-            copy(out=h_sb[i][:, nodes], in_=acc[:])
+        h_acc = {}
 
-        accs = [bank_tile(bank, f"acc0_{bank}") for bank in PIECE_BANKS]
-        for acc, nodes in zip(accs, PIECES):
-            first_pass(0, 0, acc[:, : nodes.stop - nodes.start], nodes, x_first[:, nodes])
-        for acc, nodes, words in zip(accs, PIECES, x_second):
-            first_pass(0, 1, acc[:, : nodes.stop - nodes.start], nodes, words[:])
-        for acc, nodes, copy in zip(accs, PIECES, PIECE_COPIES):
-            copy(out=h_sb[0][:, nodes], in_=acc[:, : nodes.stop - nodes.start])
-        grouped_at = at + 2048
-        grouped = {}
-        for i in range(1, TILES):
-            grouped[i] = place([P, PASSES * 512], BF16, f"w1_grouped{i}", grouped_at + 2048 * (i - 1))
-            for o in range(PASSES):
-                w1_grouped[i, o] = grouped[i][:, 512 * o : 512 * (o + 1)]
+        def first_product(i, bank):
+            h_acc[i] = bank_tile(bank, f"acc{i}")
+            first_pass(i, 0, h_acc[i][:], slice(0, S), x_first[:], False)
+            for k in range(2):
+                first_pass(i, 1, h_acc[i][:, half(k)], half(k), x_second[k][:], k == 1)
 
-        def cast_tile(i, copy):
-            for o in range(PASSES):
-                group_w1(i, o, copy)
+        def copy_h(i):
+            nc.scalar.copy(out=h_sb[i][:, :S], in_=h_acc[i][:])
 
-        def next_tile(i, bank):
-            quantise_w1(i, 0, PASSES, grouped[i][:], place([P, PASSES * P], U32, f"w1_codes{i}", None))
-            first_product(i, bank, slice(0, S), nc.scalar.copy)
+        accs = [bank_tile(k, f"acc0_{k}") for k in range(2)]
+        for k in range(2):
+            first_pass(0, 0, accs[k][:, :HALF], half(k), x_first[:, half(k)], False)
+        for k in range(2):
+            first_pass(0, 1, accs[k][:, :HALF], half(k), x_second[k][:], True)
+        for k in range(2):
+            nc.scalar.copy(out=h_sb[0][:, half(k)], in_=accs[k][:, :HALF])
 
-        def offsets(d, blocks):
-            return pos_sb[d][:, 8 * blocks[0] : 8 * (blocks[0] + len(blocks))]
+        terms = {}
+        gg_sb = {}
 
-        def nodes_of(blocks):
-            return slice(P * blocks[0], P * (blocks[0] + len(blocks)))
+        def weighted(i, d, room):
+            terms[i, d] = room
+            if h_sb[i].shape[1] > S:
+                nc.vector.tensor_tensor(room[:], h_sb[i][:].indirect(pos_sb[d][:]), gate_sb[d][:], MULT)
+                return
+            for k in range(2):
+                picked = h_sb[i][:].indirect(list_half(pos_sb[d], k))
+                nc.vector.tensor_tensor(room[:, half(k)], picked, gate_sb[d][:, half(k)], MULT)
 
-        def weighted(window, d, blocks, name):
-            term = place([P, P * len(blocks)], F32, name, None)
-            nc.vector.tensor_tensor(term[:], window[:].indirect(offsets(d, blocks)), gate_sb[d][:, nodes_of(blocks)], MULT)
-            return term
+        def first_sum(i):
+            nc.vector.tensor_tensor(gg_sb[i][:], terms[i, 0][:], terms[i, 1][:], ADD)
 
-        def turned_blocks(bank, source, count, identity):
-            for k in range(count):
-                nc.tensor.transpose(bank[:, P * k : P * (k + 1)], source[:, P * k : P * (k + 1)], identity[:])
+        def turn_blocks(out, source, identity):
+            for j in range(source.shape[1] // P):
+                nc.tensor.transpose(out[:, P * j : P * (j + 1)], source[:, P * j : P * (j + 1)], identity[:])
 
-        ALL = [0, 1, 2, 3]
-        HALVES = [[0, 1], [2, 3]]
-        zT = [keep.tile([P, 2 * H], BF16, name=f"zT{k}") for k in range(2)]
-        mT = {}
+        larger_turned = {}
+
+        larger = {}
+
+        def first_max(i, room):
+            larger[i] = room
+            nc.vector.tensor_tensor(larger[i][:], h_sb[i][:, :S], gg_sb[i][:], MAX)
+
+        def turn_larger(i):
+            if i % 2 == 0:
+                both = bank_tile(6 + i // 2, f"larger_turned{i}", BF16)
+                for j in range(2):
+                    larger_turned[i + j] = both[:, S * j : S * (j + 1)]
+            turn_blocks(larger_turned[i], larger[i][:], ident_bf)
+
+        turned_terms = {}
         scaled = {}
         ee = {}
 
-        def z_part(i, k):
-            return zT[k][:].rearrange("n (g i c) -> n g i c", i=TILES, c=64)[:, :, i, :]
+        def fetch(i, d, halves, bank, *plains):
+            parts = [plain[:, half(j)] for plain in plains for j in range(plain.shape[1] // HALF)]
+            turned_term = bank_tile(bank, f"turned{i}_{halves[0]}_{d}")
+            for j, k in enumerate(halves):
+                nc.scalar.activation(parts[j], gg_sb[i][:].indirect(list_half(pos_sb[d], k)), COPY)
+                turned_terms[i, k, d] = turned_term[:, half(j)]
+                turn_blocks(turned_terms[i, k, d], parts[j], ident)
 
-        def first_max(i, blocks, bank):
-            larger = place([P, P * len(blocks)], BF16, f"larger{i}_{blocks[0]}", None)
-            nc.vector.tensor_tensor(larger[:], h_sb[i][:, nodes_of(blocks)], gg_sb[i][:, nodes_of(blocks)], MAX)
-            turned_m = psum.tile([P, 512], BF16, name=f"mT{i}_{blocks[0]}", offset=2048 * bank)
-            turned_blocks(turned_m, larger, len(blocks), ident_bf)
-            for j, b in enumerate(blocks):
-                mT[i, b] = (turned_m, P * j)
+        def scale_first(i, halves, room):
+            for j, k in enumerate(halves):
+                scaled[i, k] = room[:, half(j)]
+                for c in range(2):
+                    b = 2 * k + c
+                    nc.scalar.activation(
+                        scaled[i, k][:, P * c : P * (c + 1)],
+                        turned_terms[i, k, 0][:, P * c : P * (c + 1)],
+                        COPY,
+                        scale=gate_cols[:, b : b + 1],
+                    )
 
-        turned_terms = {}
-
-        def plain_gather(key, window, d, blocks, bank, term=None):
-            if term is None:
-                term = place([P, P * len(blocks)], F32, f"plain{key}_{blocks[0]}_{d}", None)[:]
-            nc.scalar.activation(term, window[:].indirect(offsets(d, blocks)), COPY)
-            turned_term = bank_tile(bank, f"plainT{key}_{blocks[0]}_{d}")
-            turned_blocks(turned_term, term, len(blocks), ident)
-            for j, b in enumerate(blocks):
-                turned_terms[key, d, b] = turned_term[:, P * j : P * (j + 1)]
-
-        def scale_first(key, blocks):
-            room = place([P, P * len(blocks)], F32, f"scaled{key}_{blocks[0]}", None)
-            for j, b in enumerate(blocks):
-                scaled[key, b] = room[:, P * j : P * (j + 1)]
-                nc.scalar.activation(scaled[key, b], turned_terms[key, 0, b], COPY, scale=gate_cols[:, b : b + 1])
-
-        def scale_and_add(key, blocks, out):
-            for j, b in enumerate(blocks):
+        def second_sum(i, k, blocks=(0, 1)):
+            for c in blocks:
+                b = BLOCKS + 2 * k + c
                 nc.vector.scalar_tensor_tensor(
-                    out[:, P * j : P * (j + 1)],
-                    turned_terms[key, 1, b],
-                    gate_cols[:, BLOCKS + b : BLOCKS + b + 1],
-                    scaled[key, b],
+                    ee[i, k][:, P * c : P * (c + 1)],
+                    turned_terms[i, k, 1][:, P * c : P * (c + 1)],
+                    gate_cols[:, b : b + 1],
+                    scaled[i, k][:, P * c : P * (c + 1)],
                     MULT,
                     ADD,
                 )
 
-        def second_sum(i, k):
-            ee[i, k] = place([P, 2 * P], BF16, f"ee{i}_{k}", None)
-            scale_and_add(i, HALVES[k], ee[i, k])
+        zT = [own([P, 2 * H], BF16, f"zT{k}") for k in range(2)]
 
-        def fused_sum(terms, count, bank, name):
-            summed = bank_tile(bank, name)
-            for j in range(count):
-                for d in range(2):
-                    nc.tensor.matmul(
-                        summed[:, P * j : P * (j + 1)],
-                        terms[d][:, P * j : P * (j + 1)],
-                        ident[:],
-                        start=(d == 0),
-                        stop=(d == 1),
-                        is_transpose=True,
-                    )
-            return summed
-
-        def fused_max(i, k, summed, larger):
+        def last_max(i, k, blocks=(0, 1)):
+            cols = slice(P * blocks[0], P * (blocks[-1] + 1))
+            groups = slice(2 * blocks[0], 2 * (blocks[-1] + 1))
             nc.vector.tensor_tensor(
-                z_part(i, k),
-                summed.rearrange("n (g c) -> n g c", c=64),
-                larger.rearrange("n (g c) -> n g c", c=64),
+                zT[k][:].rearrange("n (g i c) -> n g i c", i=TILES, c=64)[:, groups, i, :],
+                larger_turned[i][:, half(k)][:, cols].rearrange("n (g c) -> n g c", c=64),
+                ee[i, k][:, cols].rearrange("n (g c) -> n g c", c=64),
                 MAX,
             )
 
-        def depth_max(i, k):
-            bank, start = mT[i, HALVES[k][0]]
-            nc.vector.tensor_tensor(
-                z_part(i, k),
-                bank[:, start : start + 2 * P].rearrange("n (g c) -> n g c", c=64),
-                ee[i, k][:].rearrange("n (g c) -> n g c", c=64),
-                MAX,
-            )
-
-        y_words = keep.tile([P, S], U32, name="y_words", align_bytes=64)
-        y_scales = keep.tile([P, S], U8, name="y_scales", align_bytes=64)
+        y_words = own([P, S], U32, "y_words")
+        y_scales = own([P, S], U8, "y_scales")
         out_rows = out_0.rearrange("(p t) n -> p t n", t=4)
         out_words = out_1[0].rearrange("p n t -> p (n t)").bitcast(I32)
-        z_grouped = [place([P, 4 * P], BF16, f"z_grouped{b}", None)[:] for b in ALL]
-        y_grouped = [place([P, 8 * P], BF16, f"y_grouped{k}", None)[:] for k in range(2)]
-        z_codes = keep.tile([P, S], U32, name="z_codes", align_bytes=64)
-        z_scales = keep.tile([P, S], U8, name="z_scales", align_bytes=64)
+        z_codes = own([P, S], U32, "z_codes")
+        z_scales = own([P, S], U8, "z_scales")
+        y_grouped = [own([P, 4 * HALF], BF16, f"y_grouped{k}") for k in range(2)]
+        z_back = {}
+        z_grouped = {}
 
-        def turn_z(b, bank, copy=nc.scalar.copy):
-            bank = bank_tile(bank, f"z_back{b}")
-            words = zT[b // 2][:].bitcast(F32)
-            for u in range(2):
-                at_word = P * (2 * (b % 2) + u)
-                nc.tensor.transpose(bank[:, P * u : P * (u + 1)], words[:, at_word : at_word + P], ident[:])
-            copy(
-                out=z_grouped[b].bitcast(F32).rearrange("p (n u) -> p n u", u=2),
-                in_=bank[:, : 2 * P].rearrange("p (u n) -> p n u", u=2),
+        def nodes_of(blocks):
+            return slice(P * blocks[0], P * (blocks[-1] + 1))
+
+        def turn_z(blocks, bank):
+            z_back[blocks] = bank_tile(bank, f"z_back{blocks[0]}")
+            words = zT[blocks[0] // 2][:].bitcast(F32)
+            start = 2 * P * (blocks[0] % 2)
+            turn_blocks(z_back[blocks], words[:, start : start + 2 * P * len(blocks)], ident)
+
+        def group_z(blocks):
+            z_grouped[blocks] = own([P, 4 * P * len(blocks)], BF16, f"z_grouped{blocks[0]}")
+            nc.scalar.copy(
+                out=z_grouped[blocks][:].bitcast(F32).rearrange("p (b n u) -> p b n u", u=2, n=P),
+                in_=z_back[blocks][:, : 2 * P * len(blocks)].rearrange("p (b u n) -> p b n u", u=2, n=P),
             )
 
-        def quantise_z(b):
-            cols = slice(P * b, P * (b + 1))
-            nc.vector.quantize_mx(out=z_codes[:, cols].bitcast(FP8X4), scales=z_scales[:, cols], in_=z_grouped[b])
-
-        def second_product(b, bank, way):
-            cols = slice(P * b, P * (b + 1))
-            rounded = y_grouped[b // 2][:, 512 * (b % 2) : 512 * (b % 2 + 1)]
-            acc = bank_tile(bank, f"y_acc{b}")
-            for t in range(4):
-                nc.tensor.matmul_mx(
-                    out=acc[:, P * t : P * (t + 1)],
-                    lhsT=w2_codes[:, t].rearrange("p m b -> p (m b)").bitcast(FP4X4),
-                    lhsT_scale=w2_sc[:, P * t : P * (t + 1)],
-                    rhs=z_codes[:, cols].bitcast(FP8X4),
-                    rhs_scale=z_scales[:, cols],
-                    start=True,
-                    stop=True,
-                )
-            if way == "vector first":
-                nc.vector.tensor_copy(
-                    out=rounded.rearrange("p (n t) -> p n t", t=4), in_=acc[:].rearrange("p (t n) -> p n t", t=4)
-                )
-            y = keep.tile([P, 4, P], F32, name=f"y{b}")
-            nc.scalar.copy(out=y[:], in_=acc[:].rearrange("p (t n) -> p t n", t=4))
-            nc.sync.dma_start(out=out_rows[:, :, cols], in_=y[:])
-            if way == "scalar":
-                nc.scalar.copy(
-                    out=rounded.rearrange("p (n t) -> p n t", t=4), in_=acc[:].rearrange("p (t n) -> p n t", t=4)
-                )
-            return y
-
-        def round_y(b, y):
-            nc.vector.tensor_copy(
-                out=y_grouped[b // 2][:, 512 * (b % 2) : 512 * (b % 2 + 1)].rearrange("p (c e t) -> p c t e", e=4, t=4),
-                in_=y[:].rearrange("p t (c e) -> p c t e", e=4),
-            )
-
-        def planes(blocks):
+        def quantise_z(blocks):
             cols = nodes_of(blocks)
-            start = 512 * (blocks[0] % 2)
-            nc.vector.quantize_mx(
-                out=y_words[:, cols].bitcast(FP8X4),
-                scales=y_scales[:, cols],
-                in_=y_grouped[blocks[0] // 2][:, start : start + 512 * len(blocks)],
+            nc.vector.quantize_mx(out=z_codes[:, cols].bitcast(FP8X4), scales=z_scales[:, cols], in_=z_grouped[blocks][:])
+
+        def second_pass(t, acc, cols):
+            nc.tensor.matmul_mx(
+                out=acc,
+                lhsT=w2_codes[:, t].rearrange("p m b -> p (m b)").bitcast(FP4X4),
+                lhsT_scale=w2_sc[:, P * t : P * (t + 1)],
+                rhs=z_codes[:, cols].bitcast(FP8X4),
+                rhs_scale=z_scales[:, cols],
+                start=True,
+                stop=True,
             )
 
-        def first_sum(i, terms):
-            nc.vector.tensor_tensor(gg_sb[i][:, :S], terms[0][:], terms[1][:], ADD)
+        def planes(k):
+            nc.vector.quantize_mx(
+                out=y_words[:, half(k)].bitcast(FP8X4), scales=y_scales[:, half(k)], in_=y_grouped[k][:]
+            )
 
-        cast_tile(1, nc.vector.tensor_copy)
-        quantise_w1(1, 0, PASSES, grouped[1][:], place([P, PASSES * P], U32, "w1_codes1", None))
+        w1_grouped[1] = tenant("x_table1", [P, PASSES * 512], BF16, "w1_grouped1", 2048)
+        w1_codes[1] = first_tenant([P, PASSES * P], U32, "w1_codes1", 2048)
         for o in range(PASSES):
-            for i in (2, 3):
-                group_w1(i, o, nc.scalar.copy)
-        first_product(1, 2, slice(0, S), nc.scalar.copy)
-        terms = [weighted(h_sb[0], d, ALL, f"first0_{d}") for d in range(2)]
-        next_tile(2, 0)
-        nc.vector.memset(gg_sb[0][:, S:], 0.0)
-        first_sum(0, terms)
-        nc.vector.memset(h_sb[1][:, S:], 0.0)
-        next_tile(3, 1)
-        plain_gather(0, gg_sb[0], 0, ALL, 3)
-        plain_gather(0, gg_sb[0], 1, ALL, 4)
-        scale_first(0, ALL)
-        terms = [weighted(h_sb[1], d, ALL, f"first1_{d}") for d in range(2)]
-        first_max(0, ALL, 6)
-        first_sum(1, terms)
-        plain_gather(1, gg_sb[1], 0, ALL, 3)
-        plain_gather(1, gg_sb[1], 1, ALL, 5)
-        scale_first(1, ALL)
-        terms = [weighted(h_sb[2], d, ALL, f"first2_{d}") for d in range(2)]
-        first_max(1, ALL, 7)
-        first_sum(2, terms)
-        plain_gather(2, gg_sb[2], 0, ALL, 3)
-        plain_gather(2, gg_sb[2], 1, ALL, 2)
-        scale_first(2, ALL)
-        terms = [weighted(h_sb[3], d, ALL, f"first3_{d}") for d in range(2)]
-        first_max(2, ALL, 0)
-        first_sum(3, terms)
-        for k in range(2):
-            second_sum(0, k)
-        for k in range(2):
-            depth_max(0, k)
-        for k in range(2):
-            plain_gather(3, gg_sb[3], 0, HALVES[k], [3, 1][k])
-            plain_gather(3, gg_sb[3], 1, HALVES[k], [4, 6][k])
-            scale_first(3, HALVES[k])
-        second_sum(1, 0)
-        second_sum(2, 0)
-        second_sum(1, 1)
-        first_max(3, ALL, 5)
-        depth_max(1, 0)
-        depth_max(2, 0)
-        second_sum(3, 0)
-        second_sum(2, 1)
-        depth_max(3, 0)
-        turn_z(0, 3)
-        turn_z(1, 4)
-        depth_max(1, 1)
-        depth_max(2, 1)
-        second_sum(3, 1)
-        depth_max(3, 1)
-        turn_z(2, 0)
-        turn_z(3, 2)
-        quantise_z(0)
-        y_done = [second_product(0, 5, "late")]
-        quantise_z(1)
-        y_done.append(second_product(1, 4, "late"))
-        quantise_z(2)
-        y_done.append(second_product(2, 3, "late"))
-        round_y(0, y_done[0])
-        quantise_z(3)
-        round_y(1, y_done[1])
-        round_y(2, y_done[2])
-        planes([0, 1])
-        second_product(3, 6, "vector first")
-        planes([2, 3])
+            cast_w1(1, o, nc.vector.tensor_copy)
+        quantise_w1(1)
+        first_product(1, 2)
+        w1_grouped[2] = tenant("w1_codes0", [P, PASSES * 512], BF16, "w1_grouped2")
+        for o in range(PASSES):
+            cast_w1(2, o, nc.scalar.copy)
+        h_sb[1] = tenant("w1_raw2_1", [P, S], F32, "h_sb1", 1024)
+        copy_h(1)
+        w1_grouped[3] = tenant("w1_codes1", [P, PASSES * 512], BF16, "w1_grouped3")
+        for o in range(PASSES):
+            cast_w1(3, o, nc.scalar.copy)
+        w2_sc = tenant("w1_raw3_1", [P, N], U8, "w2_sc", 1024)
+        nc.gpsimd.memset(w2_sc[:].bitcast(I32), 0)
+        for q in range(4):
+            nc.sync.dma_start(
+                out=w2_sc[32 * q : 32 * q + 4, :].bitcast(I32), in_=w2s_dealt[4 * q : 4 * q + 4, :].bitcast(I32)
+            )
+        starts["late_room"] = starts["end"]
+        starts["end"] = starts["late_room"] + 4096
+        w1_codes[2] = first_tenant([P, PASSES * P], U32, "w1_codes2", 2048)
+        w1_codes[3] = middle_tenant([P, PASSES * P], U32, "w1_codes3", 512, 2560)
 
+        weighted(0, 0, tenant("w1_raw1_1", [P, S], F32, "term0_0", -1024))
+        weighted(0, 1, tenant("w1_raw1_1", [P, S], F32, "term0_1", 1024))
+        quantise_w1(2)
+        first_product(2, 0)
+        gg_sb[0] = tenant("w1_raw2_1", [P, S], F32, "gg_sb0", -1024)
+        first_sum(0)
+        BOTH = (0, 1)
+        fetch(0, 0, (0,), 3, own([P, HALF], F32, "plain0_0_0"))
+        fetch(0, 0, (1,), 6, own([P, HALF], F32, "plain0_1_0"))
+        copy_h(2)
+        for d in range(2):
+            weighted(1, d, own([P, S], F32, f"term1_{d}"))
+        first_max(0, own([P, S], BF16, "larger0"))
+        quantise_w1(3)
+        gg_sb[1] = tenant("w1_raw3_1", [P, S], F32, "gg_sb1", -1024)
+        first_sum(1)
+        fetch(0, 1, BOTH, 4, tenant("w1_codes2", [P, S], F32, "plain0_1"))
+        scale_first(0, (0,), own([P, HALF], F32, "scaled0_0"))
+        scale_first(0, (1,), own([P, HALF], F32, "scaled0_1"))
+        first_product(3, 3)
+        turn_larger(0)
+        fetch(1, 0, BOTH, 1, own([P, S], F32, "plain1_0"))
+        copy_h(3)
+        fetch(1, 1, BOTH, 5, own([P, S], F32, "plain1_1"))
+        scale_first(1, BOTH, own([P, S], F32, "scaled1"))
+
+        for d in range(2):
+            weighted(2, d, own([P, S], F32, f"term2_{d}"))
+        first_max(1, tenant("w1_codes3", [P, S], BF16, "larger1", -512))
+        gg_sb[2] = tenant("w1_codes3", [P, S], F32, "gg_sb2", 512)
+        first_sum(2)
+        turn_larger(1)
+        fetch(
+            2,
+            0,
+            BOTH,
+            7,
+            middle_tenant([P, HALF], F32, "plain2_0_0", 512, 2560),
+            first_tenant([P, HALF], F32, "plain2_1_0", 1024),
+        )
+        fetch(
+            2,
+            1,
+            BOTH,
+            2,
+            tenant("late_room", [P, HALF], F32, "plain2_0_1", 512),
+            tenant("late_room", [P, HALF], F32, "plain2_1_1", 2560),
+        )
+        for d in range(2):
+            weighted(3, d, first_tenant([P, S], F32, f"term3_{d}", 2048))
+        first_max(2, tenant("plain2_0_0", [P, S], BF16, "larger2", -512))
+        scale_first(2, BOTH, own([P, S], F32, "scaled2"))
+        gg_sb[3] = tenant("plain2_0_0", [P, S], F32, "gg_sb3", 512)
+        first_sum(3)
+        turn_larger(2)
+        ee[0, 0] = tenant("plain2_1_0", [P, HALF], BF16, "ee0_0")
+        second_sum(0, 0)
+        for i in range(1, TILES):
+            ee[i, 0] = tenant("term3_1", [P, HALF], BF16, f"ee{i}_0", 512 * i)
+        ee[0, 1] = tenant("term3_1", [P, HALF], BF16, "ee0_1")
+        ee[1, 1] = tenant("term3_0", [P, HALF], BF16, "ee1_1")
+        first_max(3, own([P, S], BF16, "larger3"))
+        turn_larger(3)
+        fetch(3, 0, (0,), 1, tenant("late_room", [P, HALF], F32, "plain3_0_0", 0))
+        fetch(3, 1, (0,), 0, tenant("late_room", [P, HALF], F32, "plain3_0_1", 1024))
+        second_sum(1, 0)
+        last_max(0, 0)
+        second_sum(0, 1)
+        last_max(1, 0)
+        fetch(3, 0, (1,), 3, tenant("late_room", [P, HALF], F32, "plain3_1_0", 2048))
+        fetch(3, 1, (1,), 4, tenant("late_room", [P, HALF], F32, "plain3_1_1", 3072))
+        scale_first(3, (0,), first_tenant([P, HALF], F32, "scaled3_0", 1024))
+        scale_first(3, (1,), own([P, HALF], F32, "scaled3_1"))
+        second_sum(2, 0)
+        last_max(0, 1)
+        second_sum(1, 1)
+        last_max(2, 0)
+        second_sum(3, 0)
+        last_max(1, 1)
+        last_max(3, 0)
+        turn_z((0,), 1)
+        turn_z((1,), 5)
+        for i in (2, 3):
+            ee[i, 1] = tenant("scaled3_0", [P, HALF], BF16, f"ee{i}_1", 512 * (i - 2))
+        second_sum(2, 1)
+        second_sum(3, 1, (0,))
+        last_max(2, 1)
+        second_sum(3, 1, (1,))
+        last_max(3, 1, (0,))
+        turn_z((2,), 0)
+        last_max(3, 1, (1,))
+        turn_z((3,), 3)
+        for b in range(BLOCKS):
+            group_z((b,))
+        y_acc = {}
+        y_sb = {}
+
+        def second_product(b, bank):
+            quantise_z((b,))
+            y_acc[b] = bank_tile(bank, f"y_acc{b}")
+            for t in range(4):
+                second_pass(t, y_acc[b][:, P * t : P * (t + 1)], nodes_of((b,)))
+
+        def copy_y(b):
+            y_sb[b] = own([P, 4, P], F32, f"y{b}")
+            nc.scalar.copy(out=y_sb[b][:], in_=y_acc[b][:].rearrange("p (t n) -> p t n", t=4))
+            nc.sync.dma_start(out=out_rows[:, :, nodes_of((b,))], in_=y_sb[b][:])
+
+        def rounded(b):
+            return y_grouped[b // 2][:, 512 * (b % 2) : 512 * (b % 2 + 1)]
+
+        def round_y(b):
+            nc.vector.tensor_copy(
+                out=rounded(b).rearrange("p (c e t) -> p c t e", e=4, t=4),
+                in_=y_sb[b][:].rearrange("p t (c e) -> p c t e", e=4),
+            )
+
+        for b, bank in enumerate((6, 2, 4)):
+            second_product(b, bank)
+        copy_y(0)
+        second_product(3, 6)
+        copy_y(1)
+        copy_y(2)
+        round_y(0)
+        round_y(1)
+        nc.vector.tensor_copy(
+            out=rounded(3).rearrange("p (n t) -> p n t", t=4), in_=y_acc[3][:].rearrange("p (t n) -> p n t", t=4)
+        )
+        copy_y(3)
+        planes(0)
+        round_y(2)
+        planes(1)
         nc.sync.dma_start(out=out_words, in_=y_words[:].bitcast(I32))
         for q in range(4):
             queue = nc.sync if q % 2 == 0 else nc.scalar

@@ -70,9 +70,10 @@ def tile_picked_yjk_none_po_kernel(
         w1_raw = {}
 
         def load_w1(i, o, queue):
-            w1_raw[i, o] = middle_tenant([P, 4, P], F32, f"w1_raw{i}_{o}", 1024, 4 * (S + SPARE) + 1024)
+            wide = middle_tenant([P, 4 * P + 64], F32, f"w1_raw{i}_{o}", 1984, 4160)
+            w1_raw[i, o] = wide[:, : 4 * P].rearrange("p (j c) -> p j c", j=4)
             rows = w1[512 * o : 512 * (o + 1), P * i : P * (i + 1)]
-            queue.dma_start(out=w1_raw[i, o][:], in_=rows.rearrange("(p j) c -> p j c", j=4))
+            queue.dma_start(out=w1_raw[i, o], in_=rows.rearrange("(p j) c -> p j c", j=4))
 
         def load_x(o):
             nc.sync.dma_start(out=x_table[o][:], in_=x_words[o].rearrange("p n t -> p (n t)").bitcast(I32))
@@ -126,7 +127,7 @@ def tile_picked_yjk_none_po_kernel(
         def cast_w1(i, o, copy):
             copy(
                 out=w1_grouped[i][:, 512 * o : 512 * (o + 1)].rearrange("p (u c e j) -> p c j u e", u=2, e=2, j=4),
-                in_=w1_raw[i, o][:].rearrange("p j (c u e) -> p c j u e", u=2, e=2),
+                in_=w1_raw[i, o].rearrange("p j (c u e) -> p c j u e", u=2, e=2),
             )
 
         def scale_cols(i, o, count=1):
@@ -222,31 +223,38 @@ def tile_picked_yjk_none_po_kernel(
             nc.vector.tensor_tensor(larger[i][:], h_sb[i][:, :S], gg_sb[i][:], MAX)
 
         def turn_larger(i):
-            if i % 2 == 0:
-                both = bank_tile(6 + i // 2, f"larger_turned{i}", BF16)
-                for j in range(2):
-                    larger_turned[i + j] = both[:, S * j : S * (j + 1)]
             turn_blocks(larger_turned[i], larger[i][:], ident_bf)
 
         turned_terms = {}
         scaled = {}
         ee = {}
 
+        shared_bank = {}
+
+        def share_bank(i, bank):
+            both = bank_tile(bank, f"shared_bank{i}")
+            shared_bank[i] = both[:, :HALF]
+            larger_turned[i] = both[:, HALF:].bitcast(BF16)
+
+        def fetch_into(i, d, k, turned_term, plain):
+            nc.scalar.activation(plain, gg_sb[i][:].indirect(list_half(pos_sb[d], k)), COPY)
+            turned_terms[i, k, d] = turned_term
+            turn_blocks(turned_term, plain, ident)
+
         def fetch(i, d, halves, bank, *plains):
             parts = [plain[:, half(j)] for plain in plains for j in range(plain.shape[1] // HALF)]
             turned_term = bank_tile(bank, f"turned{i}_{halves[0]}_{d}")
             for j, k in enumerate(halves):
-                nc.scalar.activation(parts[j], gg_sb[i][:].indirect(list_half(pos_sb[d], k)), COPY)
-                turned_terms[i, k, d] = turned_term[:, half(j)]
-                turn_blocks(turned_terms[i, k, d], parts[j], ident)
+                fetch_into(i, d, k, turned_term[:, half(j)], parts[j])
 
-        def scale_first(i, halves, room):
+        def scale_first(i, halves, *rooms):
+            parts = [room[:, P * j : P * (j + 1)] for room in rooms for j in range(room.shape[1] // P)]
             for j, k in enumerate(halves):
-                scaled[i, k] = room[:, half(j)]
                 for c in range(2):
                     b = 2 * k + c
+                    scaled[i, k, c] = parts[2 * j + c]
                     nc.scalar.activation(
-                        scaled[i, k][:, P * c : P * (c + 1)],
+                        scaled[i, k, c],
                         turned_terms[i, k, 0][:, P * c : P * (c + 1)],
                         COPY,
                         scale=gate_cols[:, b : b + 1],
@@ -259,7 +267,7 @@ def tile_picked_yjk_none_po_kernel(
                     ee[i, k][:, P * c : P * (c + 1)],
                     turned_terms[i, k, 1][:, P * c : P * (c + 1)],
                     gate_cols[:, b : b + 1],
-                    scaled[i, k][:, P * c : P * (c + 1)],
+                    scaled[i, k, c],
                     MULT,
                     ADD,
                 )
@@ -331,9 +339,9 @@ def tile_picked_yjk_none_po_kernel(
         w1_grouped[2] = tenant("w1_codes0", [P, PASSES * 512], BF16, "w1_grouped2")
         for o in range(PASSES):
             cast_w1(2, o, nc.scalar.copy)
-        h_sb[1] = tenant("w1_raw2_1", [P, S], F32, "h_sb1", 1024)
+        h_sb[1] = tenant("w1_raw2_1", [P, S], F32, "h_sb1", 2112)
         copy_h(1)
-        w1_grouped[3] = tenant("w1_codes1", [P, PASSES * 512], BF16, "w1_grouped3")
+        w1_grouped[3] = tenant("w1_raw2_1", [P, PASSES * 512], BF16, "w1_grouped3", 64)
         for o in range(PASSES):
             cast_w1(3, o, nc.scalar.copy)
         w2_sc = tenant("w1_raw3_1", [P, N], U8, "w2_sc", 1024)
@@ -345,48 +353,42 @@ def tile_picked_yjk_none_po_kernel(
         starts["late_room"] = starts["end"]
         starts["end"] = starts["late_room"] + 4096
         w1_codes[2] = first_tenant([P, PASSES * P], U32, "w1_codes2", 2048)
-        w1_codes[3] = middle_tenant([P, PASSES * P], U32, "w1_codes3", 512, 2560)
+        w1_codes[3] = middle_tenant([P, 544], U32, "w1_codes3", 960, 5696)[:, : PASSES * P]
 
         weighted(0, 0, tenant("w1_raw1_1", [P, S], F32, "term0_0", -1024))
         weighted(0, 1, tenant("w1_raw1_1", [P, S], F32, "term0_1", 1024))
         quantise_w1(2)
         first_product(2, 0)
-        gg_sb[0] = tenant("w1_raw2_1", [P, S], F32, "gg_sb0", -1024)
+        gg_sb[0] = tenant("w1_raw2_1", [P, S], F32, "gg_sb0", -1984)
         first_sum(0)
         BOTH = (0, 1)
-        fetch(0, 0, (0,), 3, own([P, HALF], F32, "plain0_0_0"))
-        fetch(0, 0, (1,), 6, own([P, HALF], F32, "plain0_1_0"))
+        fetch(0, 0, BOTH, 3, own([P, S], F32, "plain0_0"))
         copy_h(2)
         for d in range(2):
             weighted(1, d, own([P, S], F32, f"term1_{d}"))
         first_max(0, own([P, S], BF16, "larger0"))
         quantise_w1(3)
+        first_product(3, 0)
         gg_sb[1] = tenant("w1_raw3_1", [P, S], F32, "gg_sb1", -1024)
         first_sum(1)
         fetch(0, 1, BOTH, 4, tenant("w1_codes2", [P, S], F32, "plain0_1"))
-        scale_first(0, (0,), own([P, HALF], F32, "scaled0_0"))
-        scale_first(0, (1,), own([P, HALF], F32, "scaled0_1"))
-        first_product(3, 3)
+        scale_first(0, BOTH, own([P, S], F32, "scaled0"))
+        for k in range(2):
+            share_bank(k, 6 + k)
+            fetch_into(1, 0, k, shared_bank[k], own([P, HALF], F32, f"plain1_{k}_0")[:])
         turn_larger(0)
-        fetch(1, 0, BOTH, 1, own([P, S], F32, "plain1_0"))
         copy_h(3)
-        fetch(1, 1, BOTH, 5, own([P, S], F32, "plain1_1"))
+        middle_plain = tenant("w1_codes3", [P, S], F32, "plain1_1", 2112)
+        fetch(1, 1, BOTH, 5, middle_plain)
         scale_first(1, BOTH, own([P, S], F32, "scaled1"))
 
         for d in range(2):
             weighted(2, d, own([P, S], F32, f"term2_{d}"))
-        first_max(1, tenant("w1_codes3", [P, S], BF16, "larger1", -512))
-        gg_sb[2] = tenant("w1_codes3", [P, S], F32, "gg_sb2", 512)
+        first_max(1, tenant("w1_codes3", [P, S], BF16, "larger1", -960))
+        gg_sb[2] = tenant("w1_codes3", [P, S], F32, "gg_sb2", 64)
         first_sum(2)
         turn_larger(1)
-        fetch(
-            2,
-            0,
-            BOTH,
-            7,
-            middle_tenant([P, HALF], F32, "plain2_0_0", 512, 2560),
-            first_tenant([P, HALF], F32, "plain2_1_0", 1024),
-        )
+        fetch(2, 0, BOTH, 3, own([P, S], F32, "plain2_0"))
         fetch(
             2,
             1,
@@ -397,48 +399,50 @@ def tile_picked_yjk_none_po_kernel(
         )
         for d in range(2):
             weighted(3, d, first_tenant([P, S], F32, f"term3_{d}", 2048))
-        first_max(2, tenant("plain2_0_0", [P, S], BF16, "larger2", -512))
+        first_max(2, tenant("plain1_1", [P, S], BF16, "larger2"))
         scale_first(2, BOTH, own([P, S], F32, "scaled2"))
-        gg_sb[3] = tenant("plain2_0_0", [P, S], F32, "gg_sb3", 512)
+        gg_sb[3] = tenant("plain1_1", [P, S], F32, "gg_sb3", 1536)
         first_sum(3)
+        late_bank = bank_tile(3, "late_bank", BF16)
+        for i in (2, 3):
+            larger_turned[i] = late_bank[:, S * (i - 2) : S * (i - 1)]
         turn_larger(2)
-        ee[0, 0] = tenant("plain2_1_0", [P, HALF], BF16, "ee0_0")
+        ee[0, 0] = tenant("plain1_1", [P, HALF], BF16, "ee0_0", 1024)
         second_sum(0, 0)
         for i in range(1, TILES):
             ee[i, 0] = tenant("term3_1", [P, HALF], BF16, f"ee{i}_0", 512 * i)
         ee[0, 1] = tenant("term3_1", [P, HALF], BF16, "ee0_1")
-        ee[1, 1] = tenant("term3_0", [P, HALF], BF16, "ee1_1")
         first_max(3, own([P, S], BF16, "larger3"))
+        fetch(3, 0, (0,), 1, tenant("late_room", [P, HALF], F32, "plain3_0_0"))
         turn_larger(3)
-        fetch(3, 0, (0,), 1, tenant("late_room", [P, HALF], F32, "plain3_0_0", 0))
         fetch(3, 1, (0,), 0, tenant("late_room", [P, HALF], F32, "plain3_0_1", 1024))
         second_sum(1, 0)
         last_max(0, 0)
         second_sum(0, 1)
         last_max(1, 0)
-        fetch(3, 0, (1,), 3, tenant("late_room", [P, HALF], F32, "plain3_1_0", 2048))
-        fetch(3, 1, (1,), 4, tenant("late_room", [P, HALF], F32, "plain3_1_1", 3072))
-        scale_first(3, (0,), first_tenant([P, HALF], F32, "scaled3_0", 1024))
+        fetch(3, 0, (1,), 4, tenant("late_room", [P, HALF], F32, "plain3_1_0", 2048))
+        scale_first(3, (0,), *[first_tenant([P, P], F32, f"scaled3_block{c}", 512) for c in range(2)])
+        fetch(3, 1, (1,), 1, tenant("plain3_0_0", [P, HALF], F32, "plain3_1_1"))
         scale_first(3, (1,), own([P, HALF], F32, "scaled3_1"))
         second_sum(2, 0)
         last_max(0, 1)
-        second_sum(1, 1)
         last_max(2, 0)
         second_sum(3, 0)
-        last_max(1, 1)
-        last_max(3, 0)
-        turn_z((0,), 1)
-        turn_z((1,), 5)
-        for i in (2, 3):
-            ee[i, 1] = tenant("scaled3_0", [P, HALF], BF16, f"ee{i}_1", 512 * (i - 2))
+        ee[2, 1] = tenant("scaled3_block0", [P, HALF], BF16, "ee2_1")
         second_sum(2, 1)
-        second_sum(3, 1, (0,))
+        last_max(3, 0)
+        turn_z((0,), 6)
+        turn_z((1,), 4)
+        ee[1, 1] = tenant("scaled3_block1", [P, HALF], BF16, "ee1_1")
+        second_sum(1, 1)
         last_max(2, 1)
-        second_sum(3, 1, (1,))
+        ee[3, 1] = own([P, HALF], BF16, "ee3_1")
+        second_sum(3, 1)
+        last_max(1, 1)
         last_max(3, 1, (0,))
         turn_z((2,), 0)
         last_max(3, 1, (1,))
-        turn_z((3,), 3)
+        turn_z((3,), 7)
         for b in range(BLOCKS):
             group_z((b,))
         y_acc = {}
@@ -464,10 +468,10 @@ def tile_picked_yjk_none_po_kernel(
                 in_=y_sb[b][:].rearrange("p t (c e) -> p c t e", e=4),
             )
 
-        for b, bank in enumerate((6, 2, 4)):
+        for b, bank in enumerate((5, 2, 3)):
             second_product(b, bank)
         copy_y(0)
-        second_product(3, 6)
+        second_product(3, 5)
         copy_y(1)
         copy_y(2)
         round_y(0)

@@ -88,8 +88,7 @@ def tile_picked_yjk_none_po_kernel(
         nc.vector.tensor_copy(out=ident_bf[:], in_=ident[:])
 
         nc.sync.dma_start(offs_sb[:], offs)
-        w2_raw = own([P, 2 * N], U8, "w2_raw")
-        nc.sync.dma_start(out=w2_raw[:].bitcast(I32), in_=w2_words[0].bitcast(I32))
+        nc.sync.dma_start(pos_sb[0][:], pos1)
         nc.sync.dma_start(out=w2s_raw[:16, :].bitcast(I32), in_=w2_scales[0].bitcast(I32))
         for o in range(PASSES):
             load_w1(0, o, nc.scalar)
@@ -103,11 +102,12 @@ def tile_picked_yjk_none_po_kernel(
         load_x(1)
         for o in range(PASSES):
             load_w1(1, o, nc.sync)
-        nc.sync.dma_start(pos_sb[0][:], pos1)
         nc.sync.dma_start(pos_sb[1][:], pos2)
         for i in (2, 3):
             for o in range(PASSES):
                 load_w1(i, o, nc.sync)
+        w2_raw = own([P, 2 * N], U8, "w2_raw")
+        nc.sync.dma_start(out=w2_raw[:].bitcast(I32), in_=w2_words[0].bitcast(I32))
 
         gate_cols = own([P, 2 * BLOCKS], F32, "gate_cols")
         turned = bank_tile(2, "turned")
@@ -140,8 +140,6 @@ def tile_picked_yjk_none_po_kernel(
 
         xs_picked = own([P, S], U8, "xs_picked")
         x_first = own([P, S], U32, "x_first")
-        w2_codes = own([P, 4, P, 2], U8, "w2_codes")
-        nc.vector.tensor_copy(out=w2_codes[:], in_=w2_raw[:].rearrange("p (m t b) -> p t m b", t=4, b=2))
         w2s_dealt = own([P, N], U8, "w2s_dealt")
         nc.vector.tensor_copy(
             out=w2s_dealt[:].rearrange("p (t m) -> p t m", t=4), in_=w2s_raw[:].rearrange("p (m t) -> p t m", t=4)
@@ -314,10 +312,12 @@ def tile_picked_yjk_none_po_kernel(
             cols = nodes_of(blocks)
             nc.vector.quantize_mx(out=z_codes[:, cols].bitcast(FP8X4), scales=z_scales[:, cols], in_=z_grouped[blocks][:])
 
+        w2_codes = []
+
         def second_pass(t, acc, cols):
             nc.tensor.matmul_mx(
                 out=acc,
-                lhsT=w2_codes[:, t].rearrange("p m b -> p (m b)").bitcast(FP4X4),
+                lhsT=w2_codes[0][:, 2 * P * t : 2 * P * (t + 1)].bitcast(FP4X4),
                 lhsT_scale=w2_sc[:, P * t : P * (t + 1)],
                 rhs=z_codes[:, cols].bitcast(FP8X4),
                 rhs_scale=z_scales[:, cols],
@@ -424,6 +424,11 @@ def tile_picked_yjk_none_po_kernel(
         scale_first(3, (0,), *[first_tenant([P, P], F32, f"scaled3_block{c}", 512) for c in range(2)])
         fetch(3, 1, (1,), 1, tenant("plain3_0_0", [P, HALF], F32, "plain3_1_1"))
         scale_first(3, (1,), own([P, HALF], F32, "scaled3_1"))
+        w2_codes.append(tenant("plain3_1_1", [P, 2 * N], U8, "w2_codes"))
+        nc.scalar.copy(
+            out=w2_codes[0][:].bitcast(U16).rearrange("p (t m) -> p t m", t=4),
+            in_=w2_raw[:].bitcast(U16).rearrange("p (m t) -> p t m", t=4),
+        )
         second_sum(2, 0)
         last_max(0, 1)
         last_max(2, 0)

@@ -70,7 +70,7 @@ def tile_picked_yjk_none_po_kernel(
         w1_raw = {}
 
         def load_w1(i, o, queue):
-            wide = middle_tenant([P, 4 * P + 64], F32, f"w1_raw{i}_{o}", 1984, 4160)
+            wide = middle_tenant([P, 4 * P + 64], F32, f"w1_raw{i}_{o}", 2048, 4160)
             w1_raw[i, o] = wide[:, : 4 * P].rearrange("p (j c) -> p j c", j=4)
             rows = w1[512 * o : 512 * (o + 1), P * i : P * (i + 1)]
             queue.dma_start(out=w1_raw[i, o], in_=rows.rearrange("(p j) c -> p j c", j=4))
@@ -205,8 +205,12 @@ def tile_picked_yjk_none_po_kernel(
                 picked = h_sb[i][:].indirect(list_half(pos_sb[d], k))
                 nc.vector.tensor_tensor(room[:, half(k)], picked, gate_sb[d][:, half(k)], MULT)
 
+        def wide_window(i, older, shift):
+            gg_sb[i] = tenant(older, [P, S + SPARE], F32, f"gg_sb{i}", shift)
+            nc.gpsimd.memset(gg_sb[i][:, S:], 0.0)
+
         def first_sum(i):
-            nc.vector.tensor_tensor(gg_sb[i][:], terms[i, 0][:], terms[i, 1][:], ADD)
+            nc.vector.tensor_tensor(gg_sb[i][:, :S], terms[i, 0][:], terms[i, 1][:], ADD)
 
         def turn_blocks(out, source, identity):
             for j in range(source.shape[1] // P):
@@ -218,7 +222,7 @@ def tile_picked_yjk_none_po_kernel(
 
         def first_max(i, room):
             larger[i] = room
-            nc.vector.tensor_tensor(larger[i][:], h_sb[i][:, :S], gg_sb[i][:], MAX)
+            nc.vector.tensor_tensor(larger[i][:], h_sb[i][:, :S], gg_sb[i][:, :S], MAX)
 
         def turn_larger(i):
             turn_blocks(larger_turned[i], larger[i][:], ident_bf)
@@ -238,6 +242,16 @@ def tile_picked_yjk_none_po_kernel(
             nc.scalar.activation(plain, gg_sb[i][:].indirect(list_half(pos_sb[d], k)), COPY)
             turned_terms[i, k, d] = turned_term
             turn_blocks(turned_term, plain, ident)
+
+        def fetch_all(i, d, plain, turned_halves):
+            nc.scalar.activation(plain[:], gg_sb[i][:].indirect(pos_sb[d][:]), COPY)
+            for k in range(2):
+                turned_terms[i, k, d] = turned_halves[k]
+                turn_blocks(turned_halves[k], plain[:, half(k)], ident)
+
+        def halves_of(bank, name):
+            both = bank_tile(bank, name)
+            return [both[:, half(k)] for k in range(2)]
 
         def fetch(i, d, halves, bank, *plains):
             parts = [plain[:, half(j)] for plain in plains for j in range(plain.shape[1] // HALF)]
@@ -344,7 +358,7 @@ def tile_picked_yjk_none_po_kernel(
         w1_grouped[3] = tenant("w1_raw2_1", [P, PASSES * 512], BF16, "w1_grouped3", 64)
         for o in range(PASSES):
             cast_w1(3, o, nc.scalar.copy)
-        w2_sc = tenant("w1_raw3_1", [P, N], U8, "w2_sc", 1024)
+        w2_sc = tenant("w1_raw3_1", [P, N], U8, "w2_sc", 1088)
         nc.gpsimd.memset(w2_sc[:].bitcast(I32), 0)
         for q in range(4):
             nc.sync.dma_start(
@@ -353,42 +367,42 @@ def tile_picked_yjk_none_po_kernel(
         starts["late_room"] = starts["end"]
         starts["end"] = starts["late_room"] + 4096
         w1_codes[2] = first_tenant([P, PASSES * P], U32, "w1_codes2", 2048)
-        w1_codes[3] = middle_tenant([P, 544], U32, "w1_codes3", 960, 5696)[:, : PASSES * P]
+        w1_codes[3] = middle_tenant([P, 560], U32, "w1_codes3", 960, 5760)[:, : PASSES * P]
 
         weighted(0, 0, tenant("w1_raw1_1", [P, S], F32, "term0_0", -1024))
         weighted(0, 1, tenant("w1_raw1_1", [P, S], F32, "term0_1", 1024))
         quantise_w1(2)
         first_product(2, 0)
-        gg_sb[0] = tenant("w1_raw2_1", [P, S], F32, "gg_sb0", -1984)
+        wide_window(0, "w1_raw2_1", -2048)
         first_sum(0)
         BOTH = (0, 1)
-        fetch(0, 0, BOTH, 3, own([P, S], F32, "plain0_0"))
+        fetch_all(0, 0, own([P, S], F32, "plain0_0"), halves_of(3, "turned0_0"))
         copy_h(2)
         for d in range(2):
             weighted(1, d, own([P, S], F32, f"term1_{d}"))
         first_max(0, own([P, S], BF16, "larger0"))
         quantise_w1(3)
         first_product(3, 0)
-        gg_sb[1] = tenant("w1_raw3_1", [P, S], F32, "gg_sb1", -1024)
+        wide_window(1, "w1_raw3_1", -1024)
         first_sum(1)
-        fetch(0, 1, BOTH, 4, tenant("w1_codes2", [P, S], F32, "plain0_1"))
+        fetch_all(0, 1, tenant("w1_codes2", [P, S], F32, "plain0_1"), halves_of(4, "turned0_1"))
         scale_first(0, BOTH, own([P, S], F32, "scaled0"))
         for k in range(2):
             share_bank(k, 6 + k)
-            fetch_into(1, 0, k, shared_bank[k], own([P, HALF], F32, f"plain1_{k}_0")[:])
+        fetch_all(1, 0, own([P, S], F32, "plain1_0"), shared_bank)
         turn_larger(0)
         copy_h(3)
-        middle_plain = tenant("w1_codes3", [P, S], F32, "plain1_1", 2112)
-        fetch(1, 1, BOTH, 5, middle_plain)
+        middle_plain = tenant("w1_codes3", [P, S], F32, "plain1_1", 2176)
+        fetch_all(1, 1, middle_plain, halves_of(5, "turned1_1"))
         scale_first(1, BOTH, own([P, S], F32, "scaled1"))
 
         for d in range(2):
             weighted(2, d, own([P, S], F32, f"term2_{d}"))
         first_max(1, tenant("w1_codes3", [P, S], BF16, "larger1", -960))
-        gg_sb[2] = tenant("w1_codes3", [P, S], F32, "gg_sb2", 64)
+        wide_window(2, "w1_codes3", 64)
         first_sum(2)
         turn_larger(1)
-        fetch(2, 0, BOTH, 3, own([P, S], F32, "plain2_0"))
+        fetch_all(2, 0, own([P, S], F32, "plain2_0"), [halves_of(3, "turned2_0")[0], shared_bank[0]])
         fetch(
             2,
             1,
@@ -400,7 +414,7 @@ def tile_picked_yjk_none_po_kernel(
         for d in range(2):
             weighted(3, d, first_tenant([P, S], F32, f"term3_{d}", 2048))
         first_max(2, tenant("plain1_1", [P, S], BF16, "larger2"))
-        scale_first(2, BOTH, own([P, S], F32, "scaled2"))
+        scale_first(2, (0,), own([P, HALF], F32, "scaled2_0"))
         gg_sb[3] = tenant("plain1_1", [P, S], F32, "gg_sb3", 1536)
         first_sum(3)
         late_bank = bank_tile(3, "late_bank", BF16)
@@ -420,30 +434,31 @@ def tile_picked_yjk_none_po_kernel(
         last_max(0, 0)
         second_sum(0, 1)
         last_max(1, 0)
+        second_sum(2, 0)
         fetch(3, 0, (1,), 4, tenant("late_room", [P, HALF], F32, "plain3_1_0", 2048))
         scale_first(3, (0,), *[first_tenant([P, P], F32, f"scaled3_block{c}", 512) for c in range(2)])
         fetch(3, 1, (1,), 1, tenant("plain3_0_0", [P, HALF], F32, "plain3_1_1"))
+        last_max(0, 1)
+        scale_first(2, (1,), tenant("plain3_0_1", [P, HALF], F32, "scaled2_1"))
         scale_first(3, (1,), own([P, HALF], F32, "scaled3_1"))
         w2_codes.append(tenant("plain3_1_1", [P, 2 * N], U8, "w2_codes"))
         nc.scalar.copy(
             out=w2_codes[0][:].bitcast(U16).rearrange("p (t m) -> p t m", t=4),
             in_=w2_raw[:].bitcast(U16).rearrange("p (m t) -> p t m", t=4),
         )
-        second_sum(2, 0)
-        last_max(0, 1)
         last_max(2, 0)
         second_sum(3, 0)
-        ee[2, 1] = tenant("scaled3_block0", [P, HALF], BF16, "ee2_1")
-        second_sum(2, 1)
+        ee[1, 1] = tenant("scaled3_block0", [P, HALF], BF16, "ee1_1")
+        second_sum(1, 1)
         last_max(3, 0)
         turn_z((0,), 6)
         turn_z((1,), 4)
-        ee[1, 1] = tenant("scaled3_block1", [P, HALF], BF16, "ee1_1")
-        second_sum(1, 1)
-        last_max(2, 1)
+        ee[2, 1] = tenant("scaled3_block1", [P, HALF], BF16, "ee2_1")
+        second_sum(2, 1)
+        last_max(1, 1)
         ee[3, 1] = own([P, HALF], BF16, "ee3_1")
         second_sum(3, 1)
-        last_max(1, 1)
+        last_max(2, 1)
         last_max(3, 1, (0,))
         turn_z((2,), 0)
         last_max(3, 1, (1,))

@@ -70,7 +70,7 @@ def tile_picked_yjk_none_po_kernel(
         w1_raw = {}
 
         def load_w1(i, o, queue):
-            wide = middle_tenant([P, 4 * P + 64], F32, f"w1_raw{i}_{o}", 2048, 4160)
+            wide = middle_tenant([P, 4 * P + 64], F32, f"w1_raw{i}_{o}", 2048, 4224)
             w1_raw[i, o] = wide[:, : 4 * P].rearrange("p (j c) -> p j c", j=4)
             rows = w1[512 * o : 512 * (o + 1), P * i : P * (i + 1)]
             queue.dma_start(out=w1_raw[i, o], in_=rows.rearrange("(p j) c -> p j c", j=4))
@@ -198,12 +198,7 @@ def tile_picked_yjk_none_po_kernel(
 
         def weighted(i, d, room):
             terms[i, d] = room
-            if h_sb[i].shape[1] > S:
-                nc.vector.tensor_tensor(room[:], h_sb[i][:].indirect(pos_sb[d][:]), gate_sb[d][:], MULT)
-                return
-            for k in range(2):
-                picked = h_sb[i][:].indirect(list_half(pos_sb[d], k))
-                nc.vector.tensor_tensor(room[:, half(k)], picked, gate_sb[d][:, half(k)], MULT)
+            nc.vector.tensor_tensor(room[:], h_sb[i][:].indirect(pos_sb[d][:]), gate_sb[d][:], MULT)
 
         def wide_window(i, older, shift):
             gg_sb[i] = tenant(older, [P, S + SPARE], F32, f"gg_sb{i}", shift)
@@ -353,7 +348,8 @@ def tile_picked_yjk_none_po_kernel(
         w1_grouped[2] = tenant("w1_codes0", [P, PASSES * 512], BF16, "w1_grouped2")
         for o in range(PASSES):
             cast_w1(2, o, nc.scalar.copy)
-        h_sb[1] = tenant("w1_raw2_1", [P, S], F32, "h_sb1", 2112)
+        h_sb[1] = tenant("w1_raw2_1", [P, S + SPARE], F32, "h_sb1", 2112)
+        nc.gpsimd.memset(h_sb[1][:, S:], 0.0)
         copy_h(1)
         w1_grouped[3] = tenant("w1_raw2_1", [P, PASSES * 512], BF16, "w1_grouped3", 64)
         for o in range(PASSES):
@@ -482,6 +478,9 @@ def tile_picked_yjk_none_po_kernel(
         def rounded(b):
             return y_grouped[b // 2][:, 512 * (b % 2) : 512 * (b % 2 + 1)]
 
+        def round_from_bank(b, copy):
+            copy(out=rounded(b).rearrange("p (n t) -> p n t", t=4), in_=y_acc[b][:].rearrange("p (t n) -> p n t", t=4))
+
         def round_y(b):
             nc.vector.tensor_copy(
                 out=rounded(b).rearrange("p (c e t) -> p c t e", e=4, t=4),
@@ -494,14 +493,12 @@ def tile_picked_yjk_none_po_kernel(
         second_product(3, 5)
         copy_y(1)
         copy_y(2)
+        round_from_bank(2, nc.scalar.copy)
         round_y(0)
         round_y(1)
-        nc.vector.tensor_copy(
-            out=rounded(3).rearrange("p (n t) -> p n t", t=4), in_=y_acc[3][:].rearrange("p (t n) -> p n t", t=4)
-        )
+        round_from_bank(3, nc.vector.tensor_copy)
         copy_y(3)
         planes(0)
-        round_y(2)
         planes(1)
         nc.sync.dma_start(out=out_words, in_=y_words[:].bitcast(I32))
         for q in range(4):

@@ -23,7 +23,7 @@ TILES = H // P
 BLOCKS = S // P
 HALF = S // 2
 SPARE = 16
-BYTES_OF = {F32: 4, I32: 4, U32: 4, BF16: 2, U8: 1}
+BYTES_OF = {F32: 4, BF16: 2}
 
 FLOPS = 2 * K * H * S + 2 * H * N * S
 
@@ -45,69 +45,88 @@ def tile_picked_yjk_none_po_kernel(
 
         starts = {"end": 0}
 
-        def first_tenant(shape, dtype, name, room):
+        def room(name, size):
             starts[name] = starts["end"]
-            starts["end"] = starts[name] + room
-            return shared.tile(shape, dtype, name=name, align_bytes=64, offset=starts[name])
-
-        def middle_tenant(shape, dtype, name, before, room):
-            starts["end"] = starts["end"] + before
-            return first_tenant(shape, dtype, name, room)
+            starts["end"] = starts[name] + size
 
         def tenant(older, shape, dtype, name, shift=0):
             starts[name] = starts[older] + shift
             return shared.tile(shape, dtype, name=name, align_bytes=64, offset=starts[name])
 
+        def first_tenant(shape, dtype, name, size):
+            room(name + "_room", size)
+            return tenant(name + "_room", shape, dtype, name)
+
+        def middle_tenant(shape, dtype, name, before, size):
+            room(name + "_front", before)
+            return first_tenant(shape, dtype, name, size)
+
+        def half(k):
+            return slice(HALF * k, HALF * (k + 1))
+
+        def list_half(tile, k):
+            return tile[:, HALF // 16 * k : HALF // 16 * (k + 1)]
+
         offs_sb = keep.tile([P, S // 16], U16, name="offs_sb")
         pos_sb = [keep.tile([P, S // 16], U16, name=f"pos_sb{d}") for d in range(2)]
-        x_table = [first_tenant([P, T], I32, f"x_table{o}", 4 * T) for o in range(PASSES)]
-        xs_table = first_tenant([P, T], U8, "xs_table", T)
+        x_table = {0: first_tenant([P, T], I32, "x_table0", 4 * T)}
+        room("x_room1", 4 * T + 1024 + 2048)
+        xs_table = tenant("x_room1", [P, T], U8, "xs_table", 4 * T - 512)
         gate_rows = own([P, P], F32, "gate_rows")
-        gate_sb = [own([P, S], F32, f"gate_sb{d}") for d in range(2)]
+        gate_sb = [first_tenant([P, S], F32, f"gate_sb{d}", 2048) for d in range(2)]
         ident = own([P, P], F32, "ident")
         ident_bf = own([P, P], BF16, "ident_bf")
+        xs_picked = own([P, S], U8, "xs_picked")
+        xs_planes = [own([P, S], U8, f"xs_planes{o}") for o in range(PASSES)]
+        w2s_raw = own([P, N], U8, "w2s_raw")
         h_sb = {i: own([P, S + SPARE], F32, f"h_sb{i}") for i in (0, 2, 3)}
         w1_raw = {}
 
-        def load_w1(i, o, queue):
-            wide = middle_tenant([P, 4 * P + 64], F32, f"w1_raw{i}_{o}", 2048, 4224)
-            w1_raw[i, o] = wide[:, : 4 * P].rearrange("p (j c) -> p j c", j=4)
+        def load_w1(i, o, queue, tile):
+            w1_raw[i, o] = tile[:, : 4 * P].rearrange("p (j c) -> p j c", j=4)
             rows = w1[512 * o : 512 * (o + 1), P * i : P * (i + 1)]
             queue.dma_start(out=w1_raw[i, o], in_=rows.rearrange("(p j) c -> p j c", j=4))
 
         def load_x(o):
             nc.sync.dma_start(out=x_table[o][:], in_=x_words[o].rearrange("p n t -> p (n t)").bitcast(I32))
 
-        nc.gpsimd.memset(xs_table[:].bitcast(I32), 0)
-        make_identity(nc, ident[:])
-        w2s_raw = own([P, N], U8, "w2s_raw")
-        nc.vector.memset(w2s_raw[:].bitcast(I32), 0)
+        nc.gpsimd.memset(xs_table[32:64, :].bitcast(I32), 0)
+        nc.gpsimd.memset(xs_table[64:128, :].bitcast(I32), 0)
         nc.vector.memset(gate_rows[:], 0.0)
+        nc.vector.memset(w2s_raw[:].bitcast(I32), 0)
+        for o in range(PASSES):
+            nc.vector.memset(xs_planes[o][:].bitcast(I32), 0)
         for i in (0, 2, 3):
             nc.vector.memset(h_sb[i][:, S:], 0.0)
+        nc.gpsimd.dma_start(out=w2s_raw[:16, :].bitcast(I32), in_=w2_scales[0].bitcast(I32))
+        make_identity(nc, ident[:])
         nc.vector.tensor_copy(out=ident_bf[:], in_=ident[:])
 
         nc.sync.dma_start(offs_sb[:], offs)
+        nc.sync.dma_start(
+            out=xs_table[:32, :].bitcast(I32), in_=x_scales.rearrange("o r c -> (o r) c").bitcast(I32)
+        )
         nc.sync.dma_start(pos_sb[0][:], pos1)
-        nc.sync.dma_start(out=w2s_raw[:16, :].bitcast(I32), in_=w2_scales[0].bitcast(I32))
-        for o in range(PASSES):
-            load_w1(0, o, nc.scalar)
-        load_x(0)
-        nc.sync.dma_start(out=gate_rows[: 2 * BLOCKS, :], in_=gate[:, 0, :].rearrange("d (b c) -> d b c", c=P))
-        for q in range(4):
-            nc.sync.dma_start(
-                out=xs_table[32 * q : 32 * q + 4 * PASSES, :].bitcast(I32),
-                in_=x_scales[:, 4 * q : 4 * q + 4, :].bitcast(I32),
-            )
-        load_x(1)
-        for o in range(PASSES):
-            load_w1(1, o, nc.sync)
         nc.sync.dma_start(pos_sb[1][:], pos2)
-        for i in (2, 3):
-            for o in range(PASSES):
-                load_w1(i, o, nc.sync)
-        w2_raw = own([P, 2 * N], U8, "w2_raw")
-        nc.sync.dma_start(out=w2_raw[:].bitcast(I32), in_=w2_words[0].bitcast(I32))
+        nc.sync.dma_start(out=gate_rows[: 2 * BLOCKS, :], in_=gate[:, 0, :].rearrange("d (b c) -> d b c", c=P))
+        for o in range(PASSES):
+            load_w1(0, o, nc.sync, middle_tenant([P, 4 * P], F32, f"w1_raw0_{o}", 2048, 4224))
+        load_x(0)
+
+        nc.vector.tensor_copy(xs_picked[:], xs_table[:].indirect(offs_sb[:]))
+
+        def move_scale_rows(o):
+            for q in range(4):
+                nc.sync.dma_start(
+                    out=xs_planes[o][32 * q : 32 * q + 4, :].bitcast(I32),
+                    in_=xs_picked[16 * o + 4 * q : 16 * o + 4 * q + 4, :].bitcast(I32),
+                )
+
+        move_scale_rows(0)
+        x_table[1] = tenant("xs_table", [P, T], I32, "x_table1", 512 - 4 * T)
+        load_x(1)
+        move_scale_rows(1)
+        load_w1(1, 0, nc.sync, tenant("xs_table", [P, 4 * P], F32, "w1_raw1_0", 1536))
 
         gate_cols = own([P, 2 * BLOCKS], F32, "gate_cols")
         turned = bank_tile(2, "turned")
@@ -126,41 +145,53 @@ def tile_picked_yjk_none_po_kernel(
 
         def cast_w1(i, o, copy):
             copy(
-                out=w1_grouped[i][:, 512 * o : 512 * (o + 1)].rearrange("p (u c e j) -> p c j u e", u=2, e=2, j=4),
+                out=w1_grouped[i, o].rearrange("p (u c e j) -> p c j u e", u=2, e=2, j=4),
                 in_=w1_raw[i, o].rearrange("p j (c u e) -> p c j u e", u=2, e=2),
             )
+
+        def cast_tile(i, tile):
+            w1_grouped[i] = tile[:]
+            for o in range(PASSES):
+                w1_grouped[i, o] = tile[:, 512 * o : 512 * (o + 1)]
 
         def scale_cols(i, o, count=1):
             return slice((i * PASSES + o) * P, (i * PASSES + o + count) * P)
 
         def quantise_w1(i):
             nc.vector.quantize_mx(
-                out=w1_codes[i][:].bitcast(FP8X4), scales=w1_scales[:, scale_cols(i, 0, PASSES)], in_=w1_grouped[i][:]
+                out=w1_codes[i][:].bitcast(FP8X4), scales=w1_scales[:, scale_cols(i, 0, PASSES)], in_=w1_grouped[i]
             )
 
-        xs_picked = own([P, S], U8, "xs_picked")
+        def quantise_pass(i, o):
+            nc.vector.quantize_mx(
+                out=w1_codes[i][:, P * o : P * (o + 1)].bitcast(FP8X4),
+                scales=w1_scales[:, scale_cols(i, o)],
+                in_=w1_grouped[i, o],
+            )
+
+        w1_codes[0] = first_tenant([P, PASSES * P], U32, "w1_codes0", 2048)
+        w1_grouped[0, 0] = tenant("xs_table", [P, 512], BF16, "w1_grouped0_0", 512)[:]
+        w1_grouped[0, 1] = middle_tenant([P, 512], BF16, "w1_grouped0_1", 2048, 4224)[:]
+        cast_w1(0, 0, nc.vector.tensor_copy)
+        load_w1(1, 1, nc.sync, tenant("w1_raw0_0", [P, 4 * P], F32, "w1_raw1_1"))
+        quantise_pass(0, 0)
+        cast_w1(0, 1, nc.vector.tensor_copy)
+        load_w1(2, 0, nc.sync, tenant("w1_raw0_1", [P, 4 * P], F32, "w1_raw2_0"))
+        quantise_pass(0, 1)
+        load_w1(2, 1, nc.sync, tenant("w1_grouped0_1", [P, 4 * P + 64], F32, "w1_raw2_1"))
         x_first = own([P, S], U32, "x_first")
+        nc.vector.tensor_copy(x_first[:], x_table[0][:].bitcast(U32).indirect(offs_sb[:]))
+        load_w1(3, 0, nc.sync, tenant("x_table0", [P, 4 * P], F32, "w1_raw3_0"))
+        load_w1(3, 1, nc.sync, tenant("x_table0", [P, 4 * P + 64], F32, "w1_raw3_1", 4096))
+        w2_raw = tenant("x_table0", [P, 2 * N], U8, "w2_raw", 2048)
+        nc.sync.dma_start(out=w2_raw[:].bitcast(I32), in_=w2_words[0].bitcast(I32))
         w2s_dealt = own([P, N], U8, "w2s_dealt")
         nc.vector.tensor_copy(
             out=w2s_dealt[:].rearrange("p (t m) -> p t m", t=4), in_=w2s_raw[:].rearrange("p (m t) -> p t m", t=4)
         )
-        w1_grouped[0] = own([P, PASSES * 512], BF16, "w1_grouped0")
-        w1_codes[0] = first_tenant([P, PASSES * P], U32, "w1_codes0", 2048)
-        for o in range(PASSES):
-            cast_w1(0, o, nc.vector.tensor_copy)
-        quantise_w1(0)
-        nc.vector.tensor_copy(x_first[:], x_table[0][:].bitcast(U32).indirect(offs_sb[:]))
-        nc.vector.tensor_copy(xs_picked[:], xs_table[:].indirect(offs_sb[:]))
-
-        def half(k):
-            return slice(HALF * k, HALF * (k + 1))
-
-        def list_half(tile, k):
-            return tile[:, HALF // 16 * k : HALF // 16 * (k + 1)]
-
         x_second = []
         for k in range(2):
-            x_second.append(tenant("xs_table", [P, HALF], U32, f"x_second{k}", 4 * HALF * k))
+            x_second.append(own([P, HALF], U32, f"x_second{k}"))
             nc.vector.tensor_copy(x_second[k][:], x_table[1][:].bitcast(U32).indirect(list_half(offs_sb, k)))
 
         def first_pass(i, o, acc, nodes, words, stop):
@@ -169,7 +200,7 @@ def tile_picked_yjk_none_po_kernel(
                 lhsT=w1_codes[i][:, P * o : P * (o + 1)].bitcast(FP8X4),
                 lhsT_scale=w1_scales[:, scale_cols(i, o)],
                 rhs=words.bitcast(FP8X4),
-                rhs_scale=xs_picked[4 * o : P, nodes],
+                rhs_scale=xs_planes[o][:, nodes],
                 start=(o == 0),
                 stop=stop,
             )
@@ -339,19 +370,19 @@ def tile_picked_yjk_none_po_kernel(
                 out=y_words[:, half(k)].bitcast(FP8X4), scales=y_scales[:, half(k)], in_=y_grouped[k][:]
             )
 
-        w1_grouped[1] = tenant("x_table1", [P, PASSES * 512], BF16, "w1_grouped1", 2048)
+        cast_tile(1, tenant("x_table1", [P, PASSES * 512], BF16, "w1_grouped1", 2048))
         w1_codes[1] = first_tenant([P, PASSES * P], U32, "w1_codes1", 2048)
         for o in range(PASSES):
             cast_w1(1, o, nc.vector.tensor_copy)
         quantise_w1(1)
         first_product(1, 2)
-        w1_grouped[2] = tenant("w1_codes0", [P, PASSES * 512], BF16, "w1_grouped2")
+        cast_tile(2, tenant("w1_codes0", [P, PASSES * 512], BF16, "w1_grouped2"))
         for o in range(PASSES):
             cast_w1(2, o, nc.scalar.copy)
         h_sb[1] = tenant("w1_raw2_1", [P, S + SPARE], F32, "h_sb1", 2112)
         nc.gpsimd.memset(h_sb[1][:, S:], 0.0)
         copy_h(1)
-        w1_grouped[3] = tenant("w1_raw2_1", [P, PASSES * 512], BF16, "w1_grouped3", 64)
+        cast_tile(3, tenant("w1_raw2_1", [P, PASSES * 512], BF16, "w1_grouped3", 64))
         for o in range(PASSES):
             cast_w1(3, o, nc.scalar.copy)
         w2_sc = tenant("w1_raw3_1", [P, N], U8, "w2_sc", 1088)

@@ -78,7 +78,6 @@ def tile_picked_yjk_none_po_kernel(
         ident_bf = own([P, P], BF16, "ident_bf")
         xs_picked = own([P, S], U8, "xs_picked")
         xs_planes = [own([P, S], U8, f"xs_planes{o}") for o in range(PASSES)]
-        w2s_raw = own([P, N], U8, "w2s_raw")
         h_sb = {i: own([P, S + SPARE], F32, f"h_sb{i}") for i in (0, 2, 3)}
         w1_raw = {}
 
@@ -93,12 +92,10 @@ def tile_picked_yjk_none_po_kernel(
         nc.gpsimd.memset(xs_table[32:64, :].bitcast(I32), 0)
         nc.gpsimd.memset(xs_table[64:128, :].bitcast(I32), 0)
         nc.vector.memset(gate_rows[:], 0.0)
-        nc.vector.memset(w2s_raw[:].bitcast(I32), 0)
         for o in range(PASSES):
             nc.vector.memset(xs_planes[o][:].bitcast(I32), 0)
         for i in (0, 2, 3):
             nc.vector.memset(h_sb[i][:, S:], 0.0)
-        nc.gpsimd.dma_start(out=w2s_raw[:16, :].bitcast(I32), in_=w2_scales[0].bitcast(I32))
         make_identity(nc, ident[:])
         nc.vector.tensor_copy(out=ident_bf[:], in_=ident[:])
 
@@ -110,7 +107,7 @@ def tile_picked_yjk_none_po_kernel(
         nc.sync.dma_start(pos_sb[1][:], pos2)
         nc.sync.dma_start(out=gate_rows[: 2 * BLOCKS, :], in_=gate[:, 0, :].rearrange("d (b c) -> d b c", c=P))
         for o in range(PASSES):
-            load_w1(0, o, nc.sync, middle_tenant([P, 4 * P], F32, f"w1_raw0_{o}", 2048, 4224))
+            load_w1(0, o, nc.scalar if o == 0 else nc.sync, middle_tenant([P, 4 * P], F32, f"w1_raw0_{o}", 2048, 4224))
         load_x(0)
 
         nc.vector.tensor_copy(xs_picked[:], xs_table[:].indirect(offs_sb[:]))
@@ -185,10 +182,13 @@ def tile_picked_yjk_none_po_kernel(
         load_w1(3, 1, nc.sync, tenant("x_table0", [P, 4 * P + 64], F32, "w1_raw3_1", 4096))
         w2_raw = tenant("x_table0", [P, 2 * N], U8, "w2_raw", 2048)
         nc.sync.dma_start(out=w2_raw[:].bitcast(I32), in_=w2_words[0].bitcast(I32))
-        w2s_dealt = own([P, N], U8, "w2s_dealt")
-        nc.vector.tensor_copy(
-            out=w2s_dealt[:].rearrange("p (t m) -> p t m", t=4), in_=w2s_raw[:].rearrange("p (m t) -> p t m", t=4)
-        )
+        w2s_raw = tenant("x_table0", [P, N], U8, "w2s_raw", 7168)
+        nc.gpsimd.memset(w2s_raw[:].bitcast(I32), 0)
+        for q in range(4):
+            nc.sync.dma_start(
+                out=w2s_raw[32 * q : 32 * q + 4, :].bitcast(I32), in_=w2_scales[0, 4 * q : 4 * q + 4, :].bitcast(I32)
+            )
+        w1_codes[1] = first_tenant([P, PASSES * P], U32, "w1_codes1", 2048)
         x_second = []
         for k in range(2):
             x_second.append(own([P, HALF], U32, f"x_second{k}"))
@@ -371,7 +371,6 @@ def tile_picked_yjk_none_po_kernel(
             )
 
         cast_tile(1, tenant("x_table1", [P, PASSES * 512], BF16, "w1_grouped1", 2048))
-        w1_codes[1] = first_tenant([P, PASSES * P], U32, "w1_codes1", 2048)
         for o in range(PASSES):
             cast_w1(1, o, nc.vector.tensor_copy)
         quantise_w1(1)
@@ -385,12 +384,6 @@ def tile_picked_yjk_none_po_kernel(
         cast_tile(3, tenant("w1_raw2_1", [P, PASSES * 512], BF16, "w1_grouped3", 64))
         for o in range(PASSES):
             cast_w1(3, o, nc.scalar.copy)
-        w2_sc = tenant("w1_raw3_1", [P, N], U8, "w2_sc", 1088)
-        nc.gpsimd.memset(w2_sc[:].bitcast(I32), 0)
-        for q in range(4):
-            nc.sync.dma_start(
-                out=w2_sc[32 * q : 32 * q + 4, :].bitcast(I32), in_=w2s_dealt[4 * q : 4 * q + 4, :].bitcast(I32)
-            )
         starts["late_room"] = starts["end"]
         starts["end"] = starts["late_room"] + 4096
         w1_codes[2] = first_tenant([P, PASSES * P], U32, "w1_codes2", 2048)
@@ -467,7 +460,7 @@ def tile_picked_yjk_none_po_kernel(
         fetch(3, 1, (1,), 1, tenant("plain3_0_0", [P, HALF], F32, "plain3_1_1"))
         last_max(0, 1)
         scale_first(2, (1,), tenant("plain3_0_1", [P, HALF], F32, "scaled2_1"))
-        scale_first(3, (1,), own([P, HALF], F32, "scaled3_1"))
+        scale_first(3, (1,), first_tenant([P, HALF], F32, "scaled3_1", 1024))
         w2_codes.append(tenant("plain3_1_1", [P, 2 * N], U8, "w2_codes"))
         nc.scalar.copy(
             out=w2_codes[0][:].bitcast(U16).rearrange("p (t m) -> p t m", t=4),
@@ -490,6 +483,10 @@ def tile_picked_yjk_none_po_kernel(
         turn_z((2,), 0)
         last_max(3, 1, (1,))
         turn_z((3,), 7)
+        w2_sc = tenant("scaled3_1", [P, N], U8, "w2_sc")
+        nc.vector.tensor_copy(
+            out=w2_sc[:].rearrange("p (t m) -> p t m", t=4), in_=w2s_raw[:].rearrange("p (m t) -> p t m", t=4)
+        )
         for b in range(BLOCKS):
             group_z((b,))
         y_acc = {}

@@ -78,7 +78,7 @@ def tile_picked_yjk_none_po_kernel(
         ident_bf = own([P, P], BF16, "ident_bf")
         xs_picked = own([P, S], U8, "xs_picked")
         xs_planes = [own([P, S], U8, f"xs_planes{o}") for o in range(PASSES)]
-        h_sb = {i: own([P, S + SPARE], F32, f"h_sb{i}") for i in (0, 2, 3)}
+        h_sb = {i: first_tenant([P, S + SPARE], F32, f"h_sb{i}", 2112) for i in (0, 2, 3)}
         w1_raw = {}
 
         def load_w1(i, o, queue, tile):
@@ -100,14 +100,14 @@ def tile_picked_yjk_none_po_kernel(
         nc.vector.tensor_copy(out=ident_bf[:], in_=ident[:])
 
         nc.sync.dma_start(offs_sb[:], offs)
-        nc.sync.dma_start(
+        nc.scalar.dma_start(
             out=xs_table[:32, :].bitcast(I32), in_=x_scales.rearrange("o r c -> (o r) c").bitcast(I32)
         )
         nc.sync.dma_start(pos_sb[0][:], pos1)
         nc.sync.dma_start(pos_sb[1][:], pos2)
         nc.sync.dma_start(out=gate_rows[: 2 * BLOCKS, :], in_=gate[:, 0, :].rearrange("d (b c) -> d b c", c=P))
         for o in range(PASSES):
-            load_w1(0, o, nc.scalar if o == 0 else nc.sync, middle_tenant([P, 4 * P], F32, f"w1_raw0_{o}", 2048, 4224))
+            load_w1(0, o, nc.scalar, middle_tenant([P, 4 * P], F32, f"w1_raw0_{o}", 2048, 4224))
         load_x(0)
 
         nc.vector.tensor_copy(xs_picked[:], xs_table[:].indirect(offs_sb[:]))
@@ -447,6 +447,10 @@ def tile_picked_yjk_none_po_kernel(
             ee[i, 0] = tenant("term3_1", [P, HALF], BF16, f"ee{i}_0", 512 * i)
         ee[0, 1] = tenant("term3_1", [P, HALF], BF16, "ee0_1")
         first_max(3, own([P, S], BF16, "larger3"))
+        w2_sc = tenant("h_sb3", [P, N], U8, "w2_sc")
+        nc.gpsimd.tensor_copy(
+            out=w2_sc[:].rearrange("p (t m) -> p t m", t=4), in_=w2s_raw[:].rearrange("p (m t) -> p t m", t=4)
+        )
         fetch(3, 0, (0,), 1, tenant("late_room", [P, HALF], F32, "plain3_0_0"))
         turn_larger(3)
         fetch(3, 1, (0,), 0, tenant("late_room", [P, HALF], F32, "plain3_0_1", 1024))
@@ -483,10 +487,6 @@ def tile_picked_yjk_none_po_kernel(
         turn_z((2,), 0)
         last_max(3, 1, (1,))
         turn_z((3,), 7)
-        w2_sc = tenant("scaled3_1", [P, N], U8, "w2_sc")
-        nc.vector.tensor_copy(
-            out=w2_sc[:].rearrange("p (t m) -> p t m", t=4), in_=w2s_raw[:].rearrange("p (m t) -> p t m", t=4)
-        )
         for b in range(BLOCKS):
             group_z((b,))
         y_acc = {}

@@ -129,12 +129,12 @@ def tile_picked_yjk_none_po_kernel(
         turned = bank_tile(2, "turned")
         nc.tensor.transpose(turned[:, :P], gate_rows[:], ident[:])
         nc.scalar.activation(gate_cols[:], turned[:, : 2 * BLOCKS], COPY)
-        for d in range(2):
-            spread = bank_tile(d, f"spread{d}")
-            for b in range(BLOCKS):
+        for d, blocks, bank in ((0, (0, 1, 2, 3), 0), (1, (0, 1), 1), (1, (2, 3), 3)):
+            spread = bank_tile(bank, f"spread{bank}")
+            for c, b in enumerate(blocks):
                 j = BLOCKS * d + b
-                nc.tensor.transpose(spread[:, P * b : P * (b + 1)], gate_cols[:, j : j + 1].to_broadcast([P, P]), ident[:])
-            nc.scalar.copy(out=gate_sb[d][:], in_=spread[:])
+                nc.tensor.transpose(spread[:, P * c : P * (c + 1)], gate_cols[:, j : j + 1].to_broadcast([P, P]), ident[:])
+            nc.scalar.copy(out=gate_sb[d][:, P * blocks[0] : P * (blocks[-1] + 1)], in_=spread[:, : P * len(blocks)])
 
         w1_scales = own([P, TILES * PASSES * P], U8, "w1_scales")
         w1_codes = {}
@@ -190,9 +190,11 @@ def tile_picked_yjk_none_po_kernel(
             )
         w1_codes[1] = first_tenant([P, PASSES * P], U32, "w1_codes1", 2048)
         x_second = []
-        for k in range(2):
-            x_second.append(own([P, HALF], U32, f"x_second{k}"))
-            nc.vector.tensor_copy(x_second[k][:], x_table[1][:].bitcast(U32).indirect(list_half(offs_sb, k)))
+        PIECES = (slice(0, HALF), slice(HALF, HALF + P), slice(HALF + P, S))
+        for k, piece in enumerate(PIECES):
+            x_second.append(own([P, piece.stop - piece.start], U32, f"x_second{k}"))
+            offsets = offs_sb[:, piece.start // 16 : piece.stop // 16]
+            nc.vector.tensor_copy(x_second[k][:], x_table[1][:].bitcast(U32).indirect(offsets))
 
         def first_pass(i, o, acc, nodes, words, stop):
             nc.tensor.matmul_mx(
@@ -210,19 +212,22 @@ def tile_picked_yjk_none_po_kernel(
         def first_product(i, bank):
             h_acc[i] = bank_tile(bank, f"acc{i}")
             first_pass(i, 0, h_acc[i][:], slice(0, S), x_first[:], False)
-            for k in range(2):
-                first_pass(i, 1, h_acc[i][:, half(k)], half(k), x_second[k][:], k == 1)
+            for k, piece in enumerate(PIECES):
+                first_pass(i, 1, h_acc[i][:, piece], piece, x_second[k][:], k == 2)
 
         def copy_h(i):
             nc.scalar.copy(out=h_sb[i][:, :S], in_=h_acc[i][:])
 
-        accs = [bank_tile(k, f"acc0_{k}") for k in range(2)]
-        for k in range(2):
-            first_pass(0, 0, accs[k][:, :HALF], half(k), x_first[:, half(k)], False)
-        for k in range(2):
-            first_pass(0, 1, accs[k][:, :HALF], half(k), x_second[k][:], True)
-        for k in range(2):
-            nc.scalar.copy(out=h_sb[0][:, half(k)], in_=accs[k][:, :HALF])
+        accs = [
+            bank_tile(bank, f"acc0_{k}")[:, : piece.stop - piece.start]
+            for k, (bank, piece) in enumerate(zip((0, 1, 3), PIECES))
+        ]
+        for k, piece in enumerate(PIECES):
+            first_pass(0, 0, accs[k], piece, x_first[:, piece], False)
+        for k, piece in enumerate(PIECES):
+            first_pass(0, 1, accs[k], piece, x_second[k][:], True)
+        for k, piece in enumerate(PIECES):
+            nc.scalar.copy(out=h_sb[0][:, piece], in_=accs[k])
 
         terms = {}
         gg_sb = {}
@@ -370,7 +375,7 @@ def tile_picked_yjk_none_po_kernel(
                 out=y_words[:, half(k)].bitcast(FP8X4), scales=y_scales[:, half(k)], in_=y_grouped[k][:]
             )
 
-        cast_tile(1, tenant("x_table1", [P, PASSES * 512], BF16, "w1_grouped1", 2048))
+        cast_tile(1, own([P, PASSES * 512], BF16, "w1_grouped1"))
         for o in range(PASSES):
             cast_w1(1, o, nc.vector.tensor_copy)
         quantise_w1(1)

@@ -503,9 +503,9 @@ def tile_picked_yjk_none_po_kernel(
             for t in range(4):
                 second_pass(t, y_acc[b][:, P * t : P * (t + 1)], nodes_of((b,)))
 
-        def copy_y(b):
+        def copy_y(b, copy):
             y_sb[b] = own([P, 4, P], F32, f"y{b}")
-            nc.scalar.copy(out=y_sb[b][:], in_=y_acc[b][:].rearrange("p (t n) -> p t n", t=4))
+            copy(out=y_sb[b][:], in_=y_acc[b][:].rearrange("p (t n) -> p t n", t=4))
             nc.sync.dma_start(out=out_rows[:, :, nodes_of((b,))], in_=y_sb[b][:])
 
         def rounded(b):
@@ -514,23 +514,13 @@ def tile_picked_yjk_none_po_kernel(
         def round_from_bank(b, copy):
             copy(out=rounded(b).rearrange("p (n t) -> p n t", t=4), in_=y_acc[b][:].rearrange("p (t n) -> p n t", t=4))
 
-        def round_y(b):
-            nc.vector.tensor_copy(
-                out=rounded(b).rearrange("p (c e t) -> p c t e", e=4, t=4),
-                in_=y_sb[b][:].rearrange("p t (c e) -> p c t e", e=4),
-            )
-
-        for b, bank in enumerate((5, 2, 3)):
+        for b, bank in enumerate((5, 2, 3, 1)):
             second_product(b, bank)
-        copy_y(0)
-        second_product(3, 5)
-        copy_y(1)
-        copy_y(2)
-        round_from_bank(2, nc.scalar.copy)
-        round_y(0)
-        round_y(1)
+        for b, copy in enumerate((nc.scalar.copy, nc.vector.tensor_copy, nc.scalar.copy)):
+            copy_y(b, copy)
+            round_from_bank(b, copy)
         round_from_bank(3, nc.vector.tensor_copy)
-        copy_y(3)
+        copy_y(3, nc.scalar.copy)
         planes(0)
         planes(1)
         nc.sync.dma_start(out=out_words, in_=y_words[:].bitcast(I32))

@@ -22,8 +22,10 @@ PASSES = K // 512
 TILES = H // P
 BLOCKS = S // P
 HALF = S // 2
+BOTH = (0, 1)
 SPARE = 16
 BYTES_OF = {F32: 4, BF16: 2}
+PIECES = (slice(0, HALF), slice(HALF, HALF + P), slice(HALF + P, S))
 
 FLOPS = 2 * K * H * S + 2 * H * N * S
 
@@ -175,11 +177,11 @@ def tile_picked_yjk_none_po_kernel(
         cast_w1(0, 1, nc.vector.tensor_copy)
         load_w1(2, 0, nc.sync, tenant("w1_raw0_1", [P, 4 * P], F32, "w1_raw2_0"))
         quantise_pass(0, 1)
-        load_w1(2, 1, nc.sync, tenant("w1_grouped0_1", [P, 4 * P + 64], F32, "w1_raw2_1"))
+        load_w1(2, 1, nc.sync, tenant("w1_grouped0_1", [P, 4 * P], F32, "w1_raw2_1"))
         x_first = own([P, S], U32, "x_first")
         nc.vector.tensor_copy(x_first[:], x_table[0][:].bitcast(U32).indirect(offs_sb[:]))
         load_w1(3, 0, nc.sync, tenant("x_table0", [P, 4 * P], F32, "w1_raw3_0"))
-        load_w1(3, 1, nc.sync, tenant("x_table0", [P, 4 * P + 64], F32, "w1_raw3_1", 4096))
+        load_w1(3, 1, nc.sync, tenant("x_table0", [P, 4 * P], F32, "w1_raw3_1", 4096))
         w2_raw = tenant("x_table0", [P, 2 * N], U8, "w2_raw", 2048)
         nc.sync.dma_start(out=w2_raw[:].bitcast(I32), in_=w2_words[0].bitcast(I32))
         w2s_raw = tenant("x_table0", [P, N], U8, "w2s_raw", 7168)
@@ -190,7 +192,6 @@ def tile_picked_yjk_none_po_kernel(
             )
         w1_codes[1] = first_tenant([P, PASSES * P], U32, "w1_codes1", 2048)
         x_second = []
-        PIECES = (slice(0, HALF), slice(HALF, HALF + P), slice(HALF + P, S))
         for k, piece in enumerate(PIECES):
             x_second.append(own([P, piece.stop - piece.start], U32, f"x_second{k}"))
             offsets = offs_sb[:, piece.start // 16 : piece.stop // 16]
@@ -232,9 +233,9 @@ def tile_picked_yjk_none_po_kernel(
         terms = {}
         gg_sb = {}
 
-        def weighted(i, d, room):
-            terms[i, d] = room
-            nc.vector.tensor_tensor(room[:], h_sb[i][:].indirect(pos_sb[d][:]), gate_sb[d][:], MULT)
+        def weighted(i, d, tile):
+            terms[i, d] = tile
+            nc.vector.tensor_tensor(tile[:], h_sb[i][:].indirect(pos_sb[d][:]), gate_sb[d][:], MULT)
 
         def wide_window(i, older, shift):
             gg_sb[i] = tenant(older, [P, S + SPARE], F32, f"gg_sb{i}", shift)
@@ -247,12 +248,11 @@ def tile_picked_yjk_none_po_kernel(
             for j in range(source.shape[1] // P):
                 nc.tensor.transpose(out[:, P * j : P * (j + 1)], source[:, P * j : P * (j + 1)], identity[:])
 
+        larger = {}
         larger_turned = {}
 
-        larger = {}
-
-        def first_max(i, room):
-            larger[i] = room
+        def first_max(i, tile):
+            larger[i] = tile
             nc.vector.tensor_tensor(larger[i][:], h_sb[i][:, :S], gg_sb[i][:, :S], MAX)
 
         def turn_larger(i):
@@ -261,7 +261,6 @@ def tile_picked_yjk_none_po_kernel(
         turned_terms = {}
         scaled = {}
         ee = {}
-
         shared_bank = {}
 
         def share_bank(i, bank):
@@ -285,13 +284,12 @@ def tile_picked_yjk_none_po_kernel(
             return [both[:, half(k)] for k in range(2)]
 
         def fetch(i, d, halves, bank, *plains):
-            parts = [plain[:, half(j)] for plain in plains for j in range(plain.shape[1] // HALF)]
             turned_term = bank_tile(bank, f"turned{i}_{halves[0]}_{d}")
             for j, k in enumerate(halves):
-                fetch_into(i, d, k, turned_term[:, half(j)], parts[j])
+                fetch_into(i, d, k, turned_term[:, half(j)], plains[j][:, :HALF])
 
-        def scale_first(i, halves, *rooms):
-            parts = [room[:, P * j : P * (j + 1)] for room in rooms for j in range(room.shape[1] // P)]
+        def scale_first(i, halves, *tiles):
+            parts = [tile[:, P * j : P * (j + 1)] for tile in tiles for j in range(tile.shape[1] // P)]
             for j, k in enumerate(halves):
                 for c in range(2):
                     b = 2 * k + c
@@ -303,8 +301,8 @@ def tile_picked_yjk_none_po_kernel(
                         scale=gate_cols[:, b : b + 1],
                     )
 
-        def second_sum(i, k, blocks=(0, 1)):
-            for c in blocks:
+        def second_sum(i, k):
+            for c in range(2):
                 b = BLOCKS + 2 * k + c
                 nc.vector.scalar_tensor_tensor(
                     ee[i, k][:, P * c : P * (c + 1)],
@@ -331,39 +329,36 @@ def tile_picked_yjk_none_po_kernel(
         y_scales = own([P, S], U8, "y_scales")
         out_rows = out_0.rearrange("(p t) n -> p t n", t=4)
         out_words = out_1[0].rearrange("p n t -> p (n t)").bitcast(I32)
-        z_codes = own([P, S], U32, "z_codes")
         z_scales = own([P, S], U8, "z_scales")
         y_grouped = [own([P, 4 * HALF], BF16, f"y_grouped{k}") for k in range(2)]
         z_back = {}
         z_grouped = {}
 
-        def nodes_of(blocks):
-            return slice(P * blocks[0], P * (blocks[-1] + 1))
+        def nodes_of(b):
+            return slice(P * b, P * (b + 1))
 
-        def turn_z(blocks, bank):
-            z_back[blocks] = bank_tile(bank, f"z_back{blocks[0]}")
-            words = zT[blocks[0] // 2][:].bitcast(F32)
-            start = 2 * P * (blocks[0] % 2)
-            turn_blocks(z_back[blocks], words[:, start : start + 2 * P * len(blocks)], ident)
+        def turn_z(b, bank):
+            z_back[b] = bank_tile(bank, f"z_back{b}")
+            words = zT[b // 2][:].bitcast(F32)
+            start = 2 * P * (b % 2)
+            turn_blocks(z_back[b], words[:, start : start + 2 * P], ident)
 
-        def group_z(blocks):
-            z_grouped[blocks] = own([P, 4 * P * len(blocks)], BF16, f"z_grouped{blocks[0]}")
+        def group_z(b):
+            z_grouped[b] = own([P, 4 * P], BF16, f"z_grouped{b}")
             nc.scalar.copy(
-                out=z_grouped[blocks][:].bitcast(F32).rearrange("p (b n u) -> p b n u", u=2, n=P),
-                in_=z_back[blocks][:, : 2 * P * len(blocks)].rearrange("p (b u n) -> p b n u", u=2, n=P),
+                out=z_grouped[b][:].bitcast(F32).rearrange("p (b n u) -> p b n u", u=2, n=P),
+                in_=z_back[b][:, : 2 * P].rearrange("p (b u n) -> p b n u", u=2, n=P),
             )
 
-        def quantise_z(blocks):
-            cols = nodes_of(blocks)
-            nc.vector.quantize_mx(out=z_codes[:, cols].bitcast(FP8X4), scales=z_scales[:, cols], in_=z_grouped[blocks][:])
-
-        w2_codes = []
+        def quantise_z(b):
+            cols = nodes_of(b)
+            nc.vector.quantize_mx(out=z_codes[:, cols].bitcast(FP8X4), scales=z_scales[:, cols], in_=z_grouped[b][:])
 
         def second_pass(t, acc, cols):
             nc.tensor.matmul_mx(
                 out=acc,
-                lhsT=w2_codes[0][:, 2 * P * t : 2 * P * (t + 1)].bitcast(FP4X4),
-                lhsT_scale=w2_sc[:, P * t : P * (t + 1)],
+                lhsT=w2_codes[t // 2][:, 2 * P * (t % 2) : 2 * P * (t % 2 + 1)].bitcast(FP4X4),
+                lhsT_scale=w2s_dealt[:, P * t : P * (t + 1)],
                 rhs=z_codes[:, cols].bitcast(FP8X4),
                 rhs_scale=z_scales[:, cols],
                 start=True,
@@ -383,14 +378,13 @@ def tile_picked_yjk_none_po_kernel(
         cast_tile(2, tenant("w1_codes0", [P, PASSES * 512], BF16, "w1_grouped2"))
         for o in range(PASSES):
             cast_w1(2, o, nc.scalar.copy)
-        h_sb[1] = tenant("w1_raw2_1", [P, S + SPARE], F32, "h_sb1", 2112)
+        h_sb[1] = tenant("w1_raw2_0", [P, S + SPARE], F32, "h_sb1")
         nc.gpsimd.memset(h_sb[1][:, S:], 0.0)
         copy_h(1)
         cast_tile(3, tenant("w1_raw2_1", [P, PASSES * 512], BF16, "w1_grouped3", 64))
         for o in range(PASSES):
             cast_w1(3, o, nc.scalar.copy)
-        starts["late_room"] = starts["end"]
-        starts["end"] = starts["late_room"] + 4096
+        room("late_room", 4096)
         w1_codes[2] = first_tenant([P, PASSES * P], U32, "w1_codes2", 2048)
         w1_codes[3] = middle_tenant([P, 560], U32, "w1_codes3", 960, 5760)[:, : PASSES * P]
 
@@ -400,7 +394,6 @@ def tile_picked_yjk_none_po_kernel(
         first_product(2, 0)
         wide_window(0, "w1_raw2_1", -2048)
         first_sum(0)
-        BOTH = (0, 1)
         fetch_all(0, 0, own([P, S], F32, "plain0_0"), halves_of(3, "turned0_0"))
         copy_h(2)
         for d in range(2):
@@ -417,8 +410,7 @@ def tile_picked_yjk_none_po_kernel(
         fetch_all(1, 0, own([P, S], F32, "plain1_0"), shared_bank)
         turn_larger(0)
         copy_h(3)
-        middle_plain = tenant("w1_codes3", [P, S], F32, "plain1_1", 2176)
-        fetch_all(1, 1, middle_plain, halves_of(5, "turned1_1"))
+        fetch_all(1, 1, tenant("w1_codes3", [P, S], F32, "plain1_1", 2176), halves_of(5, "turned1_1"))
         scale_first(1, BOTH, own([P, S], F32, "scaled1"))
 
         for d in range(2):
@@ -452,9 +444,14 @@ def tile_picked_yjk_none_po_kernel(
             ee[i, 0] = tenant("term3_1", [P, HALF], BF16, f"ee{i}_0", 512 * i)
         ee[0, 1] = tenant("term3_1", [P, HALF], BF16, "ee0_1")
         first_max(3, own([P, S], BF16, "larger3"))
-        w2_sc = tenant("h_sb3", [P, N], U8, "w2_sc")
+        w2s_dealt = tenant("h_sb3", [P, N], U8, "w2_sc")
         nc.gpsimd.tensor_copy(
-            out=w2_sc[:].rearrange("p (t m) -> p t m", t=4), in_=w2s_raw[:].rearrange("p (m t) -> p t m", t=4)
+            out=w2s_dealt[:].rearrange("p (t m) -> p t m", t=4), in_=w2s_raw[:].rearrange("p (m t) -> p t m", t=4)
+        )
+        w2_codes = {1: tenant("h_sb3", [P, N], U8, "w2_codes1", 512)}
+        nc.gpsimd.tensor_copy(
+            out=w2_codes[1][:].rearrange("p (t m e) -> p t m e", t=2, e=2),
+            in_=w2_raw[:].rearrange("p (m t e) -> p t m e", t=4, e=2)[:, 2:, :, :],
         )
         fetch(3, 0, (0,), 1, tenant("late_room", [P, HALF], F32, "plain3_0_0"))
         turn_larger(3)
@@ -462,51 +459,52 @@ def tile_picked_yjk_none_po_kernel(
         second_sum(1, 0)
         last_max(0, 0)
         second_sum(0, 1)
-        last_max(1, 0)
         second_sum(2, 0)
         fetch(3, 0, (1,), 4, tenant("late_room", [P, HALF], F32, "plain3_1_0", 2048))
         scale_first(3, (0,), *[first_tenant([P, P], F32, f"scaled3_block{c}", 512) for c in range(2)])
         fetch(3, 1, (1,), 1, tenant("plain3_0_0", [P, HALF], F32, "plain3_1_1"))
+        last_max(1, 0)
         last_max(0, 1)
         scale_first(2, (1,), tenant("plain3_0_1", [P, HALF], F32, "scaled2_1"))
         scale_first(3, (1,), first_tenant([P, HALF], F32, "scaled3_1", 1024))
-        w2_codes.append(tenant("plain3_1_1", [P, 2 * N], U8, "w2_codes"))
+        w2_codes[0] = tenant("plain3_1_1", [P, N], U8, "w2_codes0")
         nc.scalar.copy(
-            out=w2_codes[0][:].bitcast(U16).rearrange("p (t m) -> p t m", t=4),
-            in_=w2_raw[:].bitcast(U16).rearrange("p (m t) -> p t m", t=4),
+            out=w2_codes[0][:].bitcast(U16).rearrange("p (t m) -> p t m", t=2),
+            in_=w2_raw[:].bitcast(U16).rearrange("p (m t) -> p t m", t=4)[:, :2, :],
         )
-        last_max(2, 0)
-        second_sum(3, 0)
-        ee[1, 1] = tenant("scaled3_block0", [P, HALF], BF16, "ee1_1")
+        ee[1, 1] = tenant("term3_0", [P, HALF], BF16, "ee1_1")
         second_sum(1, 1)
+        second_sum(3, 0)
+        last_max(2, 0)
+        last_max(1, 1)
         last_max(3, 0)
-        turn_z((0,), 6)
-        turn_z((1,), 4)
+        turn_z(0, 6)
+        turn_z(1, 4)
         ee[2, 1] = tenant("scaled3_block1", [P, HALF], BF16, "ee2_1")
         second_sum(2, 1)
-        last_max(1, 1)
         ee[3, 1] = own([P, HALF], BF16, "ee3_1")
         second_sum(3, 1)
         last_max(2, 1)
         last_max(3, 1, (0,))
-        turn_z((2,), 0)
+        turn_z(2, 0)
         last_max(3, 1, (1,))
-        turn_z((3,), 7)
+        turn_z(3, 7)
         for b in range(BLOCKS):
-            group_z((b,))
+            group_z(b)
+        z_codes = tenant("scaled3_block0", [P, S], U32, "z_codes")
         y_acc = {}
         y_sb = {}
 
         def second_product(b, bank):
-            quantise_z((b,))
+            quantise_z(b)
             y_acc[b] = bank_tile(bank, f"y_acc{b}")
             for t in range(4):
-                second_pass(t, y_acc[b][:, P * t : P * (t + 1)], nodes_of((b,)))
+                second_pass(t, y_acc[b][:, P * t : P * (t + 1)], nodes_of(b))
 
         def copy_y(b, copy):
             y_sb[b] = own([P, 4, P], F32, f"y{b}")
             copy(out=y_sb[b][:], in_=y_acc[b][:].rearrange("p (t n) -> p t n", t=4))
-            nc.sync.dma_start(out=out_rows[:, :, nodes_of((b,))], in_=y_sb[b][:])
+            nc.sync.dma_start(out=out_rows[:, :, nodes_of(b)], in_=y_sb[b][:])
 
         def rounded(b):
             return y_grouped[b // 2][:, 512 * (b % 2) : 512 * (b % 2 + 1)]

from contextlib import ExitStack

import concourse.mybir as mybir
from concourse.masks import make_identity

F32 = mybir.dt.float32
BF16 = mybir.dt.bfloat16
I32 = mybir.dt.int32
U32 = mybir.dt.uint32
U16 = mybir.dt.uint16
U8 = mybir.dt.uint8
FP8X4 = mybir.dt.float8_e4m3fn_x4
FP4X4 = mybir.dt.float4_e2m1fn_x4
COPY = mybir.ActivationFunctionType.Copy
MULT = mybir.AluOpType.mult
MAX = mybir.AluOpType.max
ADD = mybir.AluOpType.add

P = 128
K, T, S, H, N = 1024, 2048, 512, 512, 512
PASSES = K // 512
TILES = H // P
BLOCKS = S // P
HALF = S // 2
BOTH = (0, 1)
SPARE = 16
BYTES_OF = {F32: 4, BF16: 2}
PIECES = (slice(0, HALF), slice(HALF, HALF + P), slice(HALF + P, S))

FLOPS = 2 * K * H * S + 2 * H * N * S


def tile_picked_yjk_none_po_kernel(
    tc, x_words, x_scales, w1, w2_words, w2_scales, gate, offs, pos1, pos2, out_0, out_1, out_2
):
    nc = tc.nc
    with ExitStack() as ctx:
        keep = ctx.enter_context(tc.tile_pool(name="keep", bufs=1))
        shared = ctx.enter_context(tc.tile_pool(name="shared", bufs=1))
        psum = ctx.enter_context(tc.psum_pool(name="psum", bufs=1))

        def bank_tile(bank, name, dtype=F32):
            return psum.tile([P, 2048 // BYTES_OF[dtype]], dtype, name=name, offset=2048 * bank)

        def own(shape, dtype, name):
            return keep.tile(shape, dtype, name=name, align_bytes=64)

        starts = {"end": 0}

        def room(name, size):
            starts[name] = starts["end"]
            starts["end"] = starts[name] + size

        def tenant(older, shape, dtype, name, shift=0):
            starts[name] = starts[older] + shift
            return shared.tile(shape, dtype, name=name, align_bytes=64, offset=starts[name])

        def first_tenant(shape, dtype, name, size):
            room(name + "_room", size)
            return tenant(name + "_room", shape, dtype, name)

        def middle_tenant(shape, dtype, name, before, size):
            room(name + "_front", before)
            return first_tenant(shape, dtype, name, size)

        def half(k):
            return slice(HALF * k, HALF * (k + 1))

        def list_half(tile, k):
            return tile[:, HALF // 16 * k : HALF // 16 * (k + 1)]

        offs_sb = keep.tile([P, S // 16], U16, name="offs_sb")
        pos_sb = [keep.tile([P, S // 16], U16, name=f"pos_sb{d}") for d in range(2)]
        x_table = {0: first_tenant([P, T], I32, "x_table0", 4 * T)}
        room("x_room1", 4 * T + 1024 + 2048)
        xs_table = tenant("x_room1", [P, T], U8, "xs_table", 4 * T - 512)
        gate_rows = own([P, P], F32, "gate_rows")
        gate_sb = [first_tenant([P, S], F32, f"gate_sb{d}", 2048) for d in range(2)]
        ident = own([P, P], F32, "ident")
        ident_bf = own([P, P], BF16, "ident_bf")
        xs_picked = own([P, S], U8, "xs_picked")
        xs_planes = [own([P, S], U8, f"xs_planes{o}") for o in range(PASSES)]
        h_sb = {i: first_tenant([P, S + SPARE], F32, f"h_sb{i}", 2112) for i in (0, 2, 3)}
        w1_raw = {}

        def load_w1(i, o, queue, tile):
            w1_raw[i, o] = tile[:, : 4 * P].rearrange("p (j c) -> p j c", j=4)
            rows = w1[512 * o : 512 * (o + 1), P * i : P * (i + 1)]
            queue.dma_start(out=w1_raw[i, o], in_=rows.rearrange("(p j) c -> p j c", j=4))

        def load_x(o):
            nc.sync.dma_start(out=x_table[o][:], in_=x_words[o].rearrange("p n t -> p (n t)").bitcast(I32))

        nc.gpsimd.memset(xs_table[32:64, :].bitcast(I32), 0)
        nc.gpsimd.memset(xs_table[64:128, :].bitcast(I32), 0)
        nc.vector.memset(gate_rows[:], 0.0)
        for o in range(PASSES):
            nc.vector.memset(xs_planes[o][:].bitcast(I32), 0)
        for i in (0, 2, 3):
            nc.vector.memset(h_sb[i][:, S:], 0.0)
        make_identity(nc, ident[:])
        nc.vector.tensor_copy(out=ident_bf[:], in_=ident[:])

        nc.sync.dma_start(offs_sb[:], offs)
        nc.scalar.dma_start(
            out=xs_table[:32, :].bitcast(I32), in_=x_scales.rearrange("o r c -> (o r) c").bitcast(I32)
        )
        nc.sync.dma_start(pos_sb[0][:], pos1)
        nc.sync.dma_start(pos_sb[1][:], pos2)
        nc.sync.dma_start(out=gate_rows[: 2 * BLOCKS, :], in_=gate[:, 0, :].rearrange("d (b c) -> d b c", c=P))
        for o in range(PASSES):
            load_w1(0, o, nc.scalar, middle_tenant([P, 4 * P], F32, f"w1_raw0_{o}", 2048, 4224))
        load_x(0)

        nc.vector.tensor_copy(xs_picked[:], xs_table[:].indirect(offs_sb[:]))

        def move_scale_rows(o):
            for q in range(4):
                nc.sync.dma_start(
                    out=xs_planes[o][32 * q : 32 * q + 4, :].bitcast(I32),
                    in_=xs_picked[16 * o + 4 * q : 16 * o + 4 * q + 4, :].bitcast(I32),
                )

        move_scale_rows(0)
        x_table[1] = tenant("xs_table", [P, T], I32, "x_table1", 512 - 4 * T)
        load_x(1)
        move_scale_rows(1)
        load_w1(1, 0, nc.sync, tenant("xs_table", [P, 4 * P], F32, "w1_raw1_0", 1536))

        gate_cols = own([P, 2 * BLOCKS], F32, "gate_cols")
        turned = bank_tile(2, "turned")
        nc.tensor.transpose(turned[:, :P], gate_rows[:], ident[:])
        nc.scalar.activation(gate_cols[:], turned[:, : 2 * BLOCKS], COPY)
        for d, blocks, bank in ((0, (0, 1, 2, 3), 0), (1, (0, 1), 1), (1, (2, 3), 3)):
            spread = bank_tile(bank, f"spread{bank}")
            for c, b in enumerate(blocks):
                j = BLOCKS * d + b
                nc.tensor.transpose(spread[:, P * c : P * (c + 1)], gate_cols[:, j : j + 1].to_broadcast([P, P]), ident[:])
            nc.scalar.copy(out=gate_sb[d][:, P * blocks[0] : P * (blocks[-1] + 1)], in_=spread[:, : P * len(blocks)])

        w1_scales = own([P, TILES * PASSES * P], U8, "w1_scales")
        w1_codes = {}
        w1_grouped = {}

        def cast_w1(i, o, copy):
            copy(
                out=w1_grouped[i, o].rearrange("p (u c e j) -> p c j u e", u=2, e=2, j=4),
                in_=w1_raw[i, o].rearrange("p j (c u e) -> p c j u e", u=2, e=2),
            )

        def cast_tile(i, tile):
            w1_grouped[i] = tile[:]
            for o in range(PASSES):
                w1_grouped[i, o] = tile[:, 512 * o : 512 * (o + 1)]

        def scale_cols(i, o, count=1):
            return slice((i * PASSES + o) * P, (i * PASSES + o + count) * P)

        def quantise_w1(i):
            nc.vector.quantize_mx(
                out=w1_codes[i][:].bitcast(FP8X4), scales=w1_scales[:, scale_cols(i, 0, PASSES)], in_=w1_grouped[i]
            )

        def quantise_pass(i, o):
            nc.vector.quantize_mx(
                out=w1_codes[i][:, P * o : P * (o + 1)].bitcast(FP8X4),
                scales=w1_scales[:, scale_cols(i, o)],
                in_=w1_grouped[i, o],
            )

        w1_codes[0] = first_tenant([P, PASSES * P], U32, "w1_codes0", 2048)
        w1_grouped[0, 0] = tenant("xs_table", [P, 512], BF16, "w1_grouped0_0", 512)[:]
        w1_grouped[0, 1] = middle_tenant([P, 512], BF16, "w1_grouped0_1", 2048, 4224)[:]
        cast_w1(0, 0, nc.vector.tensor_copy)
        load_w1(1, 1, nc.sync, tenant("w1_raw0_0", [P, 4 * P], F32, "w1_raw1_1"))
        quantise_pass(0, 0)
        cast_w1(0, 1, nc.vector.tensor_copy)
        load_w1(2, 0, nc.sync, tenant("w1_raw0_1", [P, 4 * P], F32, "w1_raw2_0"))
        quantise_pass(0, 1)
        load_w1(2, 1, nc.sync, tenant("w1_grouped0_1", [P, 4 * P], F32, "w1_raw2_1"))
        x_first = own([P, S], U32, "x_first")
        nc.vector.tensor_copy(x_first[:], x_table[0][:].bitcast(U32).indirect(offs_sb[:]))
        load_w1(3, 0, nc.sync, tenant("x_table0", [P, 4 * P], F32, "w1_raw3_0"))
        load_w1(3, 1, nc.sync, tenant("x_table0", [P, 4 * P], F32, "w1_raw3_1", 4096))
        w2_raw = tenant("x_table0", [P, 2 * N], U8, "w2_raw", 2048)
        nc.sync.dma_start(out=w2_raw[:].bitcast(I32), in_=w2_words[0].bitcast(I32))
        w2s_raw = tenant("x_table0", [P, N], U8, "w2s_raw", 7168)
        nc.gpsimd.memset(w2s_raw[:].bitcast(I32), 0)
        for q in range(4):
            nc.sync.dma_start(
                out=w2s_raw[32 * q : 32 * q + 4, :].bitcast(I32), in_=w2_scales[0, 4 * q : 4 * q + 4, :].bitcast(I32)
            )
        w1_codes[1] = first_tenant([P, PASSES * P], U32, "w1_codes1", 2048)
        x_second = []
        for k, piece in enumerate(PIECES):
            x_second.append(own([P, piece.stop - piece.start], U32, f"x_second{k}"))
            offsets = offs_sb[:, piece.start // 16 : piece.stop // 16]
            nc.vector.tensor_copy(x_second[k][:], x_table[1][:].bitcast(U32).indirect(offsets))

        def first_pass(i, o, acc, nodes, words, stop):
            nc.tensor.matmul_mx(
                out=acc,
                lhsT=w1_codes[i][:, P * o : P * (o + 1)].bitcast(FP8X4),
                lhsT_scale=w1_scales[:, scale_cols(i, o)],
                rhs=words.bitcast(FP8X4),
                rhs_scale=xs_planes[o][:, nodes],
                start=(o == 0),
                stop=stop,
            )

        h_acc = {}

        def first_product(i, bank):
            h_acc[i] = bank_tile(bank, f"acc{i}")
            first_pass(i, 0, h_acc[i][:], slice(0, S), x_first[:], False)
            for k, piece in enumerate(PIECES):
                first_pass(i, 1, h_acc[i][:, piece], piece, x_second[k][:], k == 2)

        def copy_h(i):
            nc.scalar.copy(out=h_sb[i][:, :S], in_=h_acc[i][:])

        accs = [
            bank_tile(bank, f"acc0_{k}")[:, : piece.stop - piece.start]
            for k, (bank, piece) in enumerate(zip((0, 1, 3), PIECES))
        ]
        for k, piece in enumerate(PIECES):
            first_pass(0, 0, accs[k], piece, x_first[:, piece], False)
        for k, piece in enumerate(PIECES):
            first_pass(0, 1, accs[k], piece, x_second[k][:], True)
        for k, piece in enumerate(PIECES):
            nc.scalar.copy(out=h_sb[0][:, piece], in_=accs[k])

        terms = {}
        gg_sb = {}

        def weighted(i, d, tile):
            terms[i, d] = tile
            nc.vector.tensor_tensor(tile[:], h_sb[i][:].indirect(pos_sb[d][:]), gate_sb[d][:], MULT)

        def wide_window(i, older, shift):
            gg_sb[i] = tenant(older, [P, S + SPARE], F32, f"gg_sb{i}", shift)
            nc.gpsimd.memset(gg_sb[i][:, S:], 0.0)

        def first_sum(i):
            nc.vector.tensor_tensor(gg_sb[i][:, :S], terms[i, 0][:], terms[i, 1][:], ADD)

        def turn_blocks(out, source, identity):
            for j in range(source.shape[1] // P):
                nc.tensor.transpose(out[:, P * j : P * (j + 1)], source[:, P * j : P * (j + 1)], identity[:])

        larger = {}
        larger_turned = {}

        def first_max(i, tile):
            larger[i] = tile
            nc.vector.tensor_tensor(larger[i][:], h_sb[i][:, :S], gg_sb[i][:, :S], MAX)

        def turn_larger(i):
            turn_blocks(larger_turned[i], larger[i][:], ident_bf)

        turned_terms = {}
        scaled = {}
        ee = {}
        shared_bank = {}

        def share_bank(i, bank):
            both = bank_tile(bank, f"shared_bank{i}")
            shared_bank[i] = both[:, :HALF]
            larger_turned[i] = both[:, HALF:].bitcast(BF16)

        def fetch_into(i, d, k, turned_term, plain):
            nc.scalar.activation(plain, gg_sb[i][:].indirect(list_half(pos_sb[d], k)), COPY)
            turned_terms[i, k, d] = turned_term
            turn_blocks(turned_term, plain, ident)

        def fetch_all(i, d, plain, turned_halves):
            nc.scalar.activation(plain[:], gg_sb[i][:].indirect(pos_sb[d][:]), COPY)
            for k in range(2):
                turned_terms[i, k, d] = turned_halves[k]
                turn_blocks(turned_halves[k], plain[:, half(k)], ident)

        def halves_of(bank, name):
            both = bank_tile(bank, name)
            return [both[:, half(k)] for k in range(2)]

        def fetch(i, d, halves, bank, *plains):
            turned_term = bank_tile(bank, f"turned{i}_{halves[0]}_{d}")
            for j, k in enumerate(halves):
                fetch_into(i, d, k, turned_term[:, half(j)], plains[j][:, :HALF])

        def scale_first(i, halves, *tiles):
            parts = [tile[:, P * j : P * (j + 1)] for tile in tiles for j in range(tile.shape[1] // P)]
            for j, k in enumerate(halves):
                for c in range(2):
                    b = 2 * k + c
                    scaled[i, k, c] = parts[2 * j + c]
                    nc.scalar.activation(
                        scaled[i, k, c],
                        turned_terms[i, k, 0][:, P * c : P * (c + 1)],
                        COPY,
                        scale=gate_cols[:, b : b + 1],
                    )

        def second_sum(i, k):
            for c in range(2):
                b = BLOCKS + 2 * k + c
                nc.vector.scalar_tensor_tensor(
                    ee[i, k][:, P * c : P * (c + 1)],
                    turned_terms[i, k, 1][:, P * c : P * (c + 1)],
                    gate_cols[:, b : b + 1],
                    scaled[i, k, c],
                    MULT,
                    ADD,
                )

        zT = [own([P, 2 * H], BF16, f"zT{k}") for k in range(2)]

        def last_max(i, k, blocks=(0, 1)):
            cols = slice(P * blocks[0], P * (blocks[-1] + 1))
            groups = slice(2 * blocks[0], 2 * (blocks[-1] + 1))
            nc.vector.tensor_tensor(
                zT[k][:].rearrange("n (g i c) -> n g i c", i=TILES, c=64)[:, groups, i, :],
                larger_turned[i][:, half(k)][:, cols].rearrange("n (g c) -> n g c", c=64),
                ee[i, k][:, cols].rearrange("n (g c) -> n g c", c=64),
                MAX,
            )

        y_words = own([P, S], U32, "y_words")
        y_scales = own([P, S], U8, "y_scales")
        out_rows = out_0.rearrange("(p t) n -> p t n", t=4)
        out_words = out_1[0].rearrange("p n t -> p (n t)").bitcast(I32)
        z_scales = own([P, S], U8, "z_scales")
        y_grouped = [own([P, 4 * HALF], BF16, f"y_grouped{k}") for k in range(2)]
        z_back = {}
        z_grouped = {}

        def nodes_of(b):
            return slice(P * b, P * (b + 1))

        def turn_z(b, bank):
            z_back[b] = bank_tile(bank, f"z_back{b}")
            words = zT[b // 2][:].bitcast(F32)
            start = 2 * P * (b % 2)
            turn_blocks(z_back[b], words[:, start : start + 2 * P], ident)

        def group_z(b):
            z_grouped[b] = own([P, 4 * P], BF16, f"z_grouped{b}")
            nc.scalar.copy(
                out=z_grouped[b][:].bitcast(F32).rearrange("p (b n u) -> p b n u", u=2, n=P),
                in_=z_back[b][:, : 2 * P].rearrange("p (b u n) -> p b n u", u=2, n=P),
            )

        def quantise_z(b):
            cols = nodes_of(b)
            nc.vector.quantize_mx(out=z_codes[:, cols].bitcast(FP8X4), scales=z_scales[:, cols], in_=z_grouped[b][:])

        def second_pass(t, acc, cols):
            nc.tensor.matmul_mx(
                out=acc,
                lhsT=w2_codes[t // 2][:, 2 * P * (t % 2) : 2 * P * (t % 2 + 1)].bitcast(FP4X4),
                lhsT_scale=w2s_dealt[:, P * t : P * (t + 1)],
                rhs=z_codes[:, cols].bitcast(FP8X4),
                rhs_scale=z_scales[:, cols],
                start=True,
                stop=True,
            )

        def planes(k):
            nc.vector.quantize_mx(
                out=y_words[:, half(k)].bitcast(FP8X4), scales=y_scales[:, half(k)], in_=y_grouped[k][:]
            )

        cast_tile(1, own([P, PASSES * 512], BF16, "w1_grouped1"))
        for o in range(PASSES):
            cast_w1(1, o, nc.vector.tensor_copy)
        quantise_w1(1)
        first_product(1, 2)
        cast_tile(2, tenant("w1_codes0", [P, PASSES * 512], BF16, "w1_grouped2"))
        for o in range(PASSES):
            cast_w1(2, o, nc.scalar.copy)
        h_sb[1] = tenant("w1_raw2_0", [P, S + SPARE], F32, "h_sb1")
        nc.gpsimd.memset(h_sb[1][:, S:], 0.0)
        copy_h(1)
        cast_tile(3, tenant("w1_raw2_1", [P, PASSES * 512], BF16, "w1_grouped3", 64))
        for o in range(PASSES):
            cast_w1(3, o, nc.scalar.copy)
        room("late_room", 4096)
        w1_codes[2] = first_tenant([P, PASSES * P], U32, "w1_codes2", 2048)
        w1_codes[3] = middle_tenant([P, 560], U32, "w1_codes3", 960, 5760)[:, : PASSES * P]

        weighted(0, 0, tenant("w1_raw1_1", [P, S], F32, "term0_0", -1024))
        weighted(0, 1, tenant("w1_raw1_1", [P, S], F32, "term0_1", 1024))
        quantise_w1(2)
        first_product(2, 0)
        wide_window(0, "w1_raw2_1", -2048)
        first_sum(0)
        fetch_all(0, 0, own([P, S], F32, "plain0_0"), halves_of(3, "turned0_0"))
        copy_h(2)
        for d in range(2):
            weighted(1, d, own([P, S], F32, f"term1_{d}"))
        first_max(0, own([P, S], BF16, "larger0"))
        quantise_w1(3)
        first_product(3, 0)
        wide_window(1, "w1_raw3_1", -1024)
        first_sum(1)
        fetch_all(0, 1, tenant("w1_codes2", [P, S], F32, "plain0_1"), halves_of(4, "turned0_1"))
        scale_first(0, BOTH, own([P, S], F32, "scaled0"))
        for k in range(2):
            share_bank(k, 6 + k)
        fetch_all(1, 0, own([P, S], F32, "plain1_0"), shared_bank)
        turn_larger(0)
        copy_h(3)
        fetch_all(1, 1, tenant("w1_codes3", [P, S], F32, "plain1_1", 2176), halves_of(5, "turned1_1"))
        scale_first(1, BOTH, own([P, S], F32, "scaled1"))

        for d in range(2):
            weighted(2, d, own([P, S], F32, f"term2_{d}"))
        first_max(1, tenant("w1_codes3", [P, S], BF16, "larger1", -960))
        wide_window(2, "w1_codes3", 64)
        first_sum(2)
        turn_larger(1)
        fetch_all(2, 0, own([P, S], F32, "plain2_0"), [halves_of(3, "turned2_0")[0], shared_bank[0]])
        fetch(
            2,
            1,
            BOTH,
            2,
            tenant("late_room", [P, HALF], F32, "plain2_0_1", 512),
            tenant("late_room", [P, HALF], F32, "plain2_1_1", 2560),
        )
        for d in range(2):
            weighted(3, d, first_tenant([P, S], F32, f"term3_{d}", 2048))
        first_max(2, tenant("plain1_1", [P, S], BF16, "larger2"))
        scale_first(2, (0,), own([P, HALF], F32, "scaled2_0"))
        gg_sb[3] = tenant("plain1_1", [P, S], F32, "gg_sb3", 1536)
        first_sum(3)
        late_bank = bank_tile(3, "late_bank", BF16)
        for i in (2, 3):
            larger_turned[i] = late_bank[:, S * (i - 2) : S * (i - 1)]
        turn_larger(2)
        ee[0, 0] = tenant("plain1_1", [P, HALF], BF16, "ee0_0", 1024)
        second_sum(0, 0)
        for i in range(1, TILES):
            ee[i, 0] = tenant("term3_1", [P, HALF], BF16, f"ee{i}_0", 512 * i)
        ee[0, 1] = tenant("term3_1", [P, HALF], BF16, "ee0_1")
        first_max(3, own([P, S], BF16, "larger3"))
        w2s_dealt = tenant("h_sb3", [P, N], U8, "w2_sc")
        nc.gpsimd.tensor_copy(
            out=w2s_dealt[:].rearrange("p (t m) -> p t m", t=4), in_=w2s_raw[:].rearrange("p (m t) -> p t m", t=4)
        )
        w2_codes = {1: tenant("h_sb3", [P, N], U8, "w2_codes1", 512)}
        nc.gpsimd.tensor_copy(
            out=w2_codes[1][:].rearrange("p (t m e) -> p t m e", t=2, e=2),
            in_=w2_raw[:].rearrange("p (m t e) -> p t m e", t=4, e=2)[:, 2:, :, :],
        )
        fetch(3, 0, (0,), 1, tenant("late_room", [P, HALF], F32, "plain3_0_0"))
        turn_larger(3)
        fetch(3, 1, (0,), 0, tenant("late_room", [P, HALF], F32, "plain3_0_1", 1024))
        second_sum(1, 0)
        last_max(0, 0)
        second_sum(0, 1)
        second_sum(2, 0)
        fetch(3, 0, (1,), 4, tenant("late_room", [P, HALF], F32, "plain3_1_0", 2048))
        scale_first(3, (0,), *[first_tenant([P, P], F32, f"scaled3_block{c}", 512) for c in range(2)])
        fetch(3, 1, (1,), 1, tenant("plain3_0_0", [P, HALF], F32, "plain3_1_1"))
        last_max(1, 0)
        last_max(0, 1)
        scale_first(2, (1,), tenant("plain3_0_1", [P, HALF], F32, "scaled2_1"))
        scale_first(3, (1,), first_tenant([P, HALF], F32, "scaled3_1", 1024))
        w2_codes[0] = tenant("plain3_1_1", [P, N], U8, "w2_codes0")
        nc.scalar.copy(
            out=w2_codes[0][:].bitcast(U16).rearrange("p (t m) -> p t m", t=2),
            in_=w2_raw[:].bitcast(U16).rearrange("p (m t) -> p t m", t=4)[:, :2, :],
        )
        ee[1, 1] = tenant("term3_0", [P, HALF], BF16, "ee1_1")
        second_sum(1, 1)
        second_sum(3, 0)
        last_max(2, 0)
        last_max(1, 1)
        last_max(3, 0)
        turn_z(0, 6)
        turn_z(1, 4)
        ee[2, 1] = tenant("scaled3_block1", [P, HALF], BF16, "ee2_1")
        second_sum(2, 1)
        ee[3, 1] = own([P, HALF], BF16, "ee3_1")
        second_sum(3, 1)
        last_max(2, 1)
        last_max(3, 1, (0,))
        turn_z(2, 0)
        last_max(3, 1, (1,))
        turn_z(3, 7)
        for b in range(BLOCKS):
            group_z(b)
        z_codes = tenant("scaled3_block0", [P, S], U32, "z_codes")
        y_acc = {}
        y_sb = {}

        def second_product(b, bank):
            quantise_z(b)
            y_acc[b] = bank_tile(bank, f"y_acc{b}")
            for t in range(4):
                second_pass(t, y_acc[b][:, P * t : P * (t + 1)], nodes_of(b))

        def copy_y(b, copy):
            y_sb[b] = own([P, 4, P], F32, f"y{b}")
            copy(out=y_sb[b][:], in_=y_acc[b][:].rearrange("p (t n) -> p t n", t=4))
            nc.sync.dma_start(out=out_rows[:, :, nodes_of(b)], in_=y_sb[b][:])

        def rounded(b):
            return y_grouped[b // 2][:, 512 * (b % 2) : 512 * (b % 2 + 1)]

        def round_from_bank(b, copy):
            copy(out=rounded(b).rearrange("p (n t) -> p n t", t=4), in_=y_acc[b][:].rearrange("p (t n) -> p n t", t=4))

        for b, bank in enumerate((5, 2, 3, 1)):
            second_product(b, bank)
        for b, copy in enumerate((nc.scalar.copy, nc.vector.tensor_copy, nc.scalar.copy)):
            copy_y(b, copy)
            round_from_bank(b, copy)
        round_from_bank(3, nc.vector.tensor_copy)
        copy_y(3, nc.scalar.copy)
        planes(0)
        planes(1)
        nc.sync.dma_start(out=out_words, in_=y_words[:].bitcast(I32))
        for q in range(4):
            queue = nc.sync if q % 2 == 0 else nc.scalar
            queue.dma_start(
                out=out_2[0, 4 * q : 4 * q + 4, :].bitcast(I32),
                in_=y_scales[32 * q : 32 * q + 4, :].bitcast(I32),
            )
